import numpy as np, ml_dtypes
CORES = [66,74,82,90,194,202,210,218]
N = 8
BF = ml_dtypes.bfloat16
def gentries(a):
    return np.ascontiguousarray(a.reshape(8, 16, -1).transpose(0, 2, 1)).reshape(8, -1)
def gtable(e):
    e = np.asarray(e); return np.ascontiguousarray(e.reshape(8, -1, 16).transpose(0, 2, 1)).reshape(128, -1).astype(np.int32)
V, L, SH, EPS, RO = 4096, 128, 2, 4, 6
Q = 256 >> SH; LQ = 8 - SH; E = 16 * Q
TIGHT = (2 ** SH - 1 - EPS, EPS)
def labels(rng):
    slot = np.argsort(rng.random((8, 16, 16)), axis=-1); size = rng.permutation(np.array([6, 7, 8, 8, 10, 12, 14, 16]))[:, None, None]
    high = 8 + np.argsort(rng.random((8, 16, 8)), axis=-1); slot[..., :8] = np.where(size == 8, high, slot[..., :8])
    u = (rng.random((N, 8, 16, V)) * size).astype(np.int64)
    return 16 * np.take_along_axis(np.ascontiguousarray(np.broadcast_to(slot, (N, 8, 16, 16))), u, 3) + 8 + rng.integers(-3, 4, (N, 8, 16, V))
def inverse(rng, s, near, lo, hi):
    near = np.broadcast_to(near, (N, 8, 16, Q, 16)); out = np.empty((N, 8, 16, Q, 16), np.int64); base = np.arange(Q) << SH
    order = np.argsort(s.astype(np.int16), axis=-1, kind="stable")
    for r in range(N):
        for g in range(8):
            for p in range(16):
                o = order[r, g, p]; v = s[r, g, p][o]
                a = np.searchsorted(v, base + lo, "left"); n = (np.searchsorted(v, base + hi, "right") - a)[:, None]
                fa = np.searchsorted(v, base - EPS, "left"); fb = np.searchsorted(v, base + 2 ** SH - 1 + EPS, "right")
                u = rng.random((Q, 16))
                far = (fb[:, None] + (u * (V - (fb - fa))[:, None]).astype(np.int64)) % V
                out[r, g, p] = o[np.where(near[r, g, p] & (n > 0), np.minimum(a[:, None] + (u * n).astype(np.int64), V - 1), far)]
    return np.ascontiguousarray(out.reshape(N, 8, E, 16).transpose(0, 1, 3, 2))
def starts(rng, s, share):
    p = rng.integers(0, 16, (N, 8, L)); c = rng.integers(0, V, (N, 8, L))
    y = s[np.arange(N)[:, None, None], np.arange(8)[None, :, None], p, c]
    return np.where(rng.random((N, 8, L)) < share, Q * p + (y >> SH), rng.integers(0, E, (N, 8, L)))
def pack(s, w, e):
    return {"st": np.ascontiguousarray(s.reshape(N, 128, V)).astype(np.float32).astype(BF), "iv": np.ascontiguousarray(w).reshape(N, 128, E).astype(np.int32), "e0": np.stack([gtable(x) for x in e])}
def setup_inputs(rng):
    s = labels(rng); near = rng.random((N, 8, 16, Q, 16)) < rng.choice(np.array([0.5, 0.7, 0.85, 0.95]), (N, 8, 1, 1, 1))
    return pack(s, inverse(rng, s, near, *TIGHT), starts(rng, s, 0.85))
def setup_inputs_spread(rng):
    pw = rng.permutation(np.array([1.0, 1.0, 1.0, 2.0, 3.0, 4.0, 6.0, 8.0]))[:, None, None]
    s = np.minimum((256 * rng.random((N, 8, 16, V)) ** pw).astype(np.int64), 255)
    s = np.where(rng.random((8, 16, 1)) < 0.5, 255 - s, s); near = rng.random((N, 8, 16, Q, 16)) < 0.6
    return pack(s, inverse(rng, s, near, *TIGHT), starts(rng, s, 0.5))
def setup_inputs_ends(rng):
    s = 255 * rng.integers(0, 2, (N, 8, 16, V))
    s[..., V - 1] = 255; s[..., V - 2] = 255 - EPS - 1; s[..., V - 4:V - 2] = 255 - 2 * EPS - 2; s[:, :, 15, V - 4:] = 255; s[::2, :, 14, V - 4:V - 2] -= 1
    s[..., 0] = 0; s[..., 1] = EPS + 1; s[..., 2] = 2 * EPS + 2; s[:, :, 0, :3] = 0
    w = np.where(rng.random((N, 8, 16, E)) < 0.75, (V - 1) * rng.integers(0, 2, (N, 8, 16, E)), rng.integers(0, V, (N, 8, 16, E)))
    alike = rng.integers(0, 2, (N, 8)); alike[:, 0] = 1; alike[:, 7] = 0
    third = V - 3 - rng.integers(0, 2, (N, 8)); third[0, 7] = V - 3; third[N - 1, 7] = V - 4
    hi = np.where(rng.random((N, 8, 16)) < 0.7, V - 1, 0); hi[:, :, 13] = V - 1; hi[:, :, 14] = V - 2; hi[:, :, 15] = third
    lo = np.where(rng.random((N, 8, 16)) < 0.7, 0, V - 1); lo[:, :, 13] = 0; lo[:, :, 14] = 1; lo[:, :, 15] = 2
    w[..., E - 1] = np.where(alike[:, :, None] == 1, V - 1, hi); w[..., 0] = np.where(alike[:, :, None] == 1, 0, lo)
    e = np.where(rng.random((N, 8, L)) < 0.85, (E - 1) * rng.integers(0, 2, (N, 8, L)), rng.integers(0, E, (N, 8, L)))
    e[:, :, 0] = 0; e[:, :, L - 1] = E - 1
    return pack(s, w, e)
def setup_inputs_corners(rng):
    s = labels(rng); lane = np.arange(L)
    s[:, 1] = rng.integers(0, 256, (16, 1)); s[:, 4] = rng.integers(0, 256, (N, 16, V))
    ta = rng.integers(0, 100, 16); ty = rng.integers(0, 2, (N, 1, V)) ^ (rng.random((N, 16, V)) < 0.03); ty[:, 5] = 0
    s[:, 5] = ta[None, :, None] + 120 * ty
    near = rng.random((N, 8, 16, Q, 16)) < 0.8
    near[:, 0] = False; near[:, 1] = True; near[:, 2] = np.arange(16) == 15; near[:, 3] = np.arange(16) == 0; near[:, 4] = True; near[:, 5] = True
    w = inverse(rng, s, near, *TIGHT); e = starts(rng, s, 0.9)
    w[:, 6] = np.where(rng.random((N, 1, E)) < 0.5, (V - 1) * rng.integers(0, 2, (N, 1, E)), w[:, 6])
    own = lane + L * rng.integers(0, E // L, (N, L)); pick = rng.integers(0, 4, (N, L))
    e[:, 5] = Q * 5 + (ta[5] >> SH)
    e[:, 6] = np.where(pick == 0, 0, np.where(pick == 1, E - 1, np.where(pick == 2, own, e[:, 6])))
    e[:, 7] = np.where(rng.random((N, L)) < 0.5, own, e[:, 7])
    return pack(s, w, e)
def setup_inputs_crowd(rng):
    s = labels(rng); t = rng.integers(0, 256, (6, 16))
    s[:, :6] = t[:, :, None]; s[:, :6, :8, 1::2] = ((t + 128) & 255)[:, :8, None]
    w = inverse(rng, s, rng.random((N, 8, 16, Q, 16)) < 0.8, *TIGHT); e = starts(rng, s, 0.8)
    cnt = (np.arange(6) % 3)[None, :, None, None]; place = np.argsort(rng.random((N, 6, 16, E)), axis=2)
    w[:, :6] = 2 * rng.integers(0, V // 2, (N, 6, 16, E)) + (place < cnt)
    p = rng.integers(8, 16, 6); p[5] = rng.integers(0, 8)
    e[:, :6] = (Q * p + (t[np.arange(6), p] >> SH))[None, :, None]
    for g in (1, 3, 5): e[np.arange(N), g, rng.integers(0, L, N)] = rng.integers(0, E, N)
    e[:, 6] = e[:, 6, :1]
    return pack(s, w, e)
def setup_inputs_ties(rng):
    kinds = rng.permutation(np.array([2, 3, 4, 5, 6, 7, 8, 8]))[:, None, None]
    shift = rng.integers(0, 30 - 2 * EPS, (8, 16, 1)); shift[:, 0] = 0; shift[:, 15] = 29 - 2 * EPS
    off = np.array([0, EPS, EPS + 1, 2 * EPS, 2 * EPS + 1, 2 * EPS + 2])
    s = 32 * (rng.random((N, 8, 16, V)) * kinds).astype(np.int64) + shift + off[rng.integers(0, 6, (N, 8, 16, V))]
    near = rng.random((N, 8, 16, Q, 16)) < 0.9
    return pack(s, inverse(rng, s, near, -EPS - 1, EPS + 2 ** SH), starts(rng, s, 0.95))
def check_inputs(d):
    bad = []
    for k, lo, hi in (("st", 0, 255), ("iv", 0, V - 1), ("e0", 0, E - 1)):
        a = np.asarray(d[k]).astype(np.float64)
        if not (np.min(a) >= lo and np.max(a) <= hi): bad.append("range of " + k)
        if np.any(a != np.floor(a)): bad.append("whole numbers in " + k)
    return bad
def carry(x):
    B = L // N
    return np.concatenate([np.roll(x[..., b * B:(b + 1) * B], b, axis=0) for b in range(N)], axis=-1)
def reference(st, iv, e0):
    s = st.astype(np.float32).astype(np.int64).reshape(N, 8, 16, V); w = iv.astype(np.int64).reshape(N, 8, 16, E)
    e = np.stack([gentries(x) for x in e0]).astype(np.int64)
    row = np.arange(16)[:, None]; lane = np.arange(L)
    core = row == (e >> LQ)[:, :, None]; kl = np.where(core, ((e & (Q - 1)) << SH)[:, :, None], 0)
    p0 = np.zeros((N, 8, 16, L), np.int64); p1 = np.zeros((N, 8, 16, L), np.int64); n = np.zeros((N, 8, L), np.int64); a = np.zeros((N, 8, L), np.int64)
    for step in range(RO):
        if step > 0: e, core, kl, p0, p1, n, a = [carry(x) for x in (e, core, kl, p0, p1, n, a)]
        c = np.take_along_axis(w, e[:, :, None], 3)
        y = np.take_along_axis(s[:, :, None], c[:, :, :, None], 4)
        el = np.all((np.abs(y - kl[:, :, None]) <= EPS) | ~core[:, :, None], axis=3)
        m = (np.abs(y - p0[:, :, None]) <= EPS) & (n > 0)[:, :, None, None]
        m = m | ((np.abs(y - p1[:, :, None]) <= EPS) & (n > 1)[:, :, None, None])
        m = m & ~core[:, :, None] & el[:, :, :, None]
        ok = el & ~np.any(m, axis=3)
        join = np.any(ok, axis=2); some = np.any(el, axis=2); grow = some & ~join; dead = ~some; full = join & (n == 2)
        pr = np.argmax(np.add.reduce(m.astype(np.int64), axis=2), axis=2)
        kr = np.argmax(np.take_along_axis(m, pr[:, :, None, None], 3)[:, :, :, 0], axis=2)
        j = np.where(join, np.argmax(ok, axis=2), kr)
        z = np.take_along_axis(y, j[:, :, None, None], 2)[:, :, 0]
        lab = np.take_along_axis(z, pr[:, :, None], 2)[:, :, 0]
        d = np.repeat((e - (e & (L - 1)) + lane)[:, :, None], 16, axis=2); old = np.take_along_axis(w, d, 3)
        new = (37 * np.take_along_axis(c, j[:, :, None], 2) + (e + a)[:, :, None]) & (V - 1)
        np.put_along_axis(w, d, np.where((row == j[:, :, None]) & join[:, :, None], new, old), 3)
        f = np.minimum(np.minimum(p0, p1), z); q = np.add.reduce(f, axis=2) & 15; lq = np.take_along_axis(f, q[:, :, None], 2)[:, :, 0]
        s0 = (n > 0) & (np.abs(np.take_along_axis(p0, pr[:, :, None], 2)[:, :, 0] - lab) <= EPS)
        s1 = (n > 1) & (np.abs(np.take_along_axis(p1, pr[:, :, None], 2)[:, :, 0] - lab) <= EPS)
        e = np.where(dead, (5 * e + 1 + a) & (E - 1), np.where(full, Q * q + (lq >> SH), np.where(grow, Q * pr + (lab >> SH), e)))
        again = dead | full; one = again[:, :, None]; enter = (row == pr[:, :, None]) & grow[:, :, None]; first = row == (e >> LQ)[:, :, None]
        core = np.where(one, first, core | enter)
        kl = np.where(one, np.where(dead, (e & (Q - 1)) << SH, lq)[:, :, None], np.where(enter, lab[:, :, None], kl))
        p0 = np.where((join & (n == 0))[:, :, None], z, np.where((grow & ~s0)[:, :, None], p1, p0))
        p1 = np.where((join & (n == 1))[:, :, None], z, p1)
        n = np.where(again, 0, np.where(join, n + 1, s0.astype(np.int64) + s1)); a = a + again
    yi = w[..., :E // 2] + V * w[..., E // 2:]
    return {"yk": np.where(core, kl, -1).reshape(N, 128, L).astype(np.float32).astype(BF), "y0": np.where((n > 0)[:, :, None], p0, -1).reshape(N, 128, L).astype(np.float32).astype(BF),
            "y1": np.where((n > 1)[:, :, None], p1, -1).reshape(N, 128, L).astype(np.float32).astype(BF), "ye": np.stack([gtable(x) for x in e]).astype(np.float32),
            "ya": np.stack([gtable(x) for x in a]).astype(np.float32), "yi": np.ascontiguousarray(yi).reshape(N, 128, -1).astype(np.float32)}

@@ -1,0 +1,732 @@
+import math
+import numpy as np
+from concourse.bass import DstId, RemoteDMATransfer
+from concourse.mybir import AluOpType, AxisListType, ActivationFunctionType
+
+AL = AluOpType
+AF = ActivationFunctionType
+STEPS = 6
+FAR = 6.0
+EPS1 = 1.0 + 2.0 ** -10
+SW = 27.0 / 32.0
+M1, M8, M16 = 1.5 * 2 ** 23, 1.5 * 2 ** 26, 1.5 * 2 ** 27
+LOW = 30000.0
+RKN = 5128
+VG = ((24, 24), (24, 24), (20, 20), (20, 20), (20, 20), (20, 20))
+GS, ZS, DS, ES = 2, 1, 2, 1
+SEED, TRIES = 1, 100
+
+SCRATCH = {
+    "sts": ("sbuf", [128, 4096], "bfloat16"), "ivs": ("sbuf", [128, 1024], "int32"), "e0s": ("sbuf", [128, 8], "int32"),
+    "lw": ("sbuf", [128, 1024], "float32"), "num": ("sbuf", [128, 1040], "float32"), "rk": ("sbuf", [128, RKN], "bfloat16"),
+    "cf": ("sbuf", [128, 1536], "float32"), "ci": ("sbuf", [128, 64], "int32"), "col": ("sbuf", [128, 16], "float32"),
+    "cb": ("sbuf", [128, 28 * 128], "bfloat16"), "bw": ("sbuf", [128, 2048], "bfloat16"), "uu": ("sbuf", [128, 144], "bfloat16"),
+    "cm": ("sbuf", [128, 768], "bfloat16"), "rs": ("sbuf", [128, 192], "float32"),
+    "snd": ("sbuf", [128, 5 * 512], "bfloat16"), "land": ("sbuf", [128, 5 * 512], "bfloat16"),
+    "oyk": ("sbuf", [128, 128], "bfloat16"), "oy0": ("sbuf", [128, 128], "bfloat16"), "oy1": ("sbuf", [128, 128], "bfloat16"),
+    "oye": ("sbuf", [128, 8], "float32"), "oya": ("sbuf", [128, 8], "float32"), "oyi": ("sbuf", [128, 512], "float32"),
+}
+for _h in range(2):
+    SCRATCH["yy%d" % _h] = ("sbuf", [128, 1040], "bfloat16")
+    SCRATCH["dd%d" % _h] = ("sbuf", [128, 1024], "bfloat16")
+    SCRATCH["bad%d" % _h] = ("sbuf", [128, 1024], "bfloat16")
+    SCRATCH["em%d" % _h] = ("sbuf", [128, 1024], "bfloat16")
+    SCRATCH["off%d" % _h] = ("sbuf", [128, 16], "uint16")
+    SCRATCH["offz%d" % _h] = ("sbuf", [128, 8], "uint16")
+    SCRATCH["cc%d" % _h] = ("sbuf", [128, 64], "uint16")
+    SCRATCH["wb%d" % _h] = ("sbuf", [128, 40 * 64], "bfloat16")
+    SCRATCH["wf%d" % _h] = ("sbuf", [128, 12 * 64], "float32")
+    SCRATCH["wi%d" % _h] = ("sbuf", [128, 128], "int32")
+for _n in ("px00", "px01", "px10", "px11", "pth", "pr", "ps0", "ps1"):
+    SCRATCH[_n] = ("psum", [128, 512], "float32")
+
+SEMAPHORES = ["sv", "sa", "sp", "sg", "sent", "le", "li", "ls0", "ls1", "tb", "stored"] + ["arr%d" % k for k in range(10)]
+
+CB = ["I", "nI", "sI", "nsI", "hI", "nhI", "I64", "nI64", "I5", "I6", "one", "one64", "none", "sone", "nsone", "bigone",
+      "hugeone", "qone", "one384", "one2k", "S4", "T4", "Mw", "Kw", "Hw", "Lw", "Gw", "zero"]
+WB = ["nc", "thr", "q0", "q1", "mid", "half", "qm0", "qm1", "pm", "rke", "rkr", "ok", "ohj", "full", "vp", "win", "wbb", "oh",
+      "z0", "zj", "wp0", "wp1", "wz", "s0", "s1", "u0", "u1", "w", "f", "oq", "fq", "kr", "dr", "kna", "ee", "x4", "xg"]
+WF = {"c37": 0, "old": 1, "dv": 2, "t": 3, "sj": 4, "sg": 5, "r": 6, "sc": 7}
+BLK0 = (4, 0)
+
+
+def build(g, T, topo, core, rank):
+    ops = []
+    tag = [-1]
+    V, S, P, Q = g.vector, g.scalar, g.tensor, g.sync
+
+    def add(eng, cost, emit, rd, wr, bank=(), own=None, lat=60.0):
+        ops.append((eng, cost, emit, tuple(rd), tuple(wr), tuple(bank), own, lat, tag[0]))
+
+    def vc(n, c):
+        return 35.0 + max(64.0, n * c)
+
+    def ts(out, in0, s1, s2, o0, o1, rd, wr, n=64, c=1.0, bank=()):
+        if o1 is None:
+            add("v", vc(n, c), lambda: V.tensor_scalar(out, in0, s1, None, o0), rd, wr, bank)
+        else:
+            add("v", vc(n, c), lambda: V.tensor_scalar(out, in0, s1, s2, o0, o1), rd, wr, bank)
+
+    def tt(out, a, b, o, rd, wr, n=64, bank=(), c=None):
+        add("v", vc(n, c or (1.0 if bank else 1.6)), lambda: V.tensor_tensor(out, a, b, o), rd, wr, bank)
+
+    def cp(out, a, rd, wr, n=64, c=1.0, bank=()):
+        add("v", vc(n, c), lambda: V.tensor_copy(out, a), rd, wr, bank)
+
+    def fill(out, k, wr, n=64):
+        add("v", vc(n, 0.5), lambda: V.memset(out, k), [], wr)
+
+    def scan(out, d0, d1, o0, o1, rd, wr, n, bank=()):
+        add("v", vc(n, 1.0), lambda: V.tensor_tensor_scan(out, d0, d1, 0.0, o0, o1), rd, wr, bank)
+
+    def act(out, a, f, rd, wr, n=64, bias=0.0, scale=1.0, c=1.0, bank=()):
+        add("a", 70.0 + n * c, lambda: S.activation(out, a, f, bias=bias, scale=scale), rd, wr, bank)
+
+    def mm(lst, rd, wr, bank):
+        def emit():
+            last = None
+            for o, l, r, a, b, n in lst:
+                last = P.matmul(o, l, r, a, b)
+            return last
+        add("p", 30.0 + sum(0.5 * max(64, x[5]) for x in lst), emit, rd, wr, [bank], lat=100.0)
+
+    def C(n):
+        j = CB.index(n)
+        return T.cb[:, 128 * j:128 * j + 128]
+
+    def group(out, terms, n=64):
+        return [(out, C(l), r, j == 0, j == len(terms) - 1, n) for j, (l, r) in enumerate(terms)]
+
+    def grp(out, terms, rd, wr, bank):
+        mm(group(out, terms), list(rd) + [l for l, r in terms], wr, bank)
+
+    def io(out, pat, base, cmul, wr, n, flt=True):
+        if flt:
+            add("g", 140.0 + 2 * n, lambda: g.iota(out, pat, base, cmul, allow_small_or_imprecise_dtypes=True), [], wr)
+        else:
+            add("g", 140.0 + 2 * n, lambda: g.iota(out, pat, base, cmul), [], wr)
+
+    def dma(q, out, in_, sem, rd, wr, lat):
+        e = {"s": Q, "a": S}[q]
+        add(q, 60.0, lambda: e.dma_start(out, in_).then_inc(T.sem[sem], 16), rd, wr, own=(sem, 16), lat=lat)
+
+    def col(j):
+        return T.col[:, j:j + 1]
+
+    dma("s", T.e0s[:], T.e0[:], "le", [], ["e0s"], 2000.0)
+    dma("a", T.ivs[:], T.iv[:], "li", [], ["ivs"], 3200.0)
+    dma("s", T.sts[:, 0:2048], T.st[:, 0:2048], "ls0", ["@e0s"], ["sts0"], 5000.0)
+    dma("a", T.sts[:, 2048:4096], T.st[:, 2048:4096], "ls1", ["@ivs"], ["sts1"], 5500.0)
+
+    mi, gi, mlo, am = T.cf[:, 0:144], T.cf[:, 144:272], T.cf[:, 272:464], T.cf[:, 528:656]
+    t1, t2, t3, c64 = T.cf[:, 656:784], T.cf[:, 784:912], T.cf[:, 912:1040], T.cf[:, 1040:1104]
+    dg, m16, t4, t5 = T.cf[:, 1104:1168], T.cf[:, 1168:1184], T.cf[:, 1184:1312], T.cf[:, 1312:1440]
+    t6 = T.cf[:, 1440:1504]
+    io(T.ci[:, 0:1], [[0, 1]], 0, 1, ["pint"], 1, False)
+    io(mi, [[1, 144]], 0, 0, ["mi"], 144)
+    io(gi, [[16, 8], [0, 16]], 0, 0, ["gi"], 128)
+    io(mlo, [[0, 12], [1, 16]], 0, 0, ["mlo"], 192)
+    io(c64, [[4, 64]], 1, 0, ["c64"], 64)
+    io(T.num[:], [[1, 1040]], -1, 0, ["num"], 1040)
+    cp(col(0), T.ci[:, 0:1], ["pint"], ["c0"])
+    for j, msk in ((1, 112), (2, 15), (3, 14), (4, 1)):
+        ts(T.ci[:, j:j + 1], T.ci[:, 0:1], msk, None, AL.bitwise_and, None, ["pint"], ["ci%d" % j])
+    cp(T.col[:, 1:5], T.ci[:, 1:5], ["ci1", "ci2", "ci3", "ci4"], ["c1"])
+    ts(am, T.cf[:, 0:128], col(0), None, AL.subtract, None, ["mi", "c0"], ["am"], 128)
+    ts(C("I"), am, 0.0, None, AL.is_equal, None, ["am"], ["I"], 128)
+    ts(C("one"), gi, col(1), None, AL.is_equal, None, ["gi", "c1"], ["one"], 128)
+    ts(T.uu[:, 0:144], mi, 15.0, col(1), AL.subtract, AL.is_equal, ["mi", "c1"], ["uu"], 144)
+    io(C("zero"), [[0, 128]], 0, 0, ["zero"], 128)
+
+    def diag(out, k, wr):
+        add("g", 180.0 + 256, lambda: g.affine_select(out, C("zero"), [[-1, 128]], AL.not_equal, k, 0, 1), ["zero"], wr)
+    for n, k in (("nI", -1.0), ("I5", 5.0)):
+        ts(C(n), C("I"), k, None, AL.mult, None, ["I"], [n], 128, 0.5)
+    for n, k in (("sI", SW), ("nsI", -SW), ("hI", 0.5), ("nhI", -0.5), ("I64", 64.0), ("nI64", -64.0), ("I6", FAR)):
+        act(C(n), C("I"), AF.Copy, ["I"], [n], 128, scale=k)
+    for n, k in (("one64", 64.0), ("none", -1.0), ("qone", 0.25), ("one2k", 2048.0)):
+        ts(C(n), C("one"), k, None, AL.mult, None, ["one"], [n], 128, 0.5)
+    for n, k in (("sone", SW), ("nsone", -SW), ("bigone", 1024.0), ("hugeone", -2.0 ** 90), ("one384", 64.0 * FAR)):
+        act(C(n), C("one"), AF.Copy, ["one"], [n], 128, scale=k)
+    for k in range(16):
+        diag(T.bw[:, 128 * k:128 * k + 128], 4.0 ** -k, ["bw%d" % k])
+    ml = T.cf[:, 272:400]
+    ts(t1, ml, 0.0, None, AL.is_equal, None, ["mlo"], ["t1"], 128)
+    ts(t2, ml, 0.0, 4.0, AL.not_equal, AL.mult, ["mlo"], ["t2"], 128)
+    scan(t3, t2, t1, AL.mult, AL.add, ["t1", "t2"], ["t3"], 128)
+    tt(C("S4"), t3, C("one"), AL.mult, ["t3", "one"], ["S4"], 128)
+    ts(t4, ml, 0.0, 0.25, AL.not_equal, AL.mult, ["mlo"], ["t4"], 128)
+    scan(t5, t4, t1, AL.mult, AL.add, ["t1", "t4"], ["t5"], 128)
+    tt(t4, t5, C("I"), AL.mult, ["t5", "I"], ["t4"], 128)
+    add("v", vc(128, 1.0), lambda: V.tensor_reduce(col(5), t4, AxisListType.X, AL.add), ["t4"], ["c5"])
+    ts(C("T4"), C("S4"), col(5), None, AL.mult, None, ["S4", "c5"], ["T4"], 128, 0.5)
+    ts(t2, am, 0.0, -93.0 / 64, AL.is_gt, AL.mult, ["am"], ["t2"], 128)
+    ts(t3, C("I"), 67.0 / 64, -3.0 / 64, AL.mult, AL.add, ["I"], ["t3"], 128)
+    tt(t5, t2, t3, AL.add, ["t2", "t3"], ["t5"], 128)
+    tt(C("Mw"), t5, C("one"), AL.mult, ["t5", "one"], ["Mw"], 128)
+    ts(C("Kw"), C("one"), col(2), None, AL.mult, None, ["one", "c1"], ["Kw"], 128, 0.5)
+    ts(C("Hw"), C("one64"), col(3), None, AL.mult, None, ["one64", "c1"], ["Hw"], 128, 0.5)
+    ts(col(6), col(4), 64.0, -1.0, AL.mult, AL.add, ["c1"], ["c6"])
+    ts(C("Lw"), C("one"), col(6), None, AL.mult, None, ["one", "c6"], ["Lw"], 128, 0.5)
+    ts(dg, T.cf[:, 272:336], col(2), None, AL.is_equal, None, ["mlo", "c1"], ["dg"])
+    CMg, CMj, NP, ONE, ICB = T.cm[:, 0:64], T.cm[:, 64:128], T.cm[:, 320:384], T.cm[:, 384:448], T.cm[:, 448:456]
+    ts(t6, T.cf[:, 0:64], 16.0, LOW + 16.0, AL.mult, AL.add, ["mi"], ["t6"])
+    tt(t6, t6, dg, AL.mult, ["t6", "dg"], ["t6"])
+    ts(CMg, t6, -LOW, None, AL.add, None, ["t6"], ["CMg"])
+    ts(CMj, t6, -LOW - 2048.0, None, AL.add, None, ["t6"], ["CMj"])
+    for q, k in enumerate((-3056.0, 0.0, 1.0)):
+        ts(T.cm[:, 128 + 64 * q:192 + 64 * q], dg, LOW + k, -LOW, AL.mult, AL.add, ["dg"], ["CMq%d" % q])
+    for q, k in enumerate((-3056.0 - 3088.0, 0.0, 1.0)):
+        ts(T.cm[:, 576 + 64 * q:640 + 64 * q], dg, LOW + k, -LOW, AL.mult, AL.add, ["dg"], ["CMg%d" % q])
+    ts(C("Gw"), C("one64"), col(4), None, AL.mult, None, ["one64", "c1"], ["Gw"], 128, 0.5)
+    CMR = ["CMq0", "CMq1", "CMq2", "CMg0", "CMg1", "CMg2"]
+    fill(ONE, 1.0, ["ONE"])
+    SIX = T.cm[:, 512:576]
+    fill(SIX, FAR, ["SIX"])
+    ts(NP, ONE, 0.5, col(2), AL.mult, AL.subtract, ["ONE", "c1"], ["NP"])
+    ts(T.rs[:], mlo, 0.0, -1.0e6, AL.is_equal, AL.mult, ["mlo"], ["rs"], 192)
+    ts(ICB, T.cf[:, 0:8], 16.0, col(2), AL.mult, AL.add, ["mi", "c1"], ["icb"])
+    ts(m16, T.cf[:, 0:16], col(2), None, AL.is_equal, None, ["mi", "c1"], ["m16"])
+    RK1 = []
+    for r in range(16):
+        act(T.rk[:, 64 * r:64 * r + 64], c64, AF.Identity, ["c64", "m16"], ["rk%d" % r], scale=T.cf[:, 1168 + r:1169 + r])
+        RK1.append("rk%d" % r)
+    act(T.rk[:, 5120:RKN], T.rk[:, 0:RKN - 5120], AF.Copy, ["rk0"], ["rkt"], 8)
+
+    def repeat():
+        for j in range(1, 5):
+            Q.dma_start(T.rk[:, 1024 * j:1024 * j + 1024], T.rk[:, 0:1024]).then_inc(T.sem.tb, 16)
+    add("s", 240.0, repeat, RK1 + ["sts0", "sts1", "ivs"], ["rkw"], own=("tb", 64), lat=4000.0)
+    RK5 = RK1 + ["rkt", "rkw"]
+    fill(T.snd[:, 3:2560:4], 0.0, ["snd%d_%dq" % (s, h) for s in range(5) for h in range(2)], 1280)
+    fill(T.snd[:, 2:512:4], -FAR, ["snd0_0p1", "snd0_1p1"], 256)
+    for h in range(2):
+        fill(T["yy%d" % h][:, 0:16], -FAR, ["ym%d" % h])
+    cp(T.lw[:], T.ivs[:], ["ivs"], ["lw"], 1024)
+
+    ts(T.ci[:, 8:16], T.e0s[:], 896, None, AL.bitwise_and, None, ["e0s"], ["i8"])
+    tt(T.ci[:, 16:24], T.ci[:, 8:16], ICB, AL.add, ["i8", "icb"], ["i16"], 8)
+    ts(T.ci[:, 24:32], T.e0s[:], 5.0, 1.0, AL.mult, AL.add, ["e0s"], ["i24"])
+    ts(T.ci[:, 32:40], T.ci[:, 24:32], 1023, None, AL.bitwise_and, None, ["i24"], ["i32"])
+    for h in range(2):
+        b0, off = BLK0[h], T["off%d" % h]
+        cp(off[:, 0:4], T.ci[:, 16 + b0:20 + b0], ["i16"], ["offd%d" % h])
+        cp(off[:, 4:8], T.e0s[:, b0:b0 + 4], ["e0s"], ["offe%d" % h])
+        cp(off[:, 8:12], T.ci[:, 32 + b0:36 + b0], ["i32"], ["offr%d" % h])
+        ts(off[:, 12:16], T.e0s[:, b0:b0 + 4], 1.0, None, AL.add, None, ["e0s"], ["offa%d" % h])
+
+    peers = [T.cores[(rank + b) % len(T.cores)] for b in range(8)]
+    eng = [e for e in topo.engines(core, peers[1]) if all(e in topo.engines(core, d) for d in peers[1:])]
+
+    def head(s, h):
+        tag[0] = 2 * s + h
+        H = str(h)
+        b0 = BLK0[h]
+        off, ps, bk = T["off" + H], T["ps" + H], "ps" + H
+        wf = T["wf" + H]
+        if s > 0:
+            base = 512 * (s - 1) + 64 * b0
+            lo, hi, a1 = [T.land[:, base + 16 * q + 3:base + 256:64] for q in range(3)]
+            LD = ["land%d_%d" % (s - 1, h), "I", "I5", "icb"]
+            mm(group(ps[:, 4:8], [("I", hi), ("I", lo)], 4) + group(ps[:, 0:4], [("I", hi), ("I", T.cm[:, 448 + b0:452 + b0])], 4), LD, ["r0" + H], bk)
+            cp(off[:, 0:8], ps[:, 0:8], ["r0" + H], ["offe" + H, "offd" + H], 8, bank=[bk])
+            mm(group(ps[:, 8:12], [("I5", hi), ("I5", lo), ("I", a1)], 4) + group(ps[:, 12:16], [("I", hi), ("I", lo), ("I", a1)], 4),
+               LD, ["r0" + H], bk)
+            cp(off[:, 8:16], ps[:, 8:16], ["r0" + H], ["offa" + H, "offr" + H], 8, bank=[bk])
+        cp(T["cc" + H][:], T.lw[:].indirect(off[:, 4:8]), ["lw", "offe" + H], ["cc" + H], 64, 2.0)
+        act(wf[:, 0:64], T.lw[:].indirect(off[:, 4:8]), AF.Copy, ["lw", "offe" + H], ["c37" + H], scale=37.0, c=1.5)
+        act(wf[:, 64:128], T.lw[:].indirect(off[:, 0:4]), AF.Copy, ["lw", "offd" + H], ["old" + H], c=1.5)
+
+    def body(s, h):
+        tag[0] = 2 * s + h
+        H = str(h)
+        b0 = BLK0[h]
+        off, ps, bk = T["off" + H], T["ps" + H], "ps" + H
+        yy, dd, bad, em, cc = T["yy" + H], T["dd" + H], T["bad" + H], T["em" + H], T["cc" + H]
+        wbuf, wf, wi, offz = T["wb" + H], T["wf" + H], T["wi" + H], T["offz" + H]
+        last, p0on, p1on = s == STEPS - 1, s >= 1, s >= 2
+        sb = 512 * s + 64 * b0
+        SN = "snd%d_%d" % (s, h)
+
+        def B(n, w=1):
+            j = WB.index(n)
+            return wbuf[:, 64 * j:64 * (j + w)]
+
+        def F(n, w=1):
+            j = WF[n]
+            return wf[:, 64 * j:64 * (j + w)]
+
+        def R(j, w=1):
+            return ps[:, 64 * j:64 * (j + w)]
+
+        def n_(*a):
+            return [x + H for x in a]
+
+        rkw, rkr = (T.rk[:], RK5) if s else (T.rk[:, 0:1024], RK1)
+        act(B("rke", 2), rkw.indirect(off[:, 4:12]), AF.Copy, rkr + n_("offe", "offr"), n_("rke"), 128, c=1.5)
+        if s > 0:
+            base = 512 * (s - 1) + 64 * b0
+            LD = ["land%d_%d" % (s - 1, h)]
+            K1, P0, P1 = [T.land[:, base + j:base + 256:4] for j in range(3)]
+            AO = T.land[:, base + 35:base + 256:64]
+        else:
+            LD, K1 = n_("rke"), B("rke")
+        vg = VG[s][h]
+        cuts = ([0] if vg else []) + [vg + (64 - vg) * j // GS // 2 * 2 for j in range(GS)] + [64]
+        YR = []
+        for j in range(len(cuts) - 1):
+            a, b = cuts[j], cuts[j + 1]
+            src = T.sts[:].indirect(cc[:, a:b])
+            if vg and j == 0:
+                cp(yy[:, 16 + 16 * a:16 + 16 * b], src, ["sts0", "sts1"] + n_("cc"), n_("y%d_" % j), 16 * (b - a), 1.5)
+            else:
+                act(yy[:, 16 + 16 * a:16 + 16 * b], src, AF.Copy, ["sts0", "sts1"] + n_("cc"), n_("y%d_" % j), 16 * (b - a), c=1.5)
+            YR += n_("y%d_" % j)
+        for j in range(len(cuts) - 1, GS + 1):
+            YR += n_("y%d_" % j)
+        tt(wi[:, 0:64], T.num[:].indirect(off[:, 12:16]), F("c37"), AL.add, ["num"] + n_("c37", "offa"), n_("vi"), c=1.8)
+        ts(wi[:, 64:128], wi[:, 0:64], 4095, None, AL.bitwise_and, None, n_("vi"), n_("nv"))
+        tt(F("dv"), wi[:, 64:128], F("old"), AL.subtract, n_("nv", "old"), n_("dv"))
+        act(B("nc"), K1, AF.Relu, LD, n_("nc"), bias=1.0, scale=-1.0)
+        act(B("thr"), B("nc"), AF.Identity, n_("nc"), n_("thr"), bias=4.5, scale=1000.0)
+        mm([(T.pth[:, 64 * j:64 * j + 64], C("I"), B("thr"), True, True, 64) for j in range(4)], n_("thr") + ["I"], ["pth"], "pth")
+        if not p0on:
+            act(B("mid"), K1, AF.Identity, LD, n_("mid"), bias=-126.0)
+        else:
+            tt(B("q0"), B("nc"), P0, AL.mult, LD + n_("nc"), n_("q0"))
+            act(B("qm0"), P0, AF.Relu, LD, n_("qm0"), scale=-1.0)
+            if p1on:
+                tt(B("q1"), B("nc"), P1, AL.mult, LD + n_("nc"), n_("q1"))
+                act(B("qm1"), P1, AF.Relu, LD, n_("qm1"), scale=-1.0)
+                tt(B("pm"), P0, P1, AL.min, LD, n_("pm"))
+                grp(R(1), [("I", K1), ("I", B("nc")), ("hI", B("q0")), ("hI", B("q1"))], LD + n_("nc", "q0", "q1"), n_("r1"), bk)
+                grp(R(2), [("I", B("q0")), ("nI", B("q1"))], n_("q0", "q1"), n_("r2"), bk)
+                act(B("half"), R(2), AF.Abs, n_("r2"), n_("half"), scale=0.5 * EPS1, bank=[bk])
+            else:
+                grp(R(1), [("I", K1), ("I", B("nc")), ("I", B("q0"))], LD + n_("nc", "q0"), n_("r1"), bk)
+            act(B("mid"), R(1), AF.Identity, n_("r1"), n_("mid"), bias=-126.0, bank=[bk])
+        XB = ["px%d%d" % (h, u) for u in range(2)]
+        EM = []
+        for u in range(2):
+            xb = XB[u]
+            px = T[xb]
+            for v in range(ZS):
+                lst = []
+                for kk in range(8 // ZS * v, 8 // ZS * (v + 1)):
+                    lst += group(px[:, 64 * kk:64 * kk + 64], [("nI", B("mid")), ("I", yy[:, 16 + 8 * u + kk:1040:16])])
+                mm(lst, YR + n_("mid") + ["I", "nI"], [xb], xb)
+            sl = slice(512 * u, 512 * u + 512)
+            DD, EU = [], []
+            for v in range(DS):
+                w = 512 // DS
+                act(dd[:, 512 * u + w * v:512 * u + w * v + w], px[:, w * v:w * v + w], AF.Abs, [xb], n_("d%d%d" % (u, v)), w,
+                    bias=-125.0 * EPS1, scale=EPS1, bank=[xb])
+                DD += n_("d%d%d" % (u, v))
+            for v in range(2):
+                sv = slice(512 * u + 256 * v, 512 * u + 256 * v + 256)
+                tt(bad[:, sv], dd[:, sv], T.pth[:, 0:256], AL.is_gt, (DD if DS == 1 else DD[v:v + 1]) + ["pth"], n_("bad%d%d" % (u, v)), 256, bank=["pth"])
+            BD = n_("bad%d0" % u, "bad%d1" % u)
+            if p0on:
+                mm([(px[:], C("sI"), dd[:, sl], True, False, 512)], DD + ["sI"], [xb], xb)
+                if p1on:
+                    mm([(px[:, 64 * kk:64 * kk + 64], C("nsI"), B("half"), False, False, 64) for kk in range(8)], n_("half") + ["nsI", xb], [xb], xb)
+                mm([(px[:], C("bigone"), bad[:, sl], False, True, 512)], BD + ["bigone", xb], [xb], xb)
+                for v in range(ES):
+                    w = 512 // ES
+                    ts(em[:, 512 * u + w * v:512 * u + w * v + w], px[:, w * v:w * v + w], M8, M8, AL.add, AL.is_equal, [xb],
+                       n_("em%d%d" % (u, v)), w, bank=[xb])
+                    EU += n_("em%d%d" % (u, v))
+            EM.append(EU)
+            src, sn = (em, EU) if p0on else (bad, BD)
+            lst = [(T.pr[:, 0:64], T.uu[:, 15 - k:143 - k], src[:, 64 * k:64 * k + 64], False, k == 15, 64) for k in range(8 * u, 8 * u + 8)]
+            if u == 0:
+                if p0on:
+                    lst = [(T.pr[:, 0:64], C("one"), B("nc"), True, False, 64)] + lst
+                else:
+                    lst[0] = lst[0][:3] + (True, False, 64)
+            mm(lst, sn + n_("nc") + ["uu", "one"] + (["pr"] if u else []), ["pr"], "pr")
+        PC, PB = T[XB[0]][:, 0:64], T[XB[1]][:, 0:64]
+        if p0on:
+            mm([(PC, C("I64"), B("nc"), True, False, 64)] + [(PC, C("I"), em[:, 64 * k:64 * k + 64], False, False, 64) for k in range(8)],
+               EM[0] + n_("nc") + ["I", "I64"], [XB[0]], XB[0])
+            mm([(PC, C("I"), em[:, 64 * k:64 * k + 64], False, k == 15, 64) for k in range(8, 16)], EM[1] + ["I", XB[0]], [XB[0]], XB[0])
+            for u in range(2):
+                mm([(PB, T.bw[:, 128 * k:128 * k + 128], em[:, 64 * k:64 * k + 64], k == 0, k == 15, 64) for k in range(8 * u, 8 * u + 8)],
+                   EM[u] + ["bw%d" % k for k in range(16)] + [XB[1]] * u, [XB[1]], XB[1])
+        ts(B("ok"), T.pr[:, 0:64], 16.0 if p0on else 0.0, None, AL.is_equal, None, ["pr"], n_("ok"), bank=["pr"])
+        grp(R(0), [("T4", B("ok"))], n_("ok"), n_("r0"), bk)
+        ts(B("ohj"), R(0), M1, M1 + 1.0, AL.add, AL.is_equal, n_("r0"), n_("ohj"), bank=[bk])
+        tt(F("t"), B("ohj"), F("dv"), AL.mult, n_("ohj", "dv"), n_("t"))
+        add("v", vc(64, 4.0), lambda: V.tensor_tensor(T.lw[:].indirect(off[:, 0:4]), F("t"), F("old"), AL.add),
+            n_("t", "old", "offd"), ["lw"])
+        grp(R(0), [("I", CMj), ("Kw", B("ohj")), ("one2k", B("ohj"))], n_("ohj") + ["CMj"], n_("r0"), bk)
+        scan(F("sj"), T.rs[:, 0:64], R(0), AL.add, AL.max, n_("r0") + ["rs"], n_("sj"), 64, bank=[bk])
+        cp(offz[:, 0:4], wf[:, 64 * WF["sj"] + 15:64 * WF["sj"] + 64:16], n_("sj"), n_("offj"), 4)
+        act(B("zj") if p0on else T.snd[:, sb + 1:sb + 256:4], yy[:].indirect(offz[:, 0:4]), AF.Copy, YR + n_("offj", "ym"),
+            n_("zj") if p0on else [SN + "p0"], c=1.5)
+        OH, OHN = (B("oh"), "oh") if p0on else (B("ohj"), "ohj")
+        FU, fu = (n_("full"), [("nI", B("full"))]) if p1on else ([], [])
+        if p1on:
+            grp(R(3), [("one", B("ohj")), ("nI", B("qm1"))], n_("ohj", "qm1"), n_("r3"), bk)
+            act(B("full"), R(3), AF.Relu, n_("r3"), n_("full"), bank=[bk])
+            pc = T.pth[:, 256 + 128 * h:384 + 128 * h]
+            pc0, pc1 = T.pth[:, 256 + 128 * h:320 + 128 * h], T.pth[:, 320 + 128 * h:384 + 128 * h]
+            mm(group(pc0, [("I", P0)]) + group(pc1, [("I", P1), ("I", SIX), ("I", B("zj"))]), LD + n_("zj") + ["I", "SIX"], n_("pc"), "pth")
+            tt(B("f"), B("pm"), B("zj"), AL.min, n_("pm", "zj"), n_("f"))
+        terms, trd = [("I", B("dr"))], n_("kr")
+        if p0on:
+            act(B("vp"), PC, AF.Exp, [XB[0]], n_("vp"), bias=-64.0 * math.log(32.0), scale=math.log(32.0), bank=[XB[0]])
+            grp(R(3), [("hugeone", B("ok")), ("Mw", B("vp"))], n_("vp", "ok"), n_("r3"), bk)
+            ts(B("win"), R(3), 2.0, None, AL.is_gt, None, n_("r3"), n_("win"), bank=[bk])
+            tt(B("wbb"), B("win"), PB, AL.mult, n_("win") + [XB[1]], n_("wbb"), bank=[XB[1]])
+            grp(R(3), [("T4", B("ok")), ("S4", B("wbb"))], n_("ok", "wbb"), n_("r3"), bk)
+            ts(B("oh"), R(3), M1, M1 + 1.0, AL.add, AL.is_equal, n_("r3"), n_("oh"), bank=[bk])
+            grp(R(0), [("I", CMg), ("Kw", B("oh"))], n_("oh") + ["CMg"], n_("r0"), bk)
+            scan(F("sg"), T.rs[:, 0:64], R(0), AL.add, AL.max, n_("r0") + ["rs"], n_("sg"), 64, bank=[bk])
+            cp(offz[:, 4:8], wf[:, 64 * WF["sg"] + 15:64 * WF["sg"] + 64:16], n_("sg"), n_("offg"), 4)
+            act(B("z0"), yy[:].indirect(offz[:, 4:8]), AF.Copy, YR + n_("offg", "ym"), n_("z0"), c=1.5)
+            tt(B("wz"), B("win"), B("z0"), AL.mult, n_("win", "z0"), n_("wz"))
+            act(B("xg"), B("wz"), AF.Identity, n_("wz"), n_("xg"), bias=770.5)
+        if p1on:
+            grp(R(1), [("I", NP), ("nhI", B("full")), ("one", B("f"))], n_("full", "f") + ["NP"], n_("r1"), bk)
+            ts(F("r"), R(1), M16, M16, AL.add, AL.subtract, n_("r1"), n_("r"), bank=[bk])
+            tt(B("oq"), F("r"), R(1), AL.is_equal, n_("r", "r1"), n_("oq"), bank=[bk])
+            tt(B("fq"), B("oq"), B("f"), AL.mult, n_("oq", "f"), n_("fq"))
+            terms = [("I", B("oq")), ("I", B("fq"))] + terms
+            trd += n_("oq", "fq")
+        mm(group(R(4), [("one", B("ohj"))] + fu) + group(R(5), [("I", ONE), ("none", OH)]), n_("ohj", OHN) + FU + ["I", "ONE", "none", "one", "nI"],
+           n_("r4", "r5"), bk)
+        tt(B("kr", 2), B("rke", 2), R(4, 2), AL.mult, n_("rke", "r4", "r5"), n_("kr"), 128, bank=[bk])
+        if p0on:
+            t0 = [("nI64", B("qm0")), ("one64", B("oh")), ("sone", B("wp0"))] + ([("nI64", B("full"))] if p1on else []) + [("nsone", B("wz"))]
+            CD = ["nI64", "one64", "one384", "sone", "nsone"]
+            if p1on:
+                tt(B("wp0"), B("win"), pc0, AL.mult, n_("win", "pc"), n_("wp0"), bank=["pth"])
+                tt(B("wp1"), B("win"), pc1, AL.mult, n_("win", "pc"), n_("wp1"), bank=["pth"])
+                t1_ = [("nI64", B("qm1")), ("one64", B("oh")), ("one384", B("ohj")), ("sone", B("wp1")), ("nsone", B("wz"))]
+                mm(group(R(6), t0) + group(R(7), t1_), n_("qm0", "oh", "wp0", "wz", "ohj", "qm1", "wp1") + FU + CD, n_("r6", "r7"), bk)
+                ts(B("s0", 2), R(6, 2), M8, M8 + 64.0, AL.add, AL.is_equal, n_("r6", "r7"), n_("s"), 128, bank=[bk])
+                tt(B("u0", 2), B("s0", 2), pc, AL.mult, n_("s", "pc"), n_("u"), 128, bank=["pth"])
+                grp(R(4), [("nI", SIX), ("I6", B("s1")), ("I", B("u1"))], n_("s", "u") + ["SIX"], n_("r4"), bk)
+                tt(B("w"), B("s0"), R(4), AL.mult, n_("s", "r4"), n_("w"), bank=[bk])
+                n0, b0_ = [("I6", B("s1")), ("I", B("u1"))], -FAR
+            else:
+                tt(B("wp0"), B("win"), P0, AL.mult, LD + n_("win"), n_("wp0"))
+                mm(group(R(6), t0), n_("qm0", "oh", "wp0", "wz") + CD, n_("r6"), bk)
+                ts(B("s0"), R(6), M8, M8 + 64.0, AL.add, AL.is_equal, n_("r6"), n_("s"), bank=[bk])
+                tt(B("u0"), B("s0"), P0, AL.mult, LD + n_("s"), n_("u"))
+                tt(B("w"), B("s0"), B("zj"), AL.mult, n_("s", "zj"), n_("w"))
+                n0, b0_ = [("I", B("zj"))], 0.0
+            mm(group(R(6), n0 + [("I", B("u0")), ("nI", B("w"))]) + group(R(7), [("I6", B("s0")), ("I", B("w"))]),
+               n_("s", "u", "w", "zj") + ["I", "nI", "I6"], n_("r6", "r7"), bk)
+            if last:
+                ts(T.oy0[:, 16 * b0:16 * b0 + 64], R(6), b0_, -1.0, AL.add, AL.max, n_("r6"), n_("oy0"), bank=[bk])
+                ts(T.oy1[:, 16 * b0:16 * b0 + 64], R(7), -FAR, -1.0, AL.add, AL.max, n_("r7"), n_("oy1"), bank=[bk])
+            else:
+                act(T.snd[:, sb + 1:sb + 256:4], R(6), AF.Identity, n_("r6"), [SN + "p0"], bias=b0_, bank=[bk])
+                act(T.snd[:, sb + 2:sb + 256:4], R(7), AF.Identity, n_("r7"), [SN + "p1"], bias=-FAR, bank=[bk])
+        grp(R(2), [("I", B("kr"))] + terms, trd, n_("r2"), bk)
+        act(B("ee"), R(2), AF.Sign, n_("r2"), n_("ee"), bank=[bk])
+        act(B("x4"), R(2), AF.Identity, n_("r2"), n_("x4"), bias=765.5, bank=[bk])
+        if p0on:
+            grp(R(3), [("one", B("oh"))] + fu, n_("oh") + FU, n_("r3"), bk)
+            tt(B("kna"), K1, R(3), AL.mult, LD + n_("r3"), n_("kna"), bank=[bk])
+            grp(R(3), [("I", B("kna"))] + terms + [("I", B("win")), ("I", B("wz"))], n_("kna", "win", "wz") + trd, n_("r3"), bk)
+        KR, KN = (R(3), "r3") if p0on else (R(2), "r2")
+        if last:
+            act(T.oyk[:, 16 * b0:16 * b0 + 64], KR, AF.Identity, n_(KN), n_("oyk"), bias=-1.0, bank=[bk])
+        else:
+            act(T.snd[:, sb:sb + 256:4], KR, AF.Copy, n_(KN), [SN + "k"], bank=[bk])
+        nq = 2 if last else 3
+        cq = 576 if p0on else 128
+        lst = [(R(0, nq), C("I"), T.cm[:, cq:cq + 64 * nq], True, False, 64 * nq), (R(nq - 1), C("none"), OH, False, False, 64)]
+        if p1on:
+            lst.append((R(nq - 1), C("I"), B("full"), False, False, 64))
+        lst += [(R(0), C("Lw"), B("ee"), False, False, 64), (R(0 if last else 1), C("Hw"), B("ee"), False, False, 64),
+                (R(0), C("qone"), B("x4"), False, not p0on, 64)]
+        if p0on:
+            lst += [(R(0), C("Gw"), B("win"), False, False, 64), (R(0 if last else 1), C("Hw"), B("win"), False, False, 64),
+                    (R(0), C("qone"), B("xg"), False, True, 64)]
+        mm(lst, n_(OHN, "x4", "ee") + (n_("win", "xg") if p0on else []) + FU + CMR + ["I", "none", "qone", "Hw", "Lw", "Gw"],
+           n_("r0", "r1", "r2"), bk)
+        scan(F("sc", nq), T.rs[:, 0:64 * nq], R(0, nq), AL.add, AL.max, n_("r0", "r1", "r2") + ["rs"], n_("sc"), 64 * nq, bank=[bk])
+        c0 = 64 * WF["sc"]
+        pick = [wf[:, c0 + 64 * q + 15:c0 + 64 * q + 64:16] for q in range(nq)]
+        if last:
+            act(T.oye[:, b0:b0 + 4], pick[0], AF.Copy, n_("sc"), n_("oye"), 4)
+            tt(T.oya[:, b0:b0 + 4], pick[1], AO, AL.add, n_("sc") + LD, n_("oya"), 4)
+            for nm, q in (("yk", "s"), ("y0", "a"), ("y1", "s")):
+                dma(q, T[nm][:, 16 * b0:16 * b0 + 64], T["o" + nm][:, 16 * b0:16 * b0 + 64], "stored", n_("o" + nm), [], 2000.0)
+            return
+        for q in range(2):
+            act(T.snd[:, sb + 16 * q + 3:sb + 256:64], pick[q], AF.Copy, n_("sc") + [SN + "q"], [SN + "q%d" % q], 4)
+        if s == 0:
+            ts(T.snd[:, sb + 35:sb + 256:64], pick[2], 1.0, None, AL.add, None, n_("sc") + [SN + "q"], [SN + "q2"], 4)
+        else:
+            tt(T.snd[:, sb + 35:sb + 256:64], pick[2], AO, AL.add, n_("sc") + LD + [SN + "q"], [SN + "q2"], 4)
+        SR = [SN + x for x in ("k", "p0", "p1", "q", "q0", "q1", "q2")]
+        blocks = [b for b in range(b0, b0 + 4) if b]
+        share = [len(eng) // 4] * 4 if len(blocks) == 4 else [len(eng) // 2, len(eng) // 4, len(eng) // 4]
+        sem = "arr%d" % (2 * s + h)
+        trs, at = [], 0
+        for b, n in zip(blocks, share):
+            rid, pid = topo.addr(peers[b], core)
+            m = sum(1 << e for e in eng[at:at + n])
+            at += n
+            piece = slice(512 * s + 64 * b, 512 * s + 64 * b + 64)
+            trs.append(RemoteDMATransfer(dst_ids=[DstId(rid=rid, pnc=pid)], dma_engine_mask=m, remote_sem=T.sem[sem],
+                                         src=T.snd[:, piece], dst=T.land[:, piece]))
+        if h == 1:
+            at += 16
+            add("s", 60.0, lambda: Q.dma_start(T.land[:, 512 * s:512 * s + 64], T.snd[:, 512 * s:512 * s + 64]).then_inc(T.sem[sem], 16),
+                SR, ["stay%d" % s], own=("none", 0), lat=0.0)
+        add("g", 900.0, lambda: g.remote_dma_fused(trs, local_sem=T.sem.sent), SR + (["@stay%d" % s] if h == 1 else []),
+            ["land%d_%d" % (s, h)], own=(sem, -at), lat=2600.0)
+
+    for s in range(STEPS):
+        head(s, 0)
+        head(s, 1)
+        body(s, 0)
+        body(s, 1)
+    for u in range(2):
+        xb = "px0%d" % u
+        pz = T[xb]
+        act(pz[:, 0:256], T.lw[:, 512 + 256 * u:768 + 256 * u], AF.Copy, ["lw"], [xb], 256, scale=4096.0, bank=[xb])
+        tt(T.oyi[:, 256 * u:256 * u + 256], T.lw[:, 256 * u:256 * u + 256], pz[:, 0:256], AL.add, ["lw", xb], ["oyi%d" % u], 256, bank=[xb])
+        dma("s", T.yi[:, 256 * u:256 * u + 256], T.oyi[:, 256 * u:256 * u + 256], "stored", ["oyi%d" % u], [], 2600.0)
+    dma("s", T.ye[:], T.oye[:], "stored", ["oye0", "oye1"], [], 2000.0)
+    dma("a", T.ya[:], T.oya[:], "stored", ["oya0", "oya1"], [], 2000.0)
+    return ops, len(eng)
+
+
+def depends(ops):
+    n = len(ops)
+    pred = [set() for _ in range(n)]
+    soft = [set() for _ in range(n)]
+    lw, rd = {}, {}
+    for i, o in enumerate(ops):
+        for r in o[3]:
+            if r[0] == "@":
+                soft[i].add(lw[r[1:]])
+            elif r in lw:
+                pred[i].add(lw[r])
+        for w in o[4]:
+            if w in lw:
+                pred[i].add(lw[w])
+            pred[i].update(rd.get(w, ()))
+        for r in o[3]:
+            rd.setdefault(r, []).append(i)
+        for w in o[4]:
+            lw[w] = i
+            rd[w] = []
+        pred[i].discard(i)
+    return pred, soft
+
+
+def schedule(ops, pred0, soft, lead, slack, noise, rng):
+    n = len(ops)
+    pred = [set(x) for x in pred0]
+    succ = [[] for _ in range(n)]
+    left = [0] * n
+    for i in range(n):
+        for j in pred[i] | soft[i]:
+            succ[j].append(i)
+            left[i] += 1
+    prio = [0.0] * n
+    for i in range(n - 1, -1, -1):
+        prio[i] = ops[i][1] + ops[i][7] + max([prio[j] for j in succ[i]], default=0.0)
+    jit = rng.random(n)
+    key = [prio[i] - lead * (ops[i][8] % 2 if ops[i][8] >= 0 else 0) + noise * float(jit[i]) for i in range(n)]
+    free, done, bankl, base = {}, [0.0] * n, {}, [0.0] * n
+    ready = [i for i in range(n) if left[i] == 0]
+    order = []
+
+    def start(i):
+        t = max(free.get(ops[i][0], 0.0), base[i])
+        for b in ops[i][5]:
+            j = bankl.get(b)
+            if j is not None and ops[j][0] != ops[i][0]:
+                t = max(t, done[j])
+        return t
+    while ready:
+        st = [(start(i), i) for i in ready]
+        t0, i0 = min(st)
+        i = max([i for t, i in st if ops[i][0] == ops[i0][0] and t <= t0 + slack], key=lambda x: key[x])
+        t = start(i)
+        for b in ops[i][5]:
+            j = bankl.get(b)
+            if j is not None and ops[j][0] != ops[i][0]:
+                pred[i].add(j)
+            bankl[b] = i
+        free[ops[i][0]] = t + ops[i][1]
+        done[i] = t + ops[i][1] + ops[i][7]
+        order.append(i)
+        ready.remove(i)
+        for j in succ[i]:
+            left[j] -= 1
+            if left[j] == 0:
+                base[j] = max([done[x] for x in pred0[j]], default=0.0)
+                ready.append(j)
+    return order, pred
+
+
+def replay(ops, order, pred, scale, lat):
+    free, done = {}, {}
+    for i in order:
+        e = ops[i][0]
+        t = max([free.get(e, 0.0)] + [done[j] for j in pred[i] if not (e == "p" and ops[j][0] == "p")])
+        free[e] = t + ops[i][1] * scale.get(e, 1.0)
+        done[i] = free[e] + ops[i][7] * lat
+    return max(done.values()), done
+
+
+CASES = (({}, 1.0), ({"p": 1.6}, 1.0), ({"v": 0.8, "p": 0.8}, 1.5))
+
+
+def place_all(ops, before, key, back):
+    n = len(ops)
+    after = [[] for _ in range(n)]
+    left = [len(x) for x in before]
+    for i in range(n):
+        for j in before[i]:
+            after[j].append(i)
+    busy, start, done = {}, [0.0] * n, [0.0] * n
+    ready = [i for i in range(n) if left[i] == 0]
+    while ready:
+        i = min(ready, key=lambda x: key[x])
+        ready.remove(i)
+        e, c, lat = ops[i][0], ops[i][1], ops[i][7]
+        t = 0.0
+        for j in before[i]:
+            if e == "p" and ops[j][0] == "p":
+                t = max(t, done[j] - (lat if back else ops[j][7]))
+            else:
+                t = max(t, done[j])
+        need = [(e, lat if back else 0.0, c)] + [(b, 0.0, c + lat) for b in ops[i][5]]
+        moved = True
+        while moved:
+            moved = False
+            for r, o, w in need:
+                for a, b, who in busy.get(r, ()):
+                    if a < t + o + w and t + o < b and (r == e or who != e):
+                        t = b - o
+                        moved = True
+        for r, o, w in need:
+            busy.setdefault(r, []).append((t + o, t + o + w, e))
+        start[i], done[i] = t, t + c + lat
+        for j in after[i]:
+            left[j] -= 1
+            if left[j] == 0:
+                ready.append(j)
+    return start, done
+
+
+def ordered(ops, pred0, before, start):
+    n = len(ops)
+    rank = list(start)
+    for i in range(n):
+        for j in before[i]:
+            rank[i] = max(rank[i], rank[j] + 1e-6)
+    order = sorted(range(n), key=lambda x: (rank[x], x))
+    pred = [set(x) for x in pred0]
+    bankl = {}
+    for i in order:
+        for b in ops[i][5]:
+            j = bankl.get(b)
+            if j is not None and ops[j][0] != ops[i][0]:
+                pred[i].add(j)
+            bankl[b] = i
+    return order, pred
+
+
+def plan(ops):
+    pred0, soft = depends(ops)
+    n = len(ops)
+    before = [pred0[i] | soft[i] for i in range(n)]
+    rev = [set() for _ in range(n)]
+    for i in range(n):
+        for j in before[i]:
+            rev[j].add(i)
+    rng = np.random.default_rng(SEED)
+    best = None
+    for j in range(TRIES):
+        lead, slack = float(rng.choice([0.0, 2000.0, 4000.0, 7000.0, 10000.0])), float(rng.choice([40.0, 120.0, 250.0]))
+        order, pred = schedule(ops, pred0, soft, lead, slack, float(rng.choice([0.0, 300.0, 800.0])), rng)
+        cost = [replay(ops, order, pred, a, b)[0] for a, b in CASES]
+        if best is None or sum(cost) < sum(best[0]):
+            best = (cost, order, pred, j)
+    done = replay(ops, best[1], best[2], {}, 1.0)[1]
+    for j in range(TRIES):
+        jit = rng.random((2, n)) * 100.0
+        done = place_all(ops, rev, [float(jit[0, i]) - done[i] for i in range(n)], True)[1]
+        start, done = place_all(ops, before, [float(jit[1, i]) - done[i] for i in range(n)], False)
+        order, pred = ordered(ops, pred0, before, start)
+        cost = [replay(ops, order, pred, a, b)[0] for a, b in CASES]
+        if sum(cost) < sum(best[0]):
+            best = (cost, order, pred, -j)
+    return best
+
+
+def waits(ops, order, pred):
+    pos, cnt = {}, {}
+    for i in order:
+        if ops[i][6] is None:
+            cnt[ops[i][0]] = cnt.get(ops[i][0], 0) + 1
+            pos[i] = (ops[i][0], cnt[ops[i][0]])
+        else:
+            pos[i] = ("x%d" % i, 1)
+    know, at, need = {}, {}, {}
+    place = {x: j for j, x in enumerate(order)}
+    for i in order:
+        e = ops[i][0]
+        k = know.setdefault(e, {})
+        lst = []
+        for j in sorted(pred[i], key=lambda x: -place[x]):
+            if e == "p" and ops[j][0] == "p":
+                continue
+            key, val = pos[j]
+            if k.get(key, 0) >= val:
+                continue
+            lst.append(j)
+            k[key] = val
+            for a, b in at[j].items():
+                if k.get(a, 0) < b:
+                    k[a] = b
+        need[i] = lst
+        arrival = ops[i][6] is not None and ops[i][6][1] < 0
+        at[i] = {} if arrival else dict(k)
+    return need
+
+
+PLAN = {}
+
+
+def rank_program(g, core, T, topo):
+    rank = T.rank_of(core)
+    if rank is None:
+        return
+    ops, neng = build(g, T, topo, core, rank)
+    if "p" not in PLAN:
+        cost, order, pred, how = plan(ops)
+        PLAN["p"] = (order, waits(ops, order, pred), pred, cost, how)
+    order, need = PLAN["p"][:2]
+    wanted = set(j for i in order for j in need[i])
+    queue = {"v": g.vector, "a": g.scalar, "p": g.tensor, "g": g, "s": g.sync}
+    sems = {"v": T.sem.sv, "a": T.sem.sa, "p": T.sem.sp, "g": T.sem.sg}
+    cnt, val, stored = {}, {}, 0
+    for i in order:
+        e, own = ops[i][0], ops[i][6]
+        for j in need[i]:
+            queue[e].wait_ge(val[j][0], val[j][1])
+        ins = ops[i][2]()
+        if own is None:
+            if i in wanted:
+                cnt[e] = cnt.get(e, 0) + 1
+                ins.then_inc(sems[e], 1)
+                val[i] = (sems[e], cnt[e])
+        elif own[0] == "stored":
+            stored += 16
+        elif own[0] != "none":
+            val[i] = (T.sem[own[0]], abs(own[1]))
+    g.wait_ge(T.sem.sent, 2 * (STEPS - 1) * neng)
+    g.sync.wait_ge(T.sem.stored, stored)

@@ -12,15 +12,17 @@ SW = 27.0 / 32.0
 M1, M8, M16 = 1.5 * 2 ** 23, 1.5 * 2 ** 26, 1.5 * 2 ** 27
 LOW = 30000.0
 RKN = 5128
-VG = ((24, 24), (24, 24), (20, 20), (20, 20), (20, 20), (20, 20))
-GS, ZS, DS, ES = 2, 1, 2, 1
-SEED, TRIES = 1, 100
+VG = ((28, 28), (28, 28), (28, 28), (28, 28), (28, 28), (28, 28))
+GS, ZS, DS, ES = 1, 2, 1, 1
+SEED, TRIES, CLIMB, P1V = 1, 30, 500, True
+FIX = {"v": (35.0, 50.0, 0.83, 80.0), "a": (70.0, 130.0, 0.83, 80.0), "p": (30.0, 40.0, 0.96, 120.0)}
+CSEND, CLAND = 600.0, 2400.0
 
 SCRATCH = {
     "sts": ("sbuf", [128, 4096], "bfloat16"), "ivs": ("sbuf", [128, 1024], "int32"), "e0s": ("sbuf", [128, 8], "int32"),
     "lw": ("sbuf", [128, 1024], "float32"), "num": ("sbuf", [128, 1040], "float32"), "rk": ("sbuf", [128, RKN], "bfloat16"),
     "cf": ("sbuf", [128, 1536], "float32"), "ci": ("sbuf", [128, 64], "int32"), "col": ("sbuf", [128, 16], "float32"),
-    "cb": ("sbuf", [128, 28 * 128], "bfloat16"), "bw": ("sbuf", [128, 2048], "bfloat16"), "uu": ("sbuf", [128, 144], "bfloat16"),
+    "cb": ("sbuf", [128, 30 * 128], "bfloat16"), "bw": ("sbuf", [128, 2048], "bfloat16"), "uu": ("sbuf", [128, 144], "bfloat16"),
     "cm": ("sbuf", [128, 768], "bfloat16"), "rs": ("sbuf", [128, 192], "float32"),
     "snd": ("sbuf", [128, 5 * 512], "bfloat16"), "land": ("sbuf", [128, 5 * 512], "bfloat16"),
     "oyk": ("sbuf", [128, 128], "bfloat16"), "oy0": ("sbuf", [128, 128], "bfloat16"), "oy1": ("sbuf", [128, 128], "bfloat16"),
@@ -43,7 +45,7 @@ for _n in ("px00", "px01", "px10", "px11", "pth", "pr", "ps0", "ps1"):
 SEMAPHORES = ["sv", "sa", "sp", "sg", "sent", "le", "li", "ls0", "ls1", "tb", "stored"] + ["arr%d" % k for k in range(10)]
 
 CB = ["I", "nI", "sI", "nsI", "hI", "nhI", "I64", "nI64", "I5", "I6", "one", "one64", "none", "sone", "nsone", "bigone",
-      "hugeone", "qone", "one384", "one2k", "S4", "T4", "Mw", "Kw", "Hw", "Lw", "Gw", "zero"]
+      "hugeone", "qone", "one384", "one2k", "S4", "T4", "Mw", "Kw", "Hw", "Lw", "Gw", "I512", "zero"]
 WB = ["nc", "thr", "q0", "q1", "mid", "half", "qm0", "qm1", "pm", "rke", "rkr", "ok", "ohj", "full", "vp", "win", "wbb", "oh",
       "z0", "zj", "wp0", "wp1", "wz", "s0", "s1", "u0", "u1", "w", "f", "oq", "fq", "kr", "dr", "kna", "ee", "x4", "xg"]
 WF = {"c37": 0, "old": 1, "dv": 2, "t": 3, "sj": 4, "sg": 5, "r": 6, "sc": 7}
@@ -56,6 +58,8 @@ def build(g, T, topo, core, rank):
     V, S, P, Q = g.vector, g.scalar, g.tensor, g.sync
 
     def add(eng, cost, emit, rd, wr, bank=(), own=None, lat=60.0):
+        if own is None and eng in FIX:
+            cost, lat = FIX[eng][1] + FIX[eng][2] * (cost - FIX[eng][0]), FIX[eng][3]
         ops.append((eng, cost, emit, tuple(rd), tuple(wr), tuple(bank), own, lat, tag[0]))
 
     def vc(n, c):
@@ -140,7 +144,7 @@ def build(g, T, topo, core, rank):
 
     def diag(out, k, wr):
         add("g", 180.0 + 256, lambda: g.affine_select(out, C("zero"), [[-1, 128]], AL.not_equal, k, 0, 1), ["zero"], wr)
-    for n, k in (("nI", -1.0), ("I5", 5.0)):
+    for n, k in (("nI", -1.0), ("I5", 5.0), ("I512", 512.0)):
         ts(C(n), C("I"), k, None, AL.mult, None, ["I"], [n], 128, 0.5)
     for n, k in (("sI", SW), ("nsI", -SW), ("hI", 0.5), ("nhI", -0.5), ("I64", 64.0), ("nI64", -64.0), ("I6", FAR)):
         act(C(n), C("I"), AF.Copy, ["I"], [n], 128, scale=k)
@@ -288,8 +292,8 @@ def build(g, T, topo, core, rank):
         ts(wi[:, 64:128], wi[:, 0:64], 4095, None, AL.bitwise_and, None, n_("vi"), n_("nv"))
         tt(F("dv"), wi[:, 64:128], F("old"), AL.subtract, n_("nv", "old"), n_("dv"))
         act(B("nc"), K1, AF.Relu, LD, n_("nc"), bias=1.0, scale=-1.0)
-        act(B("thr"), B("nc"), AF.Identity, n_("nc"), n_("thr"), bias=4.5, scale=1000.0)
-        mm([(T.pth[:, 64 * j:64 * j + 64], C("I"), B("thr"), True, True, 64) for j in range(4)], n_("thr") + ["I"], ["pth"], "pth")
+        ts(B("thr"), K1, 0.5, 4.5 / 512, AL.is_lt, AL.max, LD, n_("thr"))
+        mm([(T.pth[:, 64 * j:64 * j + 64], C("I512"), B("thr"), True, True, 64) for j in range(4)], n_("thr") + ["I512"], ["pth"], "pth")
         if not p0on:
             act(B("mid"), K1, AF.Identity, LD, n_("mid"), bias=-126.0)
         else:
@@ -367,8 +371,8 @@ def build(g, T, topo, core, rank):
         OH, OHN = (B("oh"), "oh") if p0on else (B("ohj"), "ohj")
         FU, fu = (n_("full"), [("nI", B("full"))]) if p1on else ([], [])
         if p1on:
-            grp(R(3), [("one", B("ohj")), ("nI", B("qm1"))], n_("ohj", "qm1"), n_("r3"), bk)
-            act(B("full"), R(3), AF.Relu, n_("r3"), n_("full"), bank=[bk])
+            grp(R(2), [("one", B("ohj")), ("nI", B("qm1"))], n_("ohj", "qm1"), n_("r2"), bk)
+            act(B("full"), R(2), AF.Relu, n_("r2"), n_("full"), bank=[bk])
             pc = T.pth[:, 256 + 128 * h:384 + 128 * h]
             pc0, pc1 = T.pth[:, 256 + 128 * h:320 + 128 * h], T.pth[:, 320 + 128 * h:384 + 128 * h]
             mm(group(pc0, [("I", P0)]) + group(pc1, [("I", P1), ("I", SIX), ("I", B("zj"))]), LD + n_("zj") + ["I", "SIX"], n_("pc"), "pth")
@@ -381,8 +385,8 @@ def build(g, T, topo, core, rank):
             tt(B("wbb"), B("win"), PB, AL.mult, n_("win") + [XB[1]], n_("wbb"), bank=[XB[1]])
             grp(R(3), [("T4", B("ok")), ("S4", B("wbb"))], n_("ok", "wbb"), n_("r3"), bk)
             ts(B("oh"), R(3), M1, M1 + 1.0, AL.add, AL.is_equal, n_("r3"), n_("oh"), bank=[bk])
-            grp(R(0), [("I", CMg), ("Kw", B("oh"))], n_("oh") + ["CMg"], n_("r0"), bk)
-            scan(F("sg"), T.rs[:, 0:64], R(0), AL.add, AL.max, n_("r0") + ["rs"], n_("sg"), 64, bank=[bk])
+            grp(R(6), [("I", CMg), ("Kw", B("oh"))], n_("oh") + ["CMg"], n_("r6"), bk)
+            scan(F("sg"), T.rs[:, 0:64], R(6), AL.add, AL.max, n_("r6") + ["rs"], n_("sg"), 64, bank=[bk])
             cp(offz[:, 4:8], wf[:, 64 * WF["sg"] + 15:64 * WF["sg"] + 64:16], n_("sg"), n_("offg"), 4)
             act(B("z0"), yy[:].indirect(offz[:, 4:8]), AF.Copy, YR + n_("offg", "ym"), n_("z0"), c=1.5)
             tt(B("wz"), B("win"), B("z0"), AL.mult, n_("win", "z0"), n_("wz"))
@@ -403,28 +407,38 @@ def build(g, T, topo, core, rank):
             if p1on:
                 tt(B("wp0"), B("win"), pc0, AL.mult, n_("win", "pc"), n_("wp0"), bank=["pth"])
                 tt(B("wp1"), B("win"), pc1, AL.mult, n_("win", "pc"), n_("wp1"), bank=["pth"])
-                t1_ = [("nI64", B("qm1")), ("one64", B("oh")), ("one384", B("ohj")), ("sone", B("wp1")), ("nsone", B("wz"))]
-                mm(group(R(6), t0) + group(R(7), t1_), n_("qm0", "oh", "wp0", "wz", "ohj", "qm1", "wp1") + FU + CD, n_("r6", "r7"), bk)
-                ts(B("s0", 2), R(6, 2), M8, M8 + 64.0, AL.add, AL.is_equal, n_("r6", "r7"), n_("s"), 128, bank=[bk])
+                x0, X0 = T[XB[0]], XB[0]
+                mm([(x0[:, 0:128], C("nI64"), B("qm0", 2), True, False, 128), (x0[:, 0:64], C("one64"), B("oh"), False, False, 64),
+                    (x0[:, 64:128], C("one64"), B("oh"), False, False, 64), (x0[:, 0:64], C("nI64"), B("full"), False, False, 64),
+                    (x0[:, 64:128], C("one384"), B("ohj"), False, False, 64), (x0[:, 0:128], C("sone"), B("wp0", 2), False, False, 128)],
+                   n_("qm0", "oh", "wp0", "ohj", "qm1", "wp1") + FU + CD, [X0], X0)
+                mm([(x0[:, 0:64], C("nsone"), B("wz"), False, False, 64), (x0[:, 64:128], C("nsone"), B("wz"), False, True, 64)],
+                   n_("wz") + CD + [X0], [X0], X0)
+                ts(B("s0", 2), x0[:, 0:128], M8, M8 + 64.0, AL.add, AL.is_equal, [X0], n_("s"), 128, bank=[X0])
                 tt(B("u0", 2), B("s0", 2), pc, AL.mult, n_("s", "pc"), n_("u"), 128, bank=["pth"])
                 grp(R(4), [("nI", SIX), ("I6", B("s1")), ("I", B("u1"))], n_("s", "u") + ["SIX"], n_("r4"), bk)
                 tt(B("w"), B("s0"), R(4), AL.mult, n_("s", "r4"), n_("w"), bank=[bk])
-                n0, b0_ = [("I6", B("s1")), ("I", B("u1"))], -FAR
+                N1, N0, NB, b0_ = x0[:, 0:64], x0[:, 64:128], X0, -FAR
+                mm([(x0[:, 0:128], C("I6"), B("s0", 2), True, False, 128), (N0, C("I"), B("u0"), False, False, 64),
+                    (N0, C("I"), B("u1"), False, False, 64)], n_("s", "u") + ["I", "I6"], [X0], X0)
+                mm([(N0, C("nI"), B("w"), False, False, 64), (N1, C("I"), B("w"), False, True, 64)], n_("w") + ["I", "nI", X0], [X0], X0)
+                NR = [X0]
             else:
                 tt(B("wp0"), B("win"), P0, AL.mult, LD + n_("win"), n_("wp0"))
                 mm(group(R(6), t0), n_("qm0", "oh", "wp0", "wz") + CD, n_("r6"), bk)
                 ts(B("s0"), R(6), M8, M8 + 64.0, AL.add, AL.is_equal, n_("r6"), n_("s"), bank=[bk])
                 tt(B("u0"), B("s0"), P0, AL.mult, LD + n_("s"), n_("u"))
                 tt(B("w"), B("s0"), B("zj"), AL.mult, n_("s", "zj"), n_("w"))
-                n0, b0_ = [("I", B("zj"))], 0.0
-            mm(group(R(6), n0 + [("I", B("u0")), ("nI", B("w"))]) + group(R(7), [("I6", B("s0")), ("I", B("w"))]),
-               n_("s", "u", "w", "zj") + ["I", "nI", "I6"], n_("r6", "r7"), bk)
+                N0, N1, NB, b0_, NR = R(6), R(7), bk, 0.0, n_("r6", "r7")
+                mm(group(R(6), [("I", B("zj")), ("I", B("u0")), ("nI", B("w"))]) + group(R(7), [("I6", B("s0")), ("I", B("w"))]),
+                   n_("s", "u", "w", "zj") + ["I", "nI", "I6"], NR, bk)
             if last:
-                ts(T.oy0[:, 16 * b0:16 * b0 + 64], R(6), b0_, -1.0, AL.add, AL.max, n_("r6"), n_("oy0"), bank=[bk])
-                ts(T.oy1[:, 16 * b0:16 * b0 + 64], R(7), -FAR, -1.0, AL.add, AL.max, n_("r7"), n_("oy1"), bank=[bk])
+                ts(T.oy0[:, 16 * b0:16 * b0 + 64], N0, b0_, -1.0, AL.add, AL.max, NR, n_("oy0"), bank=[NB])
+                ts(T.oy1[:, 16 * b0:16 * b0 + 64], N1, -FAR, -1.0, AL.add, AL.max, NR, n_("oy1"), bank=[NB])
             else:
-                act(T.snd[:, sb + 1:sb + 256:4], R(6), AF.Identity, n_("r6"), [SN + "p0"], bias=b0_, bank=[bk])
-                act(T.snd[:, sb + 2:sb + 256:4], R(7), AF.Identity, n_("r7"), [SN + "p1"], bias=-FAR, bank=[bk])
+                act(T.snd[:, sb + 1:sb + 256:4], N0, AF.Identity, NR, [SN + "p0"], bias=b0_, bank=[NB])
+                ts(T.snd[:, sb + 2:sb + 256:4], N1, -FAR, None, AL.add, None, NR, [SN + "p1"], bank=[NB]) if P1V else \
+                    act(T.snd[:, sb + 2:sb + 256:4], N1, AF.Identity, NR, [SN + "p1"], bias=-FAR, bank=[NB])
         grp(R(2), [("I", B("kr"))] + terms, trd, n_("r2"), bk)
         act(B("ee"), R(2), AF.Sign, n_("r2"), n_("ee"), bank=[bk])
         act(B("x4"), R(2), AF.Identity, n_("r2"), n_("x4"), bias=765.5, bank=[bk])
@@ -439,17 +453,19 @@ def build(g, T, topo, core, rank):
             act(T.snd[:, sb:sb + 256:4], KR, AF.Copy, n_(KN), [SN + "k"], bank=[bk])
         nq = 2 if last else 3
         cq = 576 if p0on else 128
-        lst = [(R(0, nq), C("I"), T.cm[:, cq:cq + 64 * nq], True, False, 64 * nq), (R(nq - 1), C("none"), OH, False, False, 64)]
+        X1 = XB[1]
+        QA, QL, QH, QN = T[X1][:, 0:64 * nq], T[X1][:, 0:64], T[X1][:, 64 * (nq - 2):64 * (nq - 1)], T[X1][:, 64 * (nq - 1):64 * nq]
+        lst = [(QA, C("I"), T.cm[:, cq:cq + 64 * nq], True, False, 64 * nq), (QN, C("none"), OH, False, False, 64)]
         if p1on:
-            lst.append((R(nq - 1), C("I"), B("full"), False, False, 64))
-        lst += [(R(0), C("Lw"), B("ee"), False, False, 64), (R(0 if last else 1), C("Hw"), B("ee"), False, False, 64),
-                (R(0), C("qone"), B("x4"), False, not p0on, 64)]
+            lst.append((QN, C("I"), B("full"), False, False, 64))
         if p0on:
-            lst += [(R(0), C("Gw"), B("win"), False, False, 64), (R(0 if last else 1), C("Hw"), B("win"), False, False, 64),
-                    (R(0), C("qone"), B("xg"), False, True, 64)]
-        mm(lst, n_(OHN, "x4", "ee") + (n_("win", "xg") if p0on else []) + FU + CMR + ["I", "none", "qone", "Hw", "Lw", "Gw"],
-           n_("r0", "r1", "r2"), bk)
-        scan(F("sc", nq), T.rs[:, 0:64 * nq], R(0, nq), AL.add, AL.max, n_("r0", "r1", "r2") + ["rs"], n_("sc"), 64 * nq, bank=[bk])
+            lst += [(QL, C("Gw"), B("win"), False, False, 64), (QH, C("Hw"), B("win"), False, False, 64)]
+        mm(lst, n_(OHN) + (n_("win") if p0on else []) + FU + CMR + ["I", "none", "Hw", "Gw"], [X1], X1)
+        mm([(QL, C("Lw"), B("ee"), False, False, 64), (QH, C("Hw"), B("ee"), False, False, 64), (QL, C("qone"), B("x4"), False, not p0on, 64)],
+           n_("x4", "ee") + ["qone", "Hw", "Lw", X1], [X1], X1)
+        if p0on:
+            mm([(QL, C("qone"), B("xg"), False, True, 64)], n_("xg") + ["qone", X1], [X1], X1)
+        scan(F("sc", nq), T.rs[:, 0:64 * nq], QA, AL.add, AL.max, [X1, "rs"], n_("sc"), 64 * nq, bank=[X1])
         c0 = 64 * WF["sc"]
         pick = [wf[:, c0 + 64 * q + 15:c0 + 64 * q + 64:16] for q in range(nq)]
         if last:
@@ -480,8 +496,8 @@ def build(g, T, topo, core, rank):
             at += 16
             add("s", 60.0, lambda: Q.dma_start(T.land[:, 512 * s:512 * s + 64], T.snd[:, 512 * s:512 * s + 64]).then_inc(T.sem[sem], 16),
                 SR, ["stay%d" % s], own=("none", 0), lat=0.0)
-        add("g", 900.0, lambda: g.remote_dma_fused(trs, local_sem=T.sem.sent), SR + (["@stay%d" % s] if h == 1 else []),
-            ["land%d_%d" % (s, h)], own=(sem, -at), lat=2600.0)
+        add("g", CSEND, lambda: g.remote_dma_fused(trs, local_sem=T.sem.sent), SR + (["@stay%d" % s] if h == 1 else []),
+            ["land%d_%d" % (s, h)], own=(sem, -at), lat=CLAND)
 
     for s in range(STEPS):
         head(s, 0)
@@ -580,7 +596,7 @@ def replay(ops, order, pred, scale, lat):
     return max(done.values()), done
 
 
-CASES = (({}, 1.0), ({"p": 1.6}, 1.0), ({"v": 0.8, "p": 0.8}, 1.5))
+CASES = (({}, 1.0), ({"p": 1.3}, 0.6), ({"a": 1.15}, 1.4))
 
 
 def place_all(ops, before, key, back):
@@ -598,7 +614,10 @@ def place_all(ops, before, key, back):
         e, c, lat = ops[i][0], ops[i][1], ops[i][7]
         t = 0.0
         for j in before[i]:
-            if e == "p" and ops[j][0] == "p":
+            if ops[i][6] is not None and ops[j][6] is not None and ops[i][8] < 0 and ops[j][8] < 0 and ops[i][0] == ops[j][0] \
+                    and "tb" not in (ops[i][6][0], ops[j][6][0]):
+                t = max(t, start[j])
+            elif e == "p" and ops[j][0] == "p":
                 t = max(t, done[j] - (lat if back else ops[j][7]))
             else:
                 t = max(t, done[j])
@@ -664,6 +683,18 @@ def plan(ops):
         cost = [replay(ops, order, pred, a, b)[0] for a, b in CASES]
         if sum(cost) < sum(best[0]):
             best = (cost, order, pred, -j)
+    for j in range(CLIMB):
+        done = replay(ops, best[1], best[2], {}, 1.0)[1]
+        jit = rng.random(n) * float(rng.choice([150.0, 400.0, 900.0])) * (rng.random(n) < 0.3)
+        if j % 2:
+            done = place_all(ops, rev, [float(jit[i]) - done[i] for i in range(n)], True)[1]
+            key = [-x for x in done]
+        else:
+            key = [done[i] - ops[i][1] - ops[i][7] - float(jit[i]) for i in range(n)]
+        order, pred = ordered(ops, pred0, before, place_all(ops, before, key, False)[0])
+        cost = [replay(ops, order, pred, a, b)[0] for a, b in CASES]
+        if sum(cost) < sum(best[0]):
+            best = (cost, order, pred, 1000 + j)
     return best
 
 

@@ -6,49 +6,61 @@ from concourse.mybir import AluOpType, AxisListType, ActivationFunctionType
 AL = AluOpType
 AF = ActivationFunctionType
 STEPS = 6
-FAR = 6.0
-EPS1 = 1.0 + 2.0 ** -10
-SW = 27.0 / 32.0
+SH = 8.0
+C0 = 296.0
+CC = C0 - SH
+BIG = 264.0
+MIDO = 792.0
+L = 1024.0
 M1, M8, M16 = 1.5 * 2 ** 23, 1.5 * 2 ** 26, 1.5 * 2 ** 27
 LOW = 30000.0
-RKN = 5128
-VG = ((28, 28), (28, 28), (28, 28), (28, 28), (28, 28), (28, 28))
-GS, ZS, DS, ES = 1, 2, 1, 1
-SEED, TRIES, CLIMB, P1V = 1, 30, 500, True
+B1 = 1039
+TWN = B1 + 5128
+HB = 20480.0
+VG = (32, 32, 16, 16, 16, 16)
+ONA = ("I4", "I5", "I64", "wI", "hugeone", "L2one", "nhone", "NP", "CD", "nCI", "CI", "C0I", "nqI", "nLI", "eI", "neI", "nB", "qone",
+       "W64", "W62", "Kw", "CMg", "hI", "jc", "jr") + tuple("rk%d" % r for r in range(0, 16, 2))
+OPT = {"ci": "a", "kout": "a", "rmode": True}
+SEED, TRIES, CLIMB, ROUNDS = 1, 8, 60, 40000
 FIX = {"v": (35.0, 50.0, 0.83, 80.0), "a": (70.0, 130.0, 0.83, 80.0), "p": (30.0, 40.0, 0.96, 120.0)}
 CSEND, CLAND = 600.0, 2400.0
 
+CB = ["I", "nI", "hI", "one", "T4", "S4", "Mw", "hugeone", "Kw", "nB", "BC", "nCI", "CI", "C0I", "nqI", "Lone", "nLone", "L2one",
+      "nLI", "nhone", "eI", "I4", "I5", "I64", "qone", "W64", "wI", "none", "neI", "nP2", "Q2"]
+CH = ["W62", "Kw2"]
+WB = ["ci", "ok", "vp", "win", "bit", "oh", "oq"]
+WH = {"k0": 0, "ra": 1, "rb": 2, "pm": 3, "mx": 4, "mid": 5, "hf": 6, "e1": 7, "er": 8, "zj": 9, "ljn": 10, "jb": 11, "f": 12, "fq": 13,
+      "wz": 14, "s": 15, "kk": 17, "dr": 18, "de": 19, "se": 20, "y1": 21}
+WF = {"sj": 0, "sg": 1, "r": 2, "prs": 3, "y": 4, "ry": 5}
+
 SCRATCH = {
     "sts": ("sbuf", [128, 4096], "bfloat16"), "ivs": ("sbuf", [128, 1024], "int32"), "e0s": ("sbuf", [128, 8], "int32"),
-    "lw": ("sbuf", [128, 1024], "float32"), "num": ("sbuf", [128, 1040], "float32"), "rk": ("sbuf", [128, RKN], "bfloat16"),
+    "lw": ("sbuf", [128, 1024], "float32"), "tw": ("sbuf", [128, TWN], "float32"),
     "cf": ("sbuf", [128, 1536], "float32"), "ci": ("sbuf", [128, 64], "int32"), "col": ("sbuf", [128, 16], "float32"),
-    "cb": ("sbuf", [128, 30 * 128], "bfloat16"), "bw": ("sbuf", [128, 2048], "bfloat16"), "uu": ("sbuf", [128, 144], "bfloat16"),
-    "cm": ("sbuf", [128, 768], "bfloat16"), "rs": ("sbuf", [128, 192], "float32"),
-    "snd": ("sbuf", [128, 5 * 512], "bfloat16"), "land": ("sbuf", [128, 5 * 512], "bfloat16"),
+    "cb": ("sbuf", [128, len(CB) * 128], "bfloat16"), "ch": ("sbuf", [128, len(CH) * 128 + 160], "float16"),
+    "bw": ("sbuf", [128, 2048], "bfloat16"), "uu": ("sbuf", [128, 144], "bfloat16"),
+    "cm": ("sbuf", [128, 320], "bfloat16"), "rs": ("sbuf", [128, 128], "float32"),
+    "snd": ("sbuf", [128, 6 * 128, 5], "float16"), "land": ("sbuf", [128, 5 * 128, 5], "float16"),
+    "offw": ("sbuf", [128, 32], "uint16"), "ee": ("sbuf", [128, 256], "float16"), "hb": ("sbuf", [128, 8], "bfloat16"), "ohj": ("sbuf", [128, 128], "bfloat16"),
+    "jf": ("sbuf", [128, 4 * 128], "float32"), "ji": ("sbuf", [128, 256], "int32"),
     "oyk": ("sbuf", [128, 128], "bfloat16"), "oy0": ("sbuf", [128, 128], "bfloat16"), "oy1": ("sbuf", [128, 128], "bfloat16"),
     "oye": ("sbuf", [128, 8], "float32"), "oya": ("sbuf", [128, 8], "float32"), "oyi": ("sbuf", [128, 512], "float32"),
 }
 for _h in range(2):
     SCRATCH["yy%d" % _h] = ("sbuf", [128, 1040], "bfloat16")
-    SCRATCH["dd%d" % _h] = ("sbuf", [128, 1024], "bfloat16")
-    SCRATCH["bad%d" % _h] = ("sbuf", [128, 1024], "bfloat16")
+    SCRATCH["dd%d" % _h] = ("sbuf", [128, 1024], "float16")
+    SCRATCH["gd%d" % _h] = ("sbuf", [128, 1024], "bfloat16")
     SCRATCH["em%d" % _h] = ("sbuf", [128, 1024], "bfloat16")
-    SCRATCH["off%d" % _h] = ("sbuf", [128, 16], "uint16")
+    SCRATCH["off%d" % _h] = ("sbuf", [128, 8], "uint16")
     SCRATCH["offz%d" % _h] = ("sbuf", [128, 8], "uint16")
     SCRATCH["cc%d" % _h] = ("sbuf", [128, 64], "uint16")
-    SCRATCH["wb%d" % _h] = ("sbuf", [128, 40 * 64], "bfloat16")
-    SCRATCH["wf%d" % _h] = ("sbuf", [128, 12 * 64], "float32")
-    SCRATCH["wi%d" % _h] = ("sbuf", [128, 128], "int32")
-for _n in ("px00", "px01", "px10", "px11", "pth", "pr", "ps0", "ps1"):
-    SCRATCH[_n] = ("psum", [128, 512], "float32")
+    SCRATCH["wb%d" % _h] = ("sbuf", [128, len(WB) * 64], "bfloat16")
+    SCRATCH["wh%d" % _h] = ("sbuf", [128, 22 * 64], "float16")
+    SCRATCH["wf%d" % _h] = ("sbuf", [128, 6 * 64], "float32")
+    for _n in ("px0", "px1", "ps", "pt"):
+        SCRATCH[_n + str(_h)] = ("psum", [128, 512], "float32")
 
-SEMAPHORES = ["sv", "sa", "sp", "sg", "sent", "le", "li", "ls0", "ls1", "tb", "stored"] + ["arr%d" % k for k in range(10)]
-
-CB = ["I", "nI", "sI", "nsI", "hI", "nhI", "I64", "nI64", "I5", "I6", "one", "one64", "none", "sone", "nsone", "bigone",
-      "hugeone", "qone", "one384", "one2k", "S4", "T4", "Mw", "Kw", "Hw", "Lw", "Gw", "I512", "zero"]
-WB = ["nc", "thr", "q0", "q1", "mid", "half", "qm0", "qm1", "pm", "rke", "rkr", "ok", "ohj", "full", "vp", "win", "wbb", "oh",
-      "z0", "zj", "wp0", "wp1", "wz", "s0", "s1", "u0", "u1", "w", "f", "oq", "fq", "kr", "dr", "kna", "ee", "x4", "xg"]
-WF = {"c37": 0, "old": 1, "dv": 2, "t": 3, "sj": 4, "sg": 5, "r": 6, "sc": 7}
+SEMAPHORES = ["sv", "sa", "sp", "sg", "sent", "le", "li", "ls0", "ls1", "stored"] + ["arr%d" % k for k in range(10)]
 BLK0 = (4, 0)
 
 
@@ -80,39 +92,52 @@ def build(g, T, topo, core, rank):
     def fill(out, k, wr, n=64):
         add("v", vc(n, 0.5), lambda: V.memset(out, k), [], wr)
 
-    def scan(out, d0, d1, o0, o1, rd, wr, n, bank=()):
-        add("v", vc(n, 1.0), lambda: V.tensor_tensor_scan(out, d0, d1, 0.0, o0, o1), rd, wr, bank)
+    def scan(out, d0, d1, o0, o1, rd, wr, n, bank=(), init=0.0):
+        add("v", vc(n, 1.0), lambda: V.tensor_tensor_scan(out, d0, d1, init, o0, o1), rd, wr, bank)
 
     def act(out, a, f, rd, wr, n=64, bias=0.0, scale=1.0, c=1.0, bank=()):
         add("a", 70.0 + n * c, lambda: S.activation(out, a, f, bias=bias, scale=scale), rd, wr, bank)
+
+    def C(n):
+        if n in CH:
+            j = CH.index(n)
+            return T.ch[:, 128 * j:128 * j + 128]
+        if n[:2] == "uu":
+            k = int(n[2:])
+            return T.uu[:, 15 - k:143 - k]
+        if n[:2] == "bw":
+            k = int(n[2:])
+            return T.bw[:, 128 * k:128 * k + 128]
+        j = CB.index(n)
+        return T.cb[:, 128 * j:128 * j + 128]
 
     def mm(lst, rd, wr, bank):
         def emit():
             last = None
             for o, l, r, a, b, n in lst:
-                last = P.matmul(o, l, r, a, b)
+                last = P.matmul(o, C(l), r, a, b)
             return last
-        add("p", 30.0 + sum(0.5 * max(64, x[5]) for x in lst), emit, rd, wr, [bank], lat=100.0)
+        names = sorted(set("uu" if x[1][:2] == "uu" else x[1] for x in lst))
+        add("p", 30.0 + sum(0.5 * max(64, x[5]) for x in lst), emit, list(rd) + names, wr, [bank], lat=100.0)
 
-    def C(n):
-        j = CB.index(n)
-        return T.cb[:, 128 * j:128 * j + 128]
-
-    def group(out, terms, n=64):
-        return [(out, C(l), r, j == 0, j == len(terms) - 1, n) for j, (l, r) in enumerate(terms)]
-
-    def grp(out, terms, rd, wr, bank):
-        mm(group(out, terms), list(rd) + [l for l, r in terms], wr, bank)
+    def group(out, terms, n=64, start=True, stop=True):
+        return [(out, l, r, start and j == 0, stop and j == len(terms) - 1, n) for j, (l, r) in enumerate(terms)]
 
     def io(out, pat, base, cmul, wr, n, flt=True):
         if flt:
-            add("g", 140.0 + 2 * n, lambda: g.iota(out, pat, base, cmul, allow_small_or_imprecise_dtypes=True), [], wr)
+            add("g", 130.0 + 1.66 * n, lambda: g.iota(out, pat, base, cmul, allow_small_or_imprecise_dtypes=True), [], wr)
         else:
-            add("g", 140.0 + 2 * n, lambda: g.iota(out, pat, base, cmul), [], wr)
+            add("g", 130.0 + 1.66 * n, lambda: g.iota(out, pat, base, cmul), [], wr)
 
     def dma(q, out, in_, sem, rd, wr, lat):
         e = {"s": Q, "a": S}[q]
         add(q, 60.0, lambda: e.dma_start(out, in_).then_inc(T.sem[sem], 16), rd, wr, own=(sem, 16), lat=lat)
+
+    def lin(out, a, k, b, rd, wr, n=64, c=1.0):
+        if wr[0] in ONA:
+            act(out, a, AF.Identity, rd, wr, n, bias=b, scale=k)
+        else:
+            ts(out, a, k, b, AL.mult, AL.add, rd, wr, n, c)
 
     def col(j):
         return T.col[:, j:j + 1]
@@ -122,102 +147,107 @@ def build(g, T, topo, core, rank):
     dma("s", T.sts[:, 0:2048], T.st[:, 0:2048], "ls0", ["@e0s"], ["sts0"], 5000.0)
     dma("a", T.sts[:, 2048:4096], T.st[:, 2048:4096], "ls1", ["@ivs"], ["sts1"], 5500.0)
 
-    mi, gi, mlo, am = T.cf[:, 0:144], T.cf[:, 144:272], T.cf[:, 272:464], T.cf[:, 528:656]
-    t1, t2, t3, c64 = T.cf[:, 656:784], T.cf[:, 784:912], T.cf[:, 912:1040], T.cf[:, 1040:1104]
-    dg, m16, t4, t5 = T.cf[:, 1104:1168], T.cf[:, 1168:1184], T.cf[:, 1184:1312], T.cf[:, 1312:1440]
-    t6 = T.cf[:, 1440:1504]
+    mi, gi, ml, am = T.cf[:, 0:144], T.cf[:, 144:272], T.cf[:, 272:400], T.cf[:, 400:528]
+    t1, t2, t3, t4, t5 = [T.cf[:, 528 + 128 * j:656 + 128 * j] for j in range(5)]
+    dg, m16, t6, t7 = T.cf[:, 1168:1232], T.cf[:, 1232:1248], T.cf[:, 1248:1312], T.cf[:, 1312:1440]
     io(T.ci[:, 0:1], [[0, 1]], 0, 1, ["pint"], 1, False)
     io(mi, [[1, 144]], 0, 0, ["mi"], 144)
     io(gi, [[16, 8], [0, 16]], 0, 0, ["gi"], 128)
-    io(mlo, [[0, 12], [1, 16]], 0, 0, ["mlo"], 192)
-    io(c64, [[4, 64]], 1, 0, ["c64"], 64)
-    io(T.num[:], [[1, 1040]], -1, 0, ["num"], 1040)
+    io(ml, [[0, 8], [1, 16]], 0, 0, ["ml"], 128)
+    io(T.tw[:, 0:B1], [[1, B1]], 0, 0, ["num"], B1)
     cp(col(0), T.ci[:, 0:1], ["pint"], ["c0"])
-    for j, msk in ((1, 112), (2, 15), (3, 14), (4, 1)):
+    for j, msk in ((1, 112), (2, 15)):
         ts(T.ci[:, j:j + 1], T.ci[:, 0:1], msk, None, AL.bitwise_and, None, ["pint"], ["ci%d" % j])
-    cp(T.col[:, 1:5], T.ci[:, 1:5], ["ci1", "ci2", "ci3", "ci4"], ["c1"])
+    cp(T.col[:, 1:3], T.ci[:, 1:3], ["ci1", "ci2"], ["c1"])
     ts(am, T.cf[:, 0:128], col(0), None, AL.subtract, None, ["mi", "c0"], ["am"], 128)
     ts(C("I"), am, 0.0, None, AL.is_equal, None, ["am"], ["I"], 128)
     ts(C("one"), gi, col(1), None, AL.is_equal, None, ["gi", "c1"], ["one"], 128)
-    ts(T.uu[:, 0:144], mi, 15.0, col(1), AL.subtract, AL.is_equal, ["mi", "c1"], ["uu"], 144)
-    io(C("zero"), [[0, 128]], 0, 0, ["zero"], 128)
-
-    def diag(out, k, wr):
-        add("g", 180.0 + 256, lambda: g.affine_select(out, C("zero"), [[-1, 128]], AL.not_equal, k, 0, 1), ["zero"], wr)
-    for n, k in (("nI", -1.0), ("I5", 5.0), ("I512", 512.0)):
-        ts(C(n), C("I"), k, None, AL.mult, None, ["I"], [n], 128, 0.5)
-    for n, k in (("sI", SW), ("nsI", -SW), ("hI", 0.5), ("nhI", -0.5), ("I64", 64.0), ("nI64", -64.0), ("I6", FAR)):
-        act(C(n), C("I"), AF.Copy, ["I"], [n], 128, scale=k)
-    for n, k in (("one64", 64.0), ("none", -1.0), ("qone", 0.25), ("one2k", 2048.0)):
-        ts(C(n), C("one"), k, None, AL.mult, None, ["one"], [n], 128, 0.5)
-    for n, k in (("sone", SW), ("nsone", -SW), ("bigone", 1024.0), ("hugeone", -2.0 ** 90), ("one384", 64.0 * FAR)):
-        act(C(n), C("one"), AF.Copy, ["one"], [n], 128, scale=k)
-    for k in range(16):
-        diag(T.bw[:, 128 * k:128 * k + 128], 4.0 ** -k, ["bw%d" % k])
-    ml = T.cf[:, 272:400]
-    ts(t1, ml, 0.0, None, AL.is_equal, None, ["mlo"], ["t1"], 128)
-    ts(t2, ml, 0.0, 4.0, AL.not_equal, AL.mult, ["mlo"], ["t2"], 128)
+    for src, lst in (("I", (("nI", -1.0), ("hI", 0.5), ("nCI", -CC), ("CI", CC), ("C0I", C0), ("nqI", -0.25), ("nLI", -L), ("eI", 0.5 / L),
+                            ("neI", -1.0 / L), ("I4", 4.0), ("I5", 5.0), ("I64", 64.0), ("wI", 17.0 / 16))),
+                     ("one", (("nB", -BIG), ("Lone", L), ("nLone", -L), ("none", -1.0), ("qone", 0.25), ("hugeone", -2.0 ** 90),
+                              ("L2one", 2 * L), ("nhone", -0.5)))):
+        for n, k in lst:
+            lin(C(n), C(src), k, 0.0, [src], [n], 128, 0.5)
+    tt(C("BC"), C("nCI"), C("nB"), AL.subtract, ["nCI", "nB"], ["BC"], 128)
+    ts(t1, ml, 0.0, None, AL.is_equal, None, ["ml"], ["t1"], 128)
+    ts(t2, ml, 0.0, 2.0, AL.not_equal, AL.mult, ["ml"], ["t2"], 128)
     scan(t3, t2, t1, AL.mult, AL.add, ["t1", "t2"], ["t3"], 128)
-    tt(C("S4"), t3, C("one"), AL.mult, ["t3", "one"], ["S4"], 128)
-    ts(t4, ml, 0.0, 0.25, AL.not_equal, AL.mult, ["mlo"], ["t4"], 128)
+    ts(t4, ml, 0.0, 0.5, AL.not_equal, AL.mult, ["ml"], ["t4"], 128)
     scan(t5, t4, t1, AL.mult, AL.add, ["t1", "t4"], ["t5"], 128)
-    tt(t4, t5, C("I"), AL.mult, ["t5", "I"], ["t4"], 128)
-    add("v", vc(128, 1.0), lambda: V.tensor_reduce(col(5), t4, AxisListType.X, AL.add), ["t4"], ["c5"])
-    ts(C("T4"), C("S4"), col(5), None, AL.mult, None, ["S4", "c5"], ["T4"], 128, 0.5)
-    ts(t2, am, 0.0, -93.0 / 64, AL.is_gt, AL.mult, ["am"], ["t2"], 128)
-    ts(t3, C("I"), 67.0 / 64, -3.0 / 64, AL.mult, AL.add, ["I"], ["t3"], 128)
-    tt(t5, t2, t3, AL.add, ["t2", "t3"], ["t5"], 128)
-    tt(C("Mw"), t5, C("one"), AL.mult, ["t5", "one"], ["Mw"], 128)
-    ts(C("Kw"), C("one"), col(2), None, AL.mult, None, ["one", "c1"], ["Kw"], 128, 0.5)
-    ts(C("Hw"), C("one64"), col(3), None, AL.mult, None, ["one64", "c1"], ["Hw"], 128, 0.5)
-    ts(col(6), col(4), 64.0, -1.0, AL.mult, AL.add, ["c1"], ["c6"])
-    ts(C("Lw"), C("one"), col(6), None, AL.mult, None, ["one", "c6"], ["Lw"], 128, 0.5)
-    ts(dg, T.cf[:, 272:336], col(2), None, AL.is_equal, None, ["mlo", "c1"], ["dg"])
-    CMg, CMj, NP, ONE, ICB = T.cm[:, 0:64], T.cm[:, 64:128], T.cm[:, 320:384], T.cm[:, 384:448], T.cm[:, 448:456]
-    ts(t6, T.cf[:, 0:64], 16.0, LOW + 16.0, AL.mult, AL.add, ["mi"], ["t6"])
-    tt(t6, t6, dg, AL.mult, ["t6", "dg"], ["t6"])
-    ts(CMg, t6, -LOW, None, AL.add, None, ["t6"], ["CMg"])
-    ts(CMj, t6, -LOW - 2048.0, None, AL.add, None, ["t6"], ["CMj"])
-    for q, k in enumerate((-3056.0, 0.0, 1.0)):
-        ts(T.cm[:, 128 + 64 * q:192 + 64 * q], dg, LOW + k, -LOW, AL.mult, AL.add, ["dg"], ["CMq%d" % q])
-    for q, k in enumerate((-3056.0 - 3088.0, 0.0, 1.0)):
-        ts(T.cm[:, 576 + 64 * q:640 + 64 * q], dg, LOW + k, -LOW, AL.mult, AL.add, ["dg"], ["CMg%d" % q])
-    ts(C("Gw"), C("one64"), col(4), None, AL.mult, None, ["one64", "c1"], ["Gw"], 128, 0.5)
-    CMR = ["CMq0", "CMq1", "CMq2", "CMg0", "CMg1", "CMg2"]
-    fill(ONE, 1.0, ["ONE"])
-    SIX = T.cm[:, 512:576]
-    fill(SIX, FAR, ["SIX"])
-    ts(NP, ONE, 0.5, col(2), AL.mult, AL.subtract, ["ONE", "c1"], ["NP"])
-    ts(T.rs[:], mlo, 0.0, -1.0e6, AL.is_equal, AL.mult, ["mlo"], ["rs"], 192)
-    ts(ICB, T.cf[:, 0:8], 16.0, col(2), AL.mult, AL.add, ["mi", "c1"], ["icb"])
     ts(m16, T.cf[:, 0:16], col(2), None, AL.is_equal, None, ["mi", "c1"], ["m16"])
+    for j, src, sn in ((5, t3, "t3"), (6, t5, "t5")):
+        tmp = T.cf[:, 1440 + 16 * (j - 5):1456 + 16 * (j - 5)]
+        tt(tmp, T.cf[:, 784 + 256 * (j - 5):800 + 256 * (j - 5)], m16, AL.mult, [sn, "m16"], ["tm%d" % j], 16)
+        add("v", vc(16, 1.0), lambda tmp=tmp, j=j: V.tensor_reduce(col(j), tmp, AxisListType.X, AL.add), ["tm%d" % j], ["c%d" % j])
+    act(t7, t3, AF.Square, ["t3"], ["t7"], 128)
+    tt(C("S4"), t7, C("one"), AL.mult, ["t7", "one"], ["S4"], 128)
+    ts(C("T4"), C("S4"), col(6), col(6), AL.mult, AL.mult, ["S4", "c6"], ["T4"], 128, 0.5)
+    if OPT["rmode"]:
+        ts(T.cf[:, 528:672], mi, 15.0, col(1), AL.subtract, AL.is_equal, ["mi", "c1", "t1", "t2"], ["t1", "t2"], 144)
+        ts(T.uu[:], T.cf[:, 528:672], col(5), None, AL.mult, None, ["t1", "t2", "c5"], ["uu"], 144)
+        ts(C("nP2"), C("none"), col(5), None, AL.mult, None, ["none", "c5"], ["nP2"], 128, 0.5)
+        ts(C("Q2"), C("one"), col(6), 0.5, AL.mult, AL.mult, ["one", "c6"], ["Q2"], 128, 0.5)
+    else:
+        ts(T.uu[:], mi, 15.0, col(1), AL.subtract, AL.is_equal, ["mi", "c1"], ["uu"], 144)
+        ts(C("nP2"), C("one"), -1.0, None, AL.mult, None, ["one"], ["nP2"], 128, 0.5)
+        for k in range(16):
+            ts(C("bw%d" % k), C("I"), 4.0 ** -k, None, AL.mult, None, ["I"], ["bw%d" % k], 128, 0.5)
+    ts(t4, am, 0.0, -93.0 / 64, AL.is_gt, AL.mult, ["am"], ["t4"], 128)
+    act(t5, C("I"), AF.Identity, ["I"], ["t5"], 128, scale=67.0 / 64, bias=-3.0 / 64)
+    tt(t7, t4, t5, AL.add, ["t4", "t5"], ["t7"], 128)
+    tt(C("Mw"), t7, C("one"), AL.mult, ["t7", "one"], ["Mw"], 128)
+    lin(col(7), col(2), 64.0, -SH / 4, ["c1"], ["c7"], 1)
+    lin(col(8), col(2), 1.0, 1040.0, ["c1"], ["c8"], 1)
+    lin(col(9), col(2), -256.0, C0 - 4 * L, ["c1"], ["c9"], 1)
+    lin(col(10), col(2), -1.0, 0.5, ["c1"], ["c10"], 1)
+    lin(col(11), col(2), -256.0, C0 - 3 * L, ["c1"], ["c11"], 1)
+    lin(col(12), col(2), 64.0, 0.0, ["c1"], ["c12"], 1)
+    for n, j in (("Kw", 2), ("W64", 12), ("W62", 7), ("Kw2", 8)):
+        lin(C(n), C("one"), col(j), 0.0, ["one", "c1" if j == 2 else "c%d" % j], [n], 128, 0.5)
+    ts(dg, T.cf[:, 272:336], col(2), None, AL.is_equal, None, ["ml", "c1"], ["dg"])
+    CMg, CMj, CMa, NP = T.cm[:, 0:64], T.cm[:, 64:128], T.cm[:, 128:192], T.cm[:, 192:256]
+    CMe, CD, JC = T.ch[:, 256:320], T.ch[:, 320:384], T.ch[:, 384:416]
+    lin(t6, T.cf[:, 0:64], 16.0, LOW + 16.0, ["mi"], ["t6"])
+    tt(t6, t6, dg, AL.mult, ["t6", "dg"], ["t6"])
+    lin(CMg, t6, 1.0, -LOW, ["t6"], ["CMg"])
+    lin(CMj, t6, 1.0, -LOW - 1040.0, ["t6"], ["CMj"])
+    lin(CMa, dg, 65.0, -64.0, ["dg"], ["CMa"])
+    lin(CMe, dg, LOW + 963.5, -LOW, ["dg"], ["CMe"])
+    lin(NP, dg, 0.0, col(10), ["dg", "c10"], ["NP"])
+    lin(CD, dg, 0.0, col(11), ["dg", "c11"], ["CD"])
+    ts(T.rs[:, 0:64], T.cf[:, 272:336], 0.0, -1.0e6, AL.is_equal, AL.mult, ["ml"], ["rs"])
+    lin(T.rs[:, 64:128], T.cf[:, 272:336], 1.0e6, L, ["ml"], ["rs2"])
+    lin(T.ch[:, 384:392], T.cf[:, 0:8], 16.0, col(2), ["mi", "c1"], ["icb"], 8)
+    lin(T.ch[:, 392:408], T.cf[:, 0:16], 0.0, HB - L, ["mi"], ["jc"], 16)
+    lin(T.ch[:, 408:416], T.cf[:, 0:8], 0.0, HB - 5 * L + 1 + B1, ["mi"], ["jr"], 8)
+    lin(T.cf[:, 1472:1488], m16, L, 0.0, ["m16"], ["mL"], 16)
     RK1 = []
     for r in range(16):
-        act(T.rk[:, 64 * r:64 * r + 64], c64, AF.Identity, ["c64", "m16"], ["rk%d" % r], scale=T.cf[:, 1168 + r:1169 + r])
+        lin(T.tw[:, B1 + 64 * r:B1 + 64 * r + 64], T.tw[:, 64 * r:64 * r + 64], T.cf[:, 1232 + r:1233 + r], T.cf[:, 1472 + r:1473 + r],
+            ["num", "m16", "mL"], ["rk%d" % r])
         RK1.append("rk%d" % r)
-    act(T.rk[:, 5120:RKN], T.rk[:, 0:RKN - 5120], AF.Copy, ["rk0"], ["rkt"], 8)
-
-    def repeat():
-        for j in range(1, 5):
-            Q.dma_start(T.rk[:, 1024 * j:1024 * j + 1024], T.rk[:, 0:1024]).then_inc(T.sem.tb, 16)
-    add("s", 240.0, repeat, RK1 + ["sts0", "sts1", "ivs"], ["rkw"], own=("tb", 64), lat=4000.0)
-    RK5 = RK1 + ["rkt", "rkw"]
-    fill(T.snd[:, 3:2560:4], 0.0, ["snd%d_%dq" % (s, h) for s in range(5) for h in range(2)], 1280)
-    fill(T.snd[:, 2:512:4], -FAR, ["snd0_0p1", "snd0_1p1"], 256)
+    RK5 = list(RK1)
+    for j, (a, n) in enumerate(((1024, 1024), (2048, 1024), (3072, 1024), (4096, 1024), (5120, 8))):
+        add("g", 170.0 + 1.66 * n, lambda a=a, n=n: g.affine_select(T.tw[:, B1 + a:B1 + a + n], T.tw[:, B1:B1 + n], [[0, n]], AL.is_gt, 0.0, 1, 0),
+            RK1, ["rkw%d" % j])
+        RK5.append("rkw%d" % j)
+    act(T.snd[:, 0:128, 0], C("I"), AF.Copy, ["I"], ["snd0_0a", "snd0_1a"], 128, scale=0.0)
     for h in range(2):
-        fill(T["yy%d" % h][:, 0:16], -FAR, ["ym%d" % h])
+        fill(T["yy%d" % h][:, 0:16], -SH, ["ym%d" % h])
     cp(T.lw[:], T.ivs[:], ["ivs"], ["lw"], 1024)
 
     ts(T.ci[:, 8:16], T.e0s[:], 896, None, AL.bitwise_and, None, ["e0s"], ["i8"])
-    tt(T.ci[:, 16:24], T.ci[:, 8:16], ICB, AL.add, ["i8", "icb"], ["i16"], 8)
+    tt(T.ci[:, 16:24], T.ci[:, 8:16], T.ch[:, 384:392], AL.add, ["i8", "icb"], ["i16"], 8)
     ts(T.ci[:, 24:32], T.e0s[:], 5.0, 1.0, AL.mult, AL.add, ["e0s"], ["i24"])
     ts(T.ci[:, 32:40], T.ci[:, 24:32], 1023, None, AL.bitwise_and, None, ["i24"], ["i32"])
+    cp(T.offw[:, 0:8], T.ci[:, 16:24], ["i16"], ["offd"])
+    for j in (8, 16):
+        cp(T.offw[:, j:j + 8], T.e0s[:], ["e0s"], ["offa" if j == 8 else "offc"])
     for h in range(2):
         b0, off = BLK0[h], T["off%d" % h]
-        cp(off[:, 0:4], T.ci[:, 16 + b0:20 + b0], ["i16"], ["offd%d" % h])
         cp(off[:, 4:8], T.e0s[:, b0:b0 + 4], ["e0s"], ["offe%d" % h])
-        cp(off[:, 8:12], T.ci[:, 32 + b0:36 + b0], ["i32"], ["offr%d" % h])
-        ts(off[:, 12:16], T.e0s[:, b0:b0 + 4], 1.0, None, AL.add, None, ["e0s"], ["offa%d" % h])
+        ts(off[:, 0:4], T.e0s[:, b0:b0 + 4], float(B1), None, AL.add, None, ["e0s"], ["offk%d" % h])
+    ts(T.offw[:, 24:32], T.ci[:, 32:40], float(B1), None, AL.add, None, ["i32"], ["offr"])
 
     peers = [T.cores[(rank + b) % len(T.cores)] for b in range(8)]
     eng = [e for e in topo.engines(core, peers[1]) if all(e in topo.engines(core, d) for d in peers[1:])]
@@ -225,262 +255,246 @@ def build(g, T, topo, core, rank):
     def head(s, h):
         tag[0] = 2 * s + h
         H = str(h)
-        b0 = BLK0[h]
-        off, ps, bk = T["off" + H], T["ps" + H], "ps" + H
-        wf = T["wf" + H]
+        off = T["off" + H]
         if s > 0:
-            base = 512 * (s - 1) + 64 * b0
-            lo, hi, a1 = [T.land[:, base + 16 * q + 3:base + 256:64] for q in range(3)]
-            LD = ["land%d_%d" % (s - 1, h), "I", "I5", "icb"]
-            mm(group(ps[:, 4:8], [("I", hi), ("I", lo)], 4) + group(ps[:, 0:4], [("I", hi), ("I", T.cm[:, 448 + b0:452 + b0])], 4), LD, ["r0" + H], bk)
-            cp(off[:, 0:8], ps[:, 0:8], ["r0" + H], ["offe" + H, "offd" + H], 8, bank=[bk])
-            mm(group(ps[:, 8:12], [("I5", hi), ("I5", lo), ("I", a1)], 4) + group(ps[:, 12:16], [("I", hi), ("I", lo), ("I", a1)], 4),
-               LD, ["r0" + H], bk)
-            cp(off[:, 8:16], ps[:, 8:16], ["r0" + H], ["offa" + H, "offr" + H], 8, bank=[bk])
-        cp(T["cc" + H][:], T.lw[:].indirect(off[:, 4:8]), ["lw", "offe" + H], ["cc" + H], 64, 2.0)
-        act(wf[:, 0:64], T.lw[:].indirect(off[:, 4:8]), AF.Copy, ["lw", "offe" + H], ["c37" + H], scale=37.0, c=1.5)
-        act(wf[:, 64:128], T.lw[:].indirect(off[:, 0:4]), AF.Copy, ["lw", "offd" + H], ["old" + H], c=1.5)
+            l0 = 128 * (s - 1) + 16 * BLK0[h]
+            LD = ["land%d_%d" % (s - 1, h)]
+            e16, a16 = T.land[:, l0 + 15:l0 + 64:16, 3], T.land[:, l0 + 15:l0 + 64:16, 4]
+            ts(off[:, 4:8], e16, -L, None, AL.add, None, LD, ["offe" + H], 4)
+        src, sn = (T.lw, "lw") if s else (T.ivs, "ivs")
+        cp(T["cc" + H][:], src[:].indirect(off[:, 4:8]), [sn, "offe" + H], ["cc" + H], 64, 2.0)
+
+    def before_write(s):
+        tag[0] = 2 * s + 1
+        if s > 0:
+            l0 = 128 * (s - 1)
+            LD = ["land%d_0" % (s - 1), "land%d_1" % (s - 1)]
+            e16, a16 = T.land[:, l0 + 15:l0 + 128:16, 3], T.land[:, l0 + 15:l0 + 128:16, 4]
+            act(T.hb[:], e16, AF.Identity, LD, ["hb"], 8, bias=HB - L - 63.75)
+            ps = T.ps1
+            mm([(ps[:, 456:488], "I", JC, True, False, 32), (ps[:, 456:464], "I", T.hb[:], False, False, 8), (ps[:, 464:472], "I", e16, False, False, 8),
+                (ps[:, 464:472], "I", a16, False, False, 8), (ps[:, 472:480], "I", e16, False, False, 8),
+                (ps[:, 480:488], "I5", e16, False, False, 8), (ps[:, 480:488], "I", a16, False, True, 8)], LD + ["hb", "icb", "jc", "jr"], ["rw"], "ps1")
+            ts(T.offw[:], ps[:, 456:488], -HB, None, AL.add, None, ["rw"], ["offd", "offa", "offc", "offr"], 32, bank=["ps1"])
+        tw, twr = (T.tw[:], RK5) if s else (T.tw[:, 0:B1 + 1024], RK1)
+        act(T.ee[:], tw.indirect(T.offw[:, 16:32]), AF.Copy, twr + ["num", "offc", "offr"], ["ee"], 256, c=1.5)
+        c37, old, dv = T.jf[:, 0:128], T.jf[:, 128:256], T.jf[:, 256:384]
+        act(c37, T.lw[:].indirect(T.offw[:, 16:24]), AF.Copy, ["lw", "offc"], ["c37"], 128, scale=37.0, c=1.5)
+        act(old, T.lw[:].indirect(T.offw[:, 0:8]), AF.Copy, ["lw", "offd"], ["old"], 128, c=1.5)
+        tt(T.ji[:, 0:128], T.tw[:, 0:B1].indirect(T.offw[:, 8:16]), c37, AL.add, ["num", "c37", "offa"], ["vi"], 128, c=1.8)
+        ts(T.ji[:, 128:256], T.ji[:, 0:128], 4095, None, AL.bitwise_and, None, ["vi"], ["nv"], 128)
+        tt(dv, T.ji[:, 128:256], old, AL.subtract, ["nv", "old"], ["dv"], 128)
+
+    def write(s):
+        tag[0] = 2 * s + 1
+        tt(T.jf[:, 384:512], T.ohj[:], T.jf[:, 256:384], AL.mult, ["ohj0", "ohj1", "dv"], ["t"], 128)
+        add("v", vc(128, 4.0), lambda: V.tensor_tensor(T.lw[:].indirect(T.offw[:, 0:8]), T.jf[:, 384:512], T.jf[:, 128:256], AL.add),
+            ["t", "old", "offd"], ["lw"])
 
     def body(s, h):
         tag[0] = 2 * s + h
         H = str(h)
         b0 = BLK0[h]
-        off, ps, bk = T["off" + H], T["ps" + H], "ps" + H
-        yy, dd, bad, em, cc = T["yy" + H], T["dd" + H], T["bad" + H], T["em" + H], T["cc" + H]
-        wbuf, wf, wi, offz = T["wb" + H], T["wf" + H], T["wi" + H], T["offz" + H]
-        last, p0on, p1on = s == STEPS - 1, s >= 1, s >= 2
-        sb = 512 * s + 64 * b0
+        off, offz, ps, bk = T["off" + H], T["offz" + H], T["ps" + H], "ps" + H
+        yy, dd, gd, em, cc = T["yy" + H], T["dd" + H], T["gd" + H], T["em" + H], T["cc" + H]
+        wb, wh, wf = T["wb" + H], T["wh" + H], T["wf" + H]
+        X0, X1, XT = "px0" + H, "px1" + H, "pt" + H
+        x0, x1, xt = T[X0], T[X1], T[XT]
+        last, one, two = s == STEPS - 1, s >= 1, s >= 2
+        sl = 128 * s + 16 * b0
         SN = "snd%d_%d" % (s, h)
+        OHJ = T.ohj[:, 16 * b0:16 * b0 + 64]
 
-        def B(n, w=1):
+        def B(n):
             j = WB.index(n)
-            return wbuf[:, 64 * j:64 * (j + w)]
+            return wb[:, 64 * j:64 * j + 64]
 
-        def F(n, w=1):
-            j = WF[n]
-            return wf[:, 64 * j:64 * (j + w)]
+        def W(n, w=1):
+            return wh[:, 64 * WH[n]:64 * (WH[n] + w)]
+
+        def F(n):
+            return wf[:, 64 * WF[n]:64 * WF[n] + 64]
 
         def R(j, w=1):
             return ps[:, 64 * j:64 * (j + w)]
 
+        def out(q):
+            return T.snd[:, sl:sl + 64, q]
+
         def n_(*a):
             return [x + H for x in a]
 
-        rkw, rkr = (T.rk[:], RK5) if s else (T.rk[:, 0:1024], RK1)
-        act(B("rke", 2), rkw.indirect(off[:, 4:12]), AF.Copy, rkr + n_("offe", "offr"), n_("rke"), 128, c=1.5)
+        ER, E1 = T.ee[:, 16 * b0:16 * b0 + 64], T.ee[:, 128 + 16 * b0:192 + 16 * b0]
         if s > 0:
-            base = 512 * (s - 1) + 64 * b0
+            l0 = 128 * (s - 1) + 16 * b0
             LD = ["land%d_%d" % (s - 1, h)]
-            K1, P0, P1 = [T.land[:, base + j:base + 256:4] for j in range(3)]
-            AO = T.land[:, base + 35:base + 256:64]
+            PA, PB_, KN, AO = [T.land[:, l0:l0 + 64, j] for j in (0, 1, 2, 4)]
+            PAB = T.land[:, l0:l0 + 64, 0:2]
         else:
-            LD, K1 = n_("rke"), B("rke")
-        vg = VG[s][h]
-        cuts = ([0] if vg else []) + [vg + (64 - vg) * j // GS // 2 * 2 for j in range(GS)] + [64]
+            LD, KN = n_("k0"), W("k0")
+            act(KN, T.tw[:, 0:B1 + 1024].indirect(off[:, 0:4]), AF.Relu, RK1 + n_("offk") + ["c9", "num"], LD, bias=col(9), scale=4.0, c=1.5)
+        vg = VG[s]
         YR = []
-        for j in range(len(cuts) - 1):
-            a, b = cuts[j], cuts[j + 1]
-            src = T.sts[:].indirect(cc[:, a:b])
-            if vg and j == 0:
-                cp(yy[:, 16 + 16 * a:16 + 16 * b], src, ["sts0", "sts1"] + n_("cc"), n_("y%d_" % j), 16 * (b - a), 1.5)
-            else:
-                act(yy[:, 16 + 16 * a:16 + 16 * b], src, AF.Copy, ["sts0", "sts1"] + n_("cc"), n_("y%d_" % j), 16 * (b - a), c=1.5)
-            YR += n_("y%d_" % j)
-        for j in range(len(cuts) - 1, GS + 1):
-            YR += n_("y%d_" % j)
-        tt(wi[:, 0:64], T.num[:].indirect(off[:, 12:16]), F("c37"), AL.add, ["num"] + n_("c37", "offa"), n_("vi"), c=1.8)
-        ts(wi[:, 64:128], wi[:, 0:64], 4095, None, AL.bitwise_and, None, n_("vi"), n_("nv"))
-        tt(F("dv"), wi[:, 64:128], F("old"), AL.subtract, n_("nv", "old"), n_("dv"))
-        act(B("nc"), K1, AF.Relu, LD, n_("nc"), bias=1.0, scale=-1.0)
-        ts(B("thr"), K1, 0.5, 4.5 / 512, AL.is_lt, AL.max, LD, n_("thr"))
-        mm([(T.pth[:, 64 * j:64 * j + 64], C("I512"), B("thr"), True, True, 64) for j in range(4)], n_("thr") + ["I512"], ["pth"], "pth")
-        if not p0on:
-            act(B("mid"), K1, AF.Identity, LD, n_("mid"), bias=-126.0)
-        else:
-            tt(B("q0"), B("nc"), P0, AL.mult, LD + n_("nc"), n_("q0"))
-            act(B("qm0"), P0, AF.Relu, LD, n_("qm0"), scale=-1.0)
-            if p1on:
-                tt(B("q1"), B("nc"), P1, AL.mult, LD + n_("nc"), n_("q1"))
-                act(B("qm1"), P1, AF.Relu, LD, n_("qm1"), scale=-1.0)
-                tt(B("pm"), P0, P1, AL.min, LD, n_("pm"))
-                grp(R(1), [("I", K1), ("I", B("nc")), ("hI", B("q0")), ("hI", B("q1"))], LD + n_("nc", "q0", "q1"), n_("r1"), bk)
-                grp(R(2), [("I", B("q0")), ("nI", B("q1"))], n_("q0", "q1"), n_("r2"), bk)
-                act(B("half"), R(2), AF.Abs, n_("r2"), n_("half"), scale=0.5 * EPS1, bank=[bk])
-            else:
-                grp(R(1), [("I", K1), ("I", B("nc")), ("I", B("q0"))], LD + n_("nc", "q0"), n_("r1"), bk)
-            act(B("mid"), R(1), AF.Identity, n_("r1"), n_("mid"), bias=-126.0, bank=[bk])
-        XB = ["px%d%d" % (h, u) for u in range(2)]
-        EM = []
-        for u in range(2):
-            xb = XB[u]
-            px = T[xb]
-            for v in range(ZS):
-                lst = []
-                for kk in range(8 // ZS * v, 8 // ZS * (v + 1)):
-                    lst += group(px[:, 64 * kk:64 * kk + 64], [("nI", B("mid")), ("I", yy[:, 16 + 8 * u + kk:1040:16])])
-                mm(lst, YR + n_("mid") + ["I", "nI"], [xb], xb)
-            sl = slice(512 * u, 512 * u + 512)
-            DD, EU = [], []
-            for v in range(DS):
-                w = 512 // DS
-                act(dd[:, 512 * u + w * v:512 * u + w * v + w], px[:, w * v:w * v + w], AF.Abs, [xb], n_("d%d%d" % (u, v)), w,
-                    bias=-125.0 * EPS1, scale=EPS1, bank=[xb])
-                DD += n_("d%d%d" % (u, v))
-            for v in range(2):
-                sv = slice(512 * u + 256 * v, 512 * u + 256 * v + 256)
-                tt(bad[:, sv], dd[:, sv], T.pth[:, 0:256], AL.is_gt, (DD if DS == 1 else DD[v:v + 1]) + ["pth"], n_("bad%d%d" % (u, v)), 256, bank=["pth"])
-            BD = n_("bad%d0" % u, "bad%d1" % u)
-            if p0on:
-                mm([(px[:], C("sI"), dd[:, sl], True, False, 512)], DD + ["sI"], [xb], xb)
-                if p1on:
-                    mm([(px[:, 64 * kk:64 * kk + 64], C("nsI"), B("half"), False, False, 64) for kk in range(8)], n_("half") + ["nsI", xb], [xb], xb)
-                mm([(px[:], C("bigone"), bad[:, sl], False, True, 512)], BD + ["bigone", xb], [xb], xb)
-                for v in range(ES):
-                    w = 512 // ES
-                    ts(em[:, 512 * u + w * v:512 * u + w * v + w], px[:, w * v:w * v + w], M8, M8, AL.add, AL.is_equal, [xb],
-                       n_("em%d%d" % (u, v)), w, bank=[xb])
-                    EU += n_("em%d%d" % (u, v))
-            EM.append(EU)
-            src, sn = (em, EU) if p0on else (bad, BD)
-            lst = [(T.pr[:, 0:64], T.uu[:, 15 - k:143 - k], src[:, 64 * k:64 * k + 64], False, k == 15, 64) for k in range(8 * u, 8 * u + 8)]
-            if u == 0:
-                if p0on:
-                    lst = [(T.pr[:, 0:64], C("one"), B("nc"), True, False, 64)] + lst
+        for e, a, b in (("v", 0, vg), ("a", vg, 64)):
+            if b > a:
+                src = T.sts[:].indirect(cc[:, a:b])
+                if e == "v":
+                    cp(yy[:, 16 + 16 * a:16 + 16 * b], src, ["sts0", "sts1"] + n_("cc"), n_("yv"), 16 * (b - a), 1.5)
                 else:
-                    lst[0] = lst[0][:3] + (True, False, 64)
-            mm(lst, sn + n_("nc") + ["uu", "one"] + (["pr"] if u else []), ["pr"], "pr")
-        PC, PB = T[XB[0]][:, 0:64], T[XB[1]][:, 0:64]
-        if p0on:
-            mm([(PC, C("I64"), B("nc"), True, False, 64)] + [(PC, C("I"), em[:, 64 * k:64 * k + 64], False, False, 64) for k in range(8)],
-               EM[0] + n_("nc") + ["I", "I64"], [XB[0]], XB[0])
-            mm([(PC, C("I"), em[:, 64 * k:64 * k + 64], False, k == 15, 64) for k in range(8, 16)], EM[1] + ["I", XB[0]], [XB[0]], XB[0])
-            for u in range(2):
-                mm([(PB, T.bw[:, 128 * k:128 * k + 128], em[:, 64 * k:64 * k + 64], k == 0, k == 15, 64) for k in range(8 * u, 8 * u + 8)],
-                   EM[u] + ["bw%d" % k for k in range(16)] + [XB[1]] * u, [XB[1]], XB[1])
-        ts(B("ok"), T.pr[:, 0:64], 16.0 if p0on else 0.0, None, AL.is_equal, None, ["pr"], n_("ok"), bank=["pr"])
-        grp(R(0), [("T4", B("ok"))], n_("ok"), n_("r0"), bk)
-        ts(B("ohj"), R(0), M1, M1 + 1.0, AL.add, AL.is_equal, n_("r0"), n_("ohj"), bank=[bk])
-        tt(F("t"), B("ohj"), F("dv"), AL.mult, n_("ohj", "dv"), n_("t"))
-        add("v", vc(64, 4.0), lambda: V.tensor_tensor(T.lw[:].indirect(off[:, 0:4]), F("t"), F("old"), AL.add),
-            n_("t", "old", "offd"), ["lw"])
-        grp(R(0), [("I", CMj), ("Kw", B("ohj")), ("one2k", B("ohj"))], n_("ohj") + ["CMj"], n_("r0"), bk)
-        scan(F("sj"), T.rs[:, 0:64], R(0), AL.add, AL.max, n_("r0") + ["rs"], n_("sj"), 64, bank=[bk])
+                    act(yy[:, 16 + 16 * a:16 + 16 * b], src, AF.Copy, ["sts0", "sts1"] + n_("cc"), n_("ya"), 16 * (b - a), c=1.5)
+        YR = n_("yv", "ya")
+        if one:
+            if OPT["ci"] == "v":
+                ts(B("ci"), KN, 0.5, None, AL.is_gt, None, LD, n_("ci"))
+            else:
+                act(B("ci"), KN, AF.Sign, LD, n_("ci"))
+        if two:
+            tt(W("pm"), PA, PB_, AL.min, LD, n_("pm"))
+            tt(W("ra"), W("pm"), KN, AL.max, LD + n_("pm"), n_("ra"))
+            mm(group(R(0), [("hI", PA), ("hI", PB_)]), LD, n_("r0"), bk)
+            tt(W("mid"), KN, R(0), AL.max, LD + n_("r0"), n_("mid"), bank=[bk])
+            mm(group(R(1), [("I", W("ra")), ("BC", B("ci")), ("nI", W("mid"))]), n_("ra", "mid", "ci"), n_("r1"), bk)
+            act(W("hf"), R(1), AF.Identity, n_("r1"), n_("hf"), bias=-MIDO, bank=[bk])
+            MID, MR, hfl, hfr, HR, ab, eb = W("mid"), n_("mid"), "I", W("hf"), n_("hf"), SH, MIDO
+        elif one:
+            tt(W("mid"), PB_, KN, AL.max, LD, n_("mid"))
+            MID, MR, hfl, hfr, HR, ab, eb = W("mid"), n_("mid"), "nCI", B("ci"), n_("ci"), SH, BIG
+        else:
+            MID, MR = KN, LD
+        PR, PC, PB = xt[:, 0:64], x0[:, 0:64], x1[:, 0:64]
+        for u in range(2):
+            xb = (X0, X1)[u]
+            px = T[xb]
+            lst = []
+            for kk in range(8):
+                lst += group(px[:, 64 * kk:64 * kk + 64], [("nI", MID), ("I", yy[:, 16 + 8 * u + kk:1040:16])])
+            mm(lst, YR + MR, [xb], xb)
+            sv = slice(512 * u, 512 * u + 512)
+            EU = n_("em%d" % u)
+            if one:
+                act(dd[:, sv], px[:], AF.Abs, [xb], n_("d%d" % u), 512, bias=ab, bank=[xb])
+                ts(gd[:, sv], dd[:, sv], M8 - CC, M8, AL.add, AL.is_equal, n_("d%d" % u), n_("g%d" % u), 512, 0.5)
+                mm([(px[:], "I", dd[:, sv], True, False, 512)] + [(px[:, 64 * kk:64 * kk + 64], hfl, hfr, False, False, 64) for kk in range(8)],
+                   n_("d%d" % u) + HR, [xb], xb)
+                mm([(px[:], "nB", gd[:, sv], False, True, 512)], n_("g%d" % u) + [xb], [xb], xb)
+                ts(em[:, sv], px[:], M8 + eb, M8, AL.add, AL.is_equal, [xb], EU, 512, bank=[xb])
+            else:
+                ts(em[:, sv], px[:], M8 + C0, M8, AL.add, AL.is_equal, [xb], EU, 512, bank=[xb])
+        for u in range(2):
+            EU = n_("em%d" % u)
+            ks = range(8 * u, 8 * u + 8)
+            if one:
+                first = [("nqI", KN)] if u == 0 else []
+                mm(group(PC, first + [("I", em[:, 64 * k:64 * k + 64]) for k in ks], 64, u == 0, u == 1), EU + LD + [X0] * u, [X0], X0)
+            first = [("nP2", B("ci"))] if one and u == 0 else []
+            mm(group(PR, first + [("uu%d" % k, em[:, 64 * k:64 * k + 64]) for k in ks], 64, u == 0, u == 1),
+               EU + (n_("ci") if one else []) + [XT] * u, [XT], XT)
+        if one and not OPT["rmode"]:
+            mm(group(PB, [("bw%d" % k, em[:, 64 * k:64 * k + 64]) for k in range(16)]), n_("em0", "em1"), [X1], X1)
+        ts(B("ok"), PR, 0.0 if one else 0.5, None, AL.is_equal if one else AL.is_gt, None, [XT], n_("ok"), bank=[XT])
+        if one and OPT["rmode"]:
+            act(F("prs"), PR, AF.Relu, [XT], n_("prs"), bias=0.25, bank=[XT])
+        mm(group(R(2), [("T4", B("ok"))]), n_("ok"), n_("r2"), bk)
+        ts(OHJ, R(2), M1, M1 + 1.0, AL.add, AL.is_equal, n_("r2"), n_("ohj"), bank=[bk])
+        mm(group(R(2), [("I", CMj), ("Kw2", OHJ)]), n_("ohj") + ["CMj"], n_("r2"), bk)
+        scan(F("sj"), T.rs[:, 0:64], R(2), AL.add, AL.max, n_("r2") + ["rs"], n_("sj"), 64, bank=[bk])
         cp(offz[:, 0:4], wf[:, 64 * WF["sj"] + 15:64 * WF["sj"] + 64:16], n_("sj"), n_("offj"), 4)
-        act(B("zj") if p0on else T.snd[:, sb + 1:sb + 256:4], yy[:].indirect(offz[:, 0:4]), AF.Copy, YR + n_("offj", "ym"),
-            n_("zj") if p0on else [SN + "p0"], c=1.5)
-        OH, OHN = (B("oh"), "oh") if p0on else (B("ohj"), "ohj")
-        FU, fu = (n_("full"), [("nI", B("full"))]) if p1on else ([], [])
-        if p1on:
-            grp(R(2), [("one", B("ohj")), ("nI", B("qm1"))], n_("ohj", "qm1"), n_("r2"), bk)
-            act(B("full"), R(2), AF.Relu, n_("r2"), n_("full"), bank=[bk])
-            pc = T.pth[:, 256 + 128 * h:384 + 128 * h]
-            pc0, pc1 = T.pth[:, 256 + 128 * h:320 + 128 * h], T.pth[:, 320 + 128 * h:384 + 128 * h]
-            mm(group(pc0, [("I", P0)]) + group(pc1, [("I", P1), ("I", SIX), ("I", B("zj"))]), LD + n_("zj") + ["I", "SIX"], n_("pc"), "pth")
-            tt(B("f"), B("pm"), B("zj"), AL.min, n_("pm", "zj"), n_("f"))
-        terms, trd = [("I", B("dr"))], n_("kr")
-        if p0on:
-            act(B("vp"), PC, AF.Exp, [XB[0]], n_("vp"), bias=-64.0 * math.log(32.0), scale=math.log(32.0), bank=[XB[0]])
-            grp(R(3), [("hugeone", B("ok")), ("Mw", B("vp"))], n_("vp", "ok"), n_("r3"), bk)
-            ts(B("win"), R(3), 2.0, None, AL.is_gt, None, n_("r3"), n_("win"), bank=[bk])
-            tt(B("wbb"), B("win"), PB, AL.mult, n_("win") + [XB[1]], n_("wbb"), bank=[XB[1]])
-            grp(R(3), [("T4", B("ok")), ("S4", B("wbb"))], n_("ok", "wbb"), n_("r3"), bk)
-            ts(B("oh"), R(3), M1, M1 + 1.0, AL.add, AL.is_equal, n_("r3"), n_("oh"), bank=[bk])
-            grp(R(6), [("I", CMg), ("Kw", B("oh"))], n_("oh") + ["CMg"], n_("r6"), bk)
+        act(W("zj") if one else out(1), yy[:].indirect(offz[:, 0:4]), AF.Identity, YR + n_("offj", "ym"), n_("zj") if one else [SN + "b"],
+            bias=SH, c=1.5)
+        if two:
+            mm(group(R(3), [("nLI", W("pm")), ("L2one", OHJ)]) + group(R(4), [("I", PB_), ("Lone", OHJ)]), LD + n_("pm", "ohj"), n_("r3", "r4"), bk)
+            act(W("ljn", 2), R(3, 2), AF.Relu, n_("r3", "r4"), n_("ljn"), 128, bias=-L, bank=[bk])
+            JN, JR, JB, JBR = ("I", W("ljn")), n_("ljn"), W("jb"), n_("ljn")
+            tt(W("f"), W("pm"), W("zj"), AL.min, n_("pm", "zj"), n_("f"))
+            mm(group(R(5), [("I", NP), ("nhone", OHJ), ("eI", W("ljn")), ("one", W("f"))]), n_("ohj", "ljn", "f") + ["NP"], n_("r5"), bk)
+            ts(F("r"), R(5), M16, M16, AL.add, AL.subtract, n_("r5"), n_("r"), bank=[bk])
+            tt(B("oq"), F("r"), R(5), AL.is_equal, n_("r", "r5"), n_("oq"), bank=[bk])
+            tt(W("fq"), B("oq"), W("f"), AL.mult, n_("oq", "f"), n_("fq"))
+        else:
+            JN, JR = ("Lone", OHJ), n_("ohj")
+            if one:
+                mm(group(R(4), [("I", PB_), ("Lone", OHJ)]), LD + n_("ohj"), n_("r4"), bk)
+                act(out(0), R(4), AF.Relu, n_("r4"), [SN + "a"], bias=-L, bank=[bk])
+                JB, JBR = out(0), [SN + "a"]
+        OH, OHR = (B("oh"), n_("oh")) if one else (OHJ, n_("ohj"))
+        if one:
+            act(B("vp"), PC, AF.Exp, [X0], n_("vp"), scale=math.log(32.0), bank=[X0])
+            mm(group(R(6), [("hugeone", B("ok")), ("Mw", B("vp"))]), n_("vp", "ok"), n_("r6"), bk)
+            ts(B("win"), R(6), 2.0, None, AL.is_gt, None, n_("r6"), n_("win"), bank=[bk])
+            if OPT["rmode"]:
+                mm(group(R(6), [("Q2", B("win"))]), n_("win"), n_("r6"), bk)
+                tt(F("y"), F("prs"), R(6), AL.mult, n_("prs", "r6"), n_("y"), bank=[bk])
+                ts(F("ry"), F("y"), M1, M1, AL.add, AL.subtract, n_("y"), n_("ry"))
+                tt(B("bit"), F("ry"), F("y"), AL.is_gt, n_("ry", "y"), n_("bit"))
+                mm(group(R(6), [("T4", B("ok")), ("T4", B("bit"))]), n_("ok", "bit"), n_("r6"), bk)
+            else:
+                tt(B("bit"), B("win"), PB, AL.mult, n_("win") + [X1], n_("bit"), bank=[X1])
+                mm(group(R(6), [("T4", B("ok")), ("S4", B("bit"))]), n_("ok", "bit"), n_("r6"), bk)
+            ts(B("oh"), R(6), M1, M1 + 1.0, AL.add, AL.is_equal, n_("r6"), n_("oh"), bank=[bk])
+            mm(group(R(6), [("I", CMg), ("Kw", B("oh"))]), n_("oh") + ["CMg"], n_("r6"), bk)
             scan(F("sg"), T.rs[:, 0:64], R(6), AL.add, AL.max, n_("r6") + ["rs"], n_("sg"), 64, bank=[bk])
             cp(offz[:, 4:8], wf[:, 64 * WF["sg"] + 15:64 * WF["sg"] + 64:16], n_("sg"), n_("offg"), 4)
-            act(B("z0"), yy[:].indirect(offz[:, 4:8]), AF.Copy, YR + n_("offg", "ym"), n_("z0"), c=1.5)
-            tt(B("wz"), B("win"), B("z0"), AL.mult, n_("win", "z0"), n_("wz"))
-            act(B("xg"), B("wz"), AF.Identity, n_("wz"), n_("xg"), bias=770.5)
-        if p1on:
-            grp(R(1), [("I", NP), ("nhI", B("full")), ("one", B("f"))], n_("full", "f") + ["NP"], n_("r1"), bk)
-            ts(F("r"), R(1), M16, M16, AL.add, AL.subtract, n_("r1"), n_("r"), bank=[bk])
-            tt(B("oq"), F("r"), R(1), AL.is_equal, n_("r", "r1"), n_("oq"), bank=[bk])
-            tt(B("fq"), B("oq"), B("f"), AL.mult, n_("oq", "f"), n_("fq"))
-            terms = [("I", B("oq")), ("I", B("fq"))] + terms
-            trd += n_("oq", "fq")
-        mm(group(R(4), [("one", B("ohj"))] + fu) + group(R(5), [("I", ONE), ("none", OH)]), n_("ohj", OHN) + FU + ["I", "ONE", "none", "one", "nI"],
-           n_("r4", "r5"), bk)
-        tt(B("kr", 2), B("rke", 2), R(4, 2), AL.mult, n_("rke", "r4", "r5"), n_("kr"), 128, bank=[bk])
-        if p0on:
-            t0 = [("nI64", B("qm0")), ("one64", B("oh")), ("sone", B("wp0"))] + ([("nI64", B("full"))] if p1on else []) + [("nsone", B("wz"))]
-            CD = ["nI64", "one64", "one384", "sone", "nsone"]
-            if p1on:
-                tt(B("wp0"), B("win"), pc0, AL.mult, n_("win", "pc"), n_("wp0"), bank=["pth"])
-                tt(B("wp1"), B("win"), pc1, AL.mult, n_("win", "pc"), n_("wp1"), bank=["pth"])
-                x0, X0 = T[XB[0]], XB[0]
-                mm([(x0[:, 0:128], C("nI64"), B("qm0", 2), True, False, 128), (x0[:, 0:64], C("one64"), B("oh"), False, False, 64),
-                    (x0[:, 64:128], C("one64"), B("oh"), False, False, 64), (x0[:, 0:64], C("nI64"), B("full"), False, False, 64),
-                    (x0[:, 64:128], C("one384"), B("ohj"), False, False, 64), (x0[:, 0:128], C("sone"), B("wp0", 2), False, False, 128)],
-                   n_("qm0", "oh", "wp0", "ohj", "qm1", "wp1") + FU + CD, [X0], X0)
-                mm([(x0[:, 0:64], C("nsone"), B("wz"), False, False, 64), (x0[:, 64:128], C("nsone"), B("wz"), False, True, 64)],
-                   n_("wz") + CD + [X0], [X0], X0)
-                ts(B("s0", 2), x0[:, 0:128], M8, M8 + 64.0, AL.add, AL.is_equal, [X0], n_("s"), 128, bank=[X0])
-                tt(B("u0", 2), B("s0", 2), pc, AL.mult, n_("s", "pc"), n_("u"), 128, bank=["pth"])
-                grp(R(4), [("nI", SIX), ("I6", B("s1")), ("I", B("u1"))], n_("s", "u") + ["SIX"], n_("r4"), bk)
-                tt(B("w"), B("s0"), R(4), AL.mult, n_("s", "r4"), n_("w"), bank=[bk])
-                N1, N0, NB, b0_ = x0[:, 0:64], x0[:, 64:128], X0, -FAR
-                mm([(x0[:, 0:128], C("I6"), B("s0", 2), True, False, 128), (N0, C("I"), B("u0"), False, False, 64),
-                    (N0, C("I"), B("u1"), False, False, 64)], n_("s", "u") + ["I", "I6"], [X0], X0)
-                mm([(N0, C("nI"), B("w"), False, False, 64), (N1, C("I"), B("w"), False, True, 64)], n_("w") + ["I", "nI", X0], [X0], X0)
-                NR = [X0]
-            else:
-                tt(B("wp0"), B("win"), P0, AL.mult, LD + n_("win"), n_("wp0"))
-                mm(group(R(6), t0), n_("qm0", "oh", "wp0", "wz") + CD, n_("r6"), bk)
-                ts(B("s0"), R(6), M8, M8 + 64.0, AL.add, AL.is_equal, n_("r6"), n_("s"), bank=[bk])
-                tt(B("u0"), B("s0"), P0, AL.mult, LD + n_("s"), n_("u"))
-                tt(B("w"), B("s0"), B("zj"), AL.mult, n_("s", "zj"), n_("w"))
-                N0, N1, NB, b0_, NR = R(6), R(7), bk, 0.0, n_("r6", "r7")
-                mm(group(R(6), [("I", B("zj")), ("I", B("u0")), ("nI", B("w"))]) + group(R(7), [("I6", B("s0")), ("I", B("w"))]),
-                   n_("s", "u", "w", "zj") + ["I", "nI", "I6"], NR, bk)
-            if last:
-                ts(T.oy0[:, 16 * b0:16 * b0 + 64], N0, b0_, -1.0, AL.add, AL.max, NR, n_("oy0"), bank=[NB])
-                ts(T.oy1[:, 16 * b0:16 * b0 + 64], N1, -FAR, -1.0, AL.add, AL.max, NR, n_("oy1"), bank=[NB])
-            else:
-                act(T.snd[:, sb + 1:sb + 256:4], N0, AF.Identity, NR, [SN + "p0"], bias=b0_, bank=[NB])
-                ts(T.snd[:, sb + 2:sb + 256:4], N1, -FAR, None, AL.add, None, NR, [SN + "p1"], bank=[NB]) if P1V else \
-                    act(T.snd[:, sb + 2:sb + 256:4], N1, AF.Identity, NR, [SN + "p1"], bias=-FAR, bank=[NB])
-        grp(R(2), [("I", B("kr"))] + terms, trd, n_("r2"), bk)
-        act(B("ee"), R(2), AF.Sign, n_("r2"), n_("ee"), bank=[bk])
-        act(B("x4"), R(2), AF.Identity, n_("r2"), n_("x4"), bias=765.5, bank=[bk])
-        if p0on:
-            grp(R(3), [("one", B("oh"))] + fu, n_("oh") + FU, n_("r3"), bk)
-            tt(B("kna"), K1, R(3), AL.mult, LD + n_("r3"), n_("kna"), bank=[bk])
-            grp(R(3), [("I", B("kna"))] + terms + [("I", B("win")), ("I", B("wz"))], n_("kna", "win", "wz") + trd, n_("r3"), bk)
-        KR, KN = (R(3), "r3") if p0on else (R(2), "r2")
-        if last:
-            act(T.oyk[:, 16 * b0:16 * b0 + 64], KR, AF.Identity, n_(KN), n_("oyk"), bias=-1.0, bank=[bk])
+            tt(W("wz"), yy[:].indirect(offz[:, 4:8]), B("win"), AL.mult, YR + n_("offg", "ym", "win"), n_("wz"), c=1.8)
+        keep = [("Lone", OH)] + ([("nLone", OHJ), JN] if two else [])
+        mm(group(xt[:, 0:64], [("I", KN)] + keep) + group(xt[:, 64:128], [("I", CD), ("I4", E1), ("nLone", OH)])
+           + group(xt[:, 128:192], [("I", E1), ("nLone", OH)]) + group(xt[:, 192:256], [("I", ER), JN]),
+           LD + OHR + JR + n_("ohj") + ["CD", "ee"], [XT], XT)
+        act(W("kk", 4), xt[:, 0:256], AF.Relu, [XT], n_("kk"), 256, bias=-L, bank=[XT])
+        if two:
+            d0, d1 = x0[:, 0:128:2], x0[:, 1:128:2]
+            mm([(x0[:, 0:128], "nI", PAB, True, False, 128), (d0, "nLI", B("win"), False, False, 64), (d1, "nLI", B("win"), False, False, 64)],
+               LD + n_("win"), [X0], X0)
+            mm([(d0, "I", W("wz"), False, False, 64), (d1, "I", W("wz"), False, True, 64)], n_("wz") + [X0], [X0], X0)
+            ts(W("s", 2), x0[:, 0:128], M8 + L + SH, M8, AL.add, AL.is_equal, [X0], n_("s"), 128, bank=[X0])
+            n0, n1 = xt[:, 0:128:2], xt[:, 1:128:2]
+            mm([(xt[:, 0:128], "I", PAB, True, False, 128), (n0, "I", JB, False, False, 64), (n1, "nI", JB, False, False, 64),
+                (n1, "I", W("zj"), False, False, 64), (n0, "I", W("ljn"), False, False, 64), (n1, "I", W("ljn"), False, False, 64)],
+               LD + n_("ljn", "zj"), [XT], XT)
+            mm([(xt[:, 0:128], "Lone", W("s", 2), False, True, 128)], n_("s") + [XT], [XT], XT)
+            act(T.snd[:, sl:sl + 64, 0:2], xt[:, 0:128], AF.Relu, [XT], [SN + "a", SN + "b"], 128, bias=-L, bank=[XT])
+        elif one:
+            mm(group(x0[:, 0:64], [("nI", PB_), ("nLI", B("win"))], 64, True, False), LD + n_("win"), [X0], X0)
+            mm(group(x0[:, 0:64], [("I", W("wz"))], 64, False, True), n_("wz") + [X0], [X0], X0)
+            ts(W("s"), x0[:, 0:64], M8 + L + SH, M8, AL.add, AL.is_equal, [X0], n_("s"), bank=[X0])
+            mm(group(xt[:, 0:64], [("I", PB_), ("nI", JB), ("I", W("zj")), JN], 64, True, False), LD + JBR + JR + n_("zj"), [XT], XT)
+            mm(group(xt[:, 0:64], [("Lone", W("s"))], 64, False, True), n_("s") + [XT], [XT], XT)
+            act(out(1), xt[:, 0:64], AF.Relu, [XT], [SN + "b"], bias=-L, bank=[XT])
+        kt, et, rd = [("I", W("kk")), ("I", W("dr"))], [("wI", CMe), ("one", W("de")), ("I", W("se"))], n_("kk")
+        if two:
+            kt += [("CI", B("oq")), ("I", W("fq"))]
+            et += [("W62", B("oq")), ("qone", W("fq"))]
+            rd += n_("oq", "fq")
+        at = [("I", CMa), ("none", OH)] + ([("I", AO)] if one else []) + ([("one", OHJ), ("neI", W("ljn"))] if two else [])
+        mm(group(x1[:, 64:128], at), LD + OHR + JR + n_("ohj") + ["CMa"], [X1], X1)
+        scan(out(4), T.rs[:, 0:64], x1[:, 64:128], AL.add, AL.max, [X1, "rs"], [SN + "n"], 64, bank=[X1])
+        if one:
+            mm(group(x1[:, 0:64], et + [("W64", B("win"))], 64, True, False), rd + n_("win") + ["CMe"], [X1], X1)
+            mm(group(x1[:, 0:64], [("qone", W("wz"))], 64, False, True), n_("wz") + [X1], [X1], X1)
+            kt += [("C0I", B("win")), ("I", W("wz"))]
+            rd += n_("win", "wz")
         else:
-            act(T.snd[:, sb:sb + 256:4], KR, AF.Copy, n_(KN), [SN + "k"], bank=[bk])
-        nq = 2 if last else 3
-        cq = 576 if p0on else 128
-        X1 = XB[1]
-        QA, QL, QH, QN = T[X1][:, 0:64 * nq], T[X1][:, 0:64], T[X1][:, 64 * (nq - 2):64 * (nq - 1)], T[X1][:, 64 * (nq - 1):64 * nq]
-        lst = [(QA, C("I"), T.cm[:, cq:cq + 64 * nq], True, False, 64 * nq), (QN, C("none"), OH, False, False, 64)]
-        if p1on:
-            lst.append((QN, C("I"), B("full"), False, False, 64))
-        if p0on:
-            lst += [(QL, C("Gw"), B("win"), False, False, 64), (QH, C("Hw"), B("win"), False, False, 64)]
-        mm(lst, n_(OHN) + (n_("win") if p0on else []) + FU + CMR + ["I", "none", "Hw", "Gw"], [X1], X1)
-        mm([(QL, C("Lw"), B("ee"), False, False, 64), (QH, C("Hw"), B("ee"), False, False, 64), (QL, C("qone"), B("x4"), False, not p0on, 64)],
-           n_("x4", "ee") + ["qone", "Hw", "Lw", X1], [X1], X1)
-        if p0on:
-            mm([(QL, C("qone"), B("xg"), False, True, 64)], n_("xg") + ["qone", X1], [X1], X1)
-        scan(F("sc", nq), T.rs[:, 0:64 * nq], QA, AL.add, AL.max, [X1, "rs"], n_("sc"), 64 * nq, bank=[X1])
-        c0 = 64 * WF["sc"]
-        pick = [wf[:, c0 + 64 * q + 15:c0 + 64 * q + 64:16] for q in range(nq)]
+            mm(group(x1[:, 0:64], et), rd + ["CMe"], [X1], X1)
+        scan(out(3), T.rs[:, 64:128], x1[:, 0:64], AL.min, AL.max, [X1, "rs2"], [SN + "e"], 64, bank=[X1], init=L)
+        mm(group(R(0), kt), rd, n_("r0"), bk)
         if last:
-            act(T.oye[:, b0:b0 + 4], pick[0], AF.Copy, n_("sc"), n_("oye"), 4)
-            tt(T.oya[:, b0:b0 + 4], pick[1], AO, AL.add, n_("sc") + LD, n_("oya"), 4)
+            o = slice(16 * b0, 16 * b0 + 64)
+            ts(T.oyk[:, o], R(0), -C0, -1.0, AL.add, AL.max, n_("r0"), n_("oyk"), bank=[bk])
+            AB = [SN + "a", SN + "b"]
+            mm(group(R(1), [("I64", out(0))]), AB, n_("r1"), bk)
+            tt(W("y1"), out(1), R(1), AL.min, AB + n_("r1"), n_("y1"), bank=[bk])
+            mm(group(R(1), [("I", out(0)), ("I", out(1)), ("nI", W("y1"))]), AB + n_("y1"), n_("r1"), bk)
+            ts(T.oy0[:, o], R(1), -SH, -1.0, AL.add, AL.max, n_("r1"), n_("oy0"), bank=[bk])
+            ts(T.oy1[:, o], W("y1"), -SH, -1.0, AL.add, AL.max, n_("y1"), n_("oy1"))
+            act(T.oye[:, b0:b0 + 4], T.snd[:, sl + 15:sl + 64:16, 3], AF.Identity, [SN + "e"], n_("oye"), 4, bias=-L)
+            act(T.oya[:, b0:b0 + 4], T.snd[:, sl + 15:sl + 64:16, 4], AF.Copy, [SN + "n"], n_("oya"), 4)
             for nm, q in (("yk", "s"), ("y0", "a"), ("y1", "s")):
-                dma(q, T[nm][:, 16 * b0:16 * b0 + 64], T["o" + nm][:, 16 * b0:16 * b0 + 64], "stored", n_("o" + nm), [], 2000.0)
+                dma(q, T[nm][:, o], T["o" + nm][:, o], "stored", n_("o" + nm), [], 2000.0)
             return
-        for q in range(2):
-            act(T.snd[:, sb + 16 * q + 3:sb + 256:64], pick[q], AF.Copy, n_("sc") + [SN + "q"], [SN + "q%d" % q], 4)
-        if s == 0:
-            ts(T.snd[:, sb + 35:sb + 256:64], pick[2], 1.0, None, AL.add, None, n_("sc") + [SN + "q"], [SN + "q2"], 4)
+        if OPT["kout"] == "a":
+            act(out(2), R(0), AF.Copy, n_("r0"), [SN + "k"], bank=[bk])
         else:
-            tt(T.snd[:, sb + 35:sb + 256:64], pick[2], AO, AL.add, n_("sc") + LD + [SN + "q"], [SN + "q2"], 4)
-        SR = [SN + x for x in ("k", "p0", "p1", "q", "q0", "q1", "q2")]
+            cp(out(2), R(0), n_("r0"), [SN + "k"], bank=[bk])
+        SR = [SN + x for x in "abken"]
         blocks = [b for b in range(b0, b0 + 4) if b]
         share = [len(eng) // 4] * 4 if len(blocks) == 4 else [len(eng) // 2, len(eng) // 4, len(eng) // 4]
         sem = "arr%d" % (2 * s + h)
@@ -489,12 +503,12 @@ def build(g, T, topo, core, rank):
             rid, pid = topo.addr(peers[b], core)
             m = sum(1 << e for e in eng[at:at + n])
             at += n
-            piece = slice(512 * s + 64 * b, 512 * s + 64 * b + 64)
+            piece = slice(128 * s + 16 * b, 128 * s + 16 * b + 16)
             trs.append(RemoteDMATransfer(dst_ids=[DstId(rid=rid, pnc=pid)], dma_engine_mask=m, remote_sem=T.sem[sem],
-                                         src=T.snd[:, piece], dst=T.land[:, piece]))
+                                         src=T.snd[:, piece, :], dst=T.land[:, piece, :]))
         if h == 1:
             at += 16
-            add("s", 60.0, lambda: Q.dma_start(T.land[:, 512 * s:512 * s + 64], T.snd[:, 512 * s:512 * s + 64]).then_inc(T.sem[sem], 16),
+            add("s", 60.0, lambda: Q.dma_start(T.land[:, 128 * s:128 * s + 16, :], T.snd[:, 128 * s:128 * s + 16, :]).then_inc(T.sem[sem], 16),
                 SR, ["stay%d" % s], own=("none", 0), lat=0.0)
         add("g", CSEND, lambda: g.remote_dma_fused(trs, local_sem=T.sem.sent), SR + (["@stay%d" % s] if h == 1 else []),
             ["land%d_%d" % (s, h)], own=(sem, -at), lat=CLAND)
@@ -502,10 +516,12 @@ def build(g, T, topo, core, rank):
     for s in range(STEPS):
         head(s, 0)
         head(s, 1)
+        before_write(s)
         body(s, 0)
         body(s, 1)
+        write(s)
     for u in range(2):
-        xb = "px0%d" % u
+        xb = "px%d0" % u
         pz = T[xb]
         act(pz[:, 0:256], T.lw[:, 512 + 256 * u:768 + 256 * u], AF.Copy, ["lw"], [xb], 256, scale=4096.0, bank=[xb])
         tt(T.oyi[:, 256 * u:256 * u + 256], T.lw[:, 256 * u:256 * u + 256], pz[:, 0:256], AL.add, ["lw", xb], ["oyi%d" % u], 256, bank=[xb])
@@ -596,7 +612,7 @@ def replay(ops, order, pred, scale, lat):
     return max(done.values()), done
 
 
-CASES = (({}, 1.0), ({"p": 1.3}, 0.6), ({"a": 1.15}, 1.4))
+CASES = (({}, 1.0), ({"p": 1.2, "v": 1.1}, 1.2))
 
 
 def place_all(ops, before, key, back):
@@ -614,8 +630,7 @@ def place_all(ops, before, key, back):
         e, c, lat = ops[i][0], ops[i][1], ops[i][7]
         t = 0.0
         for j in before[i]:
-            if ops[i][6] is not None and ops[j][6] is not None and ops[i][8] < 0 and ops[j][8] < 0 and ops[i][0] == ops[j][0] \
-                    and "tb" not in (ops[i][6][0], ops[j][6][0]):
+            if ops[i][6] is not None and ops[j][6] is not None and ops[i][8] < 0 and ops[j][8] < 0 and ops[i][0] == ops[j][0]:
                 t = max(t, start[j])
             elif e == "p" and ops[j][0] == "p":
                 t = max(t, done[j] - (lat if back else ops[j][7]))
@@ -695,7 +710,74 @@ def plan(ops):
         cost = [replay(ops, order, pred, a, b)[0] for a, b in CASES]
         if sum(cost) < sum(best[0]):
             best = (cost, order, pred, 1000 + j)
-    return best
+    order = tighten(ops, pred0, soft, best[1], rng)
+    place = {x: j for j, x in enumerate(order)}
+    order, pred = ordered(ops, pred0, before, [place[i] for i in range(n)])
+    return [replay(ops, order, pred, a, b)[0] for a, b in CASES], order, pred, 0
+
+
+def tighten(ops, pred0, soft, order, rng, temp=120.0):
+    n = len(ops)
+    names = sorted(set(o[0] for o in ops) | set(b for o in ops for b in o[5]))
+    eng = [names.index(o[0]) for o in ops]
+    banks = [[names.index(b) for b in o[5]] for o in ops]
+    pe = names.index("p")
+    before = [sorted(pred0[i] | soft[i]) for i in range(n)]
+    after = [[] for _ in range(n)]
+    for i in range(n):
+        for j in before[i]:
+            after[j].append(i)
+    hard = [[j for j in pred0[i] if not (eng[i] == pe and eng[j] == pe)] for i in range(n)]
+    sets = [([o[1] * a.get(o[0], 1.0) for o in ops], [o[7] * b for o in ops]) for a, b in CASES]
+
+    def run(order, cost, lat):
+        free, last, done, why = [0.0] * len(names), [-1] * len(names), [0.0] * n, [-1] * n
+        for i in order:
+            e = eng[i]
+            t, w = free[e], last[e]
+            for j in hard[i]:
+                if done[j] > t:
+                    t, w = done[j], j
+            for b in banks[i]:
+                j = last[b]
+                if j >= 0 and eng[j] != e and done[j] > t:
+                    t, w = done[j], j
+                last[b] = i
+            t += cost[i]
+            free[e], last[e], done[i], why[i] = t, i, t + lat[i], w
+        return done, why
+
+    def value(order):
+        res = [run(order, c, l) for c, l in sets]
+        return sum(max(d) for d, w in res) / len(res), res
+
+    now, res = value(order)
+    best, keep = now, order
+    for r in range(ROUNDS):
+        done, why = res[int(rng.integers(len(res)))]
+        i = max(range(n), key=lambda x: done[x])
+        pairs = []
+        while why[i] >= 0:
+            if why[i] not in before[i]:
+                pairs.append((why[i], i))
+            i = why[i]
+        j, i = pairs[int(rng.integers(len(pairs)))]
+        a, b = order.index(j), order.index(i)
+        seg = order[a:b + 1]
+        ahead = rng.random() < 0.5
+        move = {i if ahead else j}
+        for x in (reversed(seg) if ahead else seg):
+            if any(y in move for y in (after[x] if ahead else before[x])):
+                move.add(x)
+        if i in move and j in move:
+            continue
+        trial = order[:a] + [x for x in seg if (x in move) == ahead] + [x for x in seg if (x in move) != ahead] + order[b + 1:]
+        v, rs = value(trial)
+        if v <= now or rng.random() < math.exp((now - v) / (temp * (1.0 - r / ROUNDS))):
+            order, now, res = trial, v, rs
+            if v < best:
+                best, keep = v, trial
+    return keep
 
 
 def waits(ops, order, pred):

@@ -12,26 +12,26 @@ CC = C0 - SH
 BIG = 264.0
 MIDO = 792.0
 L = 1024.0
-M1, M8, M16 = 1.5 * 2 ** 23, 1.5 * 2 ** 26, 1.5 * 2 ** 27
+M1, M8, M16, M64 = 1.5 * 2 ** 23, 1.5 * 2 ** 26, 1.5 * 2 ** 27, 1.5 * 2 ** 29
 LOW = 30000.0
 B1 = 1039
 TWN = B1 + 5128
 HB = 20480.0
-VG = (32, 32, 16, 16, 16, 16)
+VG = (32, 32, 24, 24, 24, 24)
 ONA = ("I4", "I5", "I64", "wI", "hugeone", "L2one", "nhone", "NP", "CD", "nCI", "CI", "C0I", "nqI", "nLI", "eI", "neI", "nB", "qone",
        "W64", "W62", "Kw", "CMg", "hI", "jc", "jr") + tuple("rk%d" % r for r in range(0, 16, 2))
-OPT = {"ci": "a", "kout": "a", "rmode": True}
+OPT = {"ci": "a", "kout": "a", "rmode": True, "r": "v", "fq": "v", "hi": "v"}
 SEED, TRIES, CLIMB, ROUNDS = 1, 8, 60, 40000
 FIX = {"v": (35.0, 50.0, 0.83, 80.0), "a": (70.0, 130.0, 0.83, 80.0), "p": (30.0, 40.0, 0.96, 120.0)}
 CSEND, CLAND = 600.0, 2400.0
 
-CB = ["I", "nI", "hI", "one", "T4", "S4", "Mw", "hugeone", "Kw", "nB", "BC", "nCI", "CI", "C0I", "nqI", "Lone", "nLone", "L2one",
-      "nLI", "nhone", "eI", "I4", "I5", "I64", "qone", "W64", "wI", "none", "neI", "nP2", "Q2"]
+CB = ["I", "nI", "hI", "one", "T4", "Mw", "hugeone", "Kw", "nB", "BC", "nCI", "CI", "C0I", "Lone", "nLone", "L2one",
+      "nLI", "nhone", "eI", "I4", "I5", "I64", "qone", "W64", "wI", "none", "neI", "nP2", "Q2", "LI"]
 CH = ["W62", "Kw2"]
-WB = ["ci", "ok", "vp", "win", "bit", "oh", "oq"]
+WB = ["ci", "ok", "vp", "win", "bit", "oh", "oq", "cnt"]
 WH = {"k0": 0, "ra": 1, "rb": 2, "pm": 3, "mx": 4, "mid": 5, "hf": 6, "e1": 7, "er": 8, "zj": 9, "ljn": 10, "jb": 11, "f": 12, "fq": 13,
       "wz": 14, "s": 15, "kk": 17, "dr": 18, "de": 19, "se": 20, "y1": 21}
-WF = {"sj": 0, "sg": 1, "r": 2, "prs": 3, "y": 4, "ry": 5}
+WF = {"sj": 0, "sg": 1, "r": 2, "prs": 3, "y": 4, "ry": 5, "hi": 6}
 
 SCRATCH = {
     "sts": ("sbuf", [128, 4096], "bfloat16"), "ivs": ("sbuf", [128, 1024], "int32"), "e0s": ("sbuf", [128, 8], "int32"),
@@ -39,6 +39,7 @@ SCRATCH = {
     "cf": ("sbuf", [128, 1536], "float32"), "ci": ("sbuf", [128, 64], "int32"), "col": ("sbuf", [128, 16], "float32"),
     "cb": ("sbuf", [128, len(CB) * 128], "bfloat16"), "ch": ("sbuf", [128, len(CH) * 128 + 160], "float16"),
     "bw": ("sbuf", [128, 2048], "bfloat16"), "uu": ("sbuf", [128, 144], "bfloat16"),
+    "bt": ("sbuf", [128, 384], "bfloat16"), "bv": ("sbuf", [128, 2048], "bfloat16"),
     "cm": ("sbuf", [128, 320], "bfloat16"), "rs": ("sbuf", [128, 128], "float32"),
     "snd": ("sbuf", [128, 6 * 128, 5], "float16"), "land": ("sbuf", [128, 5 * 128, 5], "float16"),
     "offw": ("sbuf", [128, 32], "uint16"), "ee": ("sbuf", [128, 256], "float16"), "hb": ("sbuf", [128, 8], "bfloat16"), "ohj": ("sbuf", [128, 128], "bfloat16"),
@@ -56,7 +57,7 @@ for _h in range(2):
     SCRATCH["cc%d" % _h] = ("sbuf", [128, 64], "uint16")
     SCRATCH["wb%d" % _h] = ("sbuf", [128, len(WB) * 64], "bfloat16")
     SCRATCH["wh%d" % _h] = ("sbuf", [128, 22 * 64], "float16")
-    SCRATCH["wf%d" % _h] = ("sbuf", [128, 6 * 64], "float32")
+    SCRATCH["wf%d" % _h] = ("sbuf", [128, 7 * 64], "float32")
     for _n in ("px0", "px1", "ps", "pt"):
         SCRATCH[_n + str(_h)] = ("psum", [128, 512], "float32")
 
@@ -105,9 +106,9 @@ def build(g, T, topo, core, rank):
         if n[:2] == "uu":
             k = int(n[2:])
             return T.uu[:, 15 - k:143 - k]
-        if n[:2] == "bw":
+        if n[:2] in ("bw", "bv"):
             k = int(n[2:])
-            return T.bw[:, 128 * k:128 * k + 128]
+            return T[n[:2]][:, 128 * k:128 * k + 128]
         j = CB.index(n)
         return T.cb[:, 128 * j:128 * j + 128]
 
@@ -117,7 +118,7 @@ def build(g, T, topo, core, rank):
             for o, l, r, a, b, n in lst:
                 last = P.matmul(o, C(l), r, a, b)
             return last
-        names = sorted(set("uu" if x[1][:2] == "uu" else x[1] for x in lst))
+        names = sorted(set(x[1][:2] if x[1][:2] in ("uu", "bw", "bv") else x[1] for x in lst))
         add("p", 30.0 + sum(0.5 * max(64, x[5]) for x in lst), emit, list(rd) + names, wr, [bank], lat=100.0)
 
     def group(out, terms, n=64, start=True, stop=True):
@@ -162,36 +163,47 @@ def build(g, T, topo, core, rank):
     ts(am, T.cf[:, 0:128], col(0), None, AL.subtract, None, ["mi", "c0"], ["am"], 128)
     ts(C("I"), am, 0.0, None, AL.is_equal, None, ["am"], ["I"], 128)
     ts(C("one"), gi, col(1), None, AL.is_equal, None, ["gi", "c1"], ["one"], 128)
-    for src, lst in (("I", (("nI", -1.0), ("hI", 0.5), ("nCI", -CC), ("CI", CC), ("C0I", C0), ("nqI", -0.25), ("nLI", -L), ("eI", 0.5 / L),
+    for src, lst in (("I", (("nI", -1.0), ("hI", 0.5), ("nCI", -CC), ("CI", CC), ("C0I", C0), ("nLI", -L), ("eI", 0.5 / L),
                             ("neI", -1.0 / L), ("I4", 4.0), ("I5", 5.0), ("I64", 64.0), ("wI", 17.0 / 16))),
                      ("one", (("nB", -BIG), ("Lone", L), ("nLone", -L), ("none", -1.0), ("qone", 0.25), ("hugeone", -2.0 ** 90),
                               ("L2one", 2 * L), ("nhone", -0.5)))):
         for n, k in lst:
             lin(C(n), C(src), k, 0.0, [src], [n], 128, 0.5)
     tt(C("BC"), C("nCI"), C("nB"), AL.subtract, ["nCI", "nB"], ["BC"], 128)
-    ts(t1, ml, 0.0, None, AL.is_equal, None, ["ml"], ["t1"], 128)
-    ts(t2, ml, 0.0, 2.0, AL.not_equal, AL.mult, ["ml"], ["t2"], 128)
-    scan(t3, t2, t1, AL.mult, AL.add, ["t1", "t2"], ["t3"], 128)
-    ts(t4, ml, 0.0, 0.5, AL.not_equal, AL.mult, ["ml"], ["t4"], 128)
-    scan(t5, t4, t1, AL.mult, AL.add, ["t1", "t4"], ["t5"], 128)
     ts(m16, T.cf[:, 0:16], col(2), None, AL.is_equal, None, ["mi", "c1"], ["m16"])
-    for j, src, sn in ((5, t3, "t3"), (6, t5, "t5")):
-        tmp = T.cf[:, 1440 + 16 * (j - 5):1456 + 16 * (j - 5)]
-        tt(tmp, T.cf[:, 784 + 256 * (j - 5):800 + 256 * (j - 5)], m16, AL.mult, [sn, "m16"], ["tm%d" % j], 16)
-        add("v", vc(16, 1.0), lambda tmp=tmp, j=j: V.tensor_reduce(col(j), tmp, AxisListType.X, AL.add), ["tm%d" % j], ["c%d" % j])
-    act(t7, t3, AF.Square, ["t3"], ["t7"], 128)
-    tt(C("S4"), t7, C("one"), AL.mult, ["t7", "one"], ["S4"], 128)
-    ts(C("T4"), C("S4"), col(6), col(6), AL.mult, AL.mult, ["S4", "c6"], ["T4"], 128, 0.5)
+    ts(T.uu[:], mi, 15.0, col(1), AL.subtract, AL.is_equal, ["mi", "c1"], ["uu"], 144)
+    LN2 = math.log(2.0)
+    e1, e2, e3 = [T.bt[:, 128 * j:128 * j + 128] for j in range(3)]
+    lin(col(5), col(2), -2 * LN2, 0.0, ["c1"], ["c5"], 1)
+    act(e1, ml, AF.Exp, ["ml", "c5"], ["e1"], 128, bias=col(5), scale=2 * LN2)
+    tt(C("T4"), e1, C("one"), AL.mult, ["e1", "one"], ["T4"], 128)
+    wk, gm = T.cf[:, 1440:1456], T.cf[:, 1456:1464]
     if OPT["rmode"]:
-        ts(T.cf[:, 528:672], mi, 15.0, col(1), AL.subtract, AL.is_equal, ["mi", "c1", "t1", "t2"], ["t1", "t2"], 144)
-        ts(T.uu[:], T.cf[:, 528:672], col(5), None, AL.mult, None, ["t1", "t2", "c5"], ["uu"], 144)
-        ts(C("nP2"), C("none"), col(5), None, AL.mult, None, ["none", "c5"], ["nP2"], 128, 0.5)
-        ts(C("Q2"), C("one"), col(6), 0.5, AL.mult, AL.mult, ["one", "c6"], ["Q2"], 128, 0.5)
+        io(T.ji[:, 0:128], [[-1, 128]], 128, 1, ["vi"], 128, False)
+        ts(T.ji[:, 128:256], T.ji[:, 0:128], 15, None, AL.bitwise_and, None, ["vi"], ["nv"], 128)
+        cp(t1, T.ji[:, 128:256], ["nv"], ["t1"], 128)
+        act(e2, t1, AF.Exp, ["t1"], ["e2"], 128, bias=6 * LN2, scale=LN2)
+        act(e3, t1, AF.Exp, ["t1"], ["e3"], 128, bias=-7 * LN2, scale=-LN2)
+        tt(C("Q2"), e3, C("one"), AL.mult, ["e3", "one"], ["Q2"], 128)
+        tt(t2, e2, C("none"), AL.mult, ["e2", "none"], ["t2"], 128)
+        tt(wk, T.bt[:, 128:144], m16, AL.add, ["e2", "m16"], ["wk"], 16)
     else:
-        ts(T.uu[:], mi, 15.0, col(1), AL.subtract, AL.is_equal, ["mi", "c1"], ["uu"], 144)
-        ts(C("nP2"), C("one"), -1.0, None, AL.mult, None, ["one"], ["nP2"], 128, 0.5)
-        for k in range(16):
-            ts(C("bw%d" % k), C("I"), 4.0 ** -k, None, AL.mult, None, ["I"], ["bw%d" % k], 128, 0.5)
+        act(e3, ml, AF.Exp, ["ml"], ["e3"], 128, scale=2 * LN2)
+        tt(C("Q2"), e3, C("one"), AL.mult, ["e3", "one"], ["Q2"], 128)
+        lin(t2, C("one"), -64.0, 0.0, ["one"], ["t2"], 128)
+        lin(wk, m16, 1.0, 64.0, ["m16"], ["wk"], 16)
+        lin(T.bv[:, 0:128], C("I"), 1.0, 0.0, ["I"], ["bv"], 128, 0.5)
+        for j in range(4):
+            lin(T.bv[:, 128 << j:256 << j], T.bv[:, 0:128 << j], 4.0 ** -(1 << j), 0.0, ["bv"], ["bv"], 128 << j, 0.5)
+    lin(t3, C("I"), -16.0, 0.0, ["I"], ["t3"], 128)
+    tt(C("nP2"), t2, t3, AL.add, ["t2", "t3"], ["nP2"], 128)
+    ts(gm, T.cf[:, 144:272:16], col(1), None, AL.is_equal, None, ["gi", "c1"], ["gm"], 8)
+    lin(T.bw[:, 0:128], C("I"), 1.0, 0.0, ["I"], ["z0"], 128, 0.5)
+    for j in range(4):
+        lin(T.bw[:, 128 << j:256 << j], T.bw[:, 0:128 << j], 1.0, 0.0, ["z%d" % x for x in range(j + 1)], ["z%d" % (j + 1)], 128 << j, 0.5)
+    for q in range(8):
+        lin(T.bw[:, 16 * q:16 * q + 1936:129], wk, T.cf[:, 1456 + q:1457 + q], 0.0, ["wk", "gm"] + ["z%d" % x for x in range(5)], ["zz%d" % q], 16)
+    ZZ = ["zz%d" % q for q in range(8)]
     ts(t4, am, 0.0, -93.0 / 64, AL.is_gt, AL.mult, ["am"], ["t4"], 128)
     act(t5, C("I"), AF.Identity, ["I"], ["t5"], 128, scale=67.0 / 64, bias=-3.0 / 64)
     tt(t7, t4, t5, AL.add, ["t4", "t5"], ["t7"], 128)
@@ -214,6 +226,10 @@ def build(g, T, topo, core, rank):
     lin(CMa, dg, 65.0, -64.0, ["dg"], ["CMa"])
     lin(CMe, dg, LOW + 963.5, -LOW, ["dg"], ["CMe"])
     lin(NP, dg, 0.0, col(10), ["dg", "c10"], ["NP"])
+    if OPT["r"] == "a":
+        fill(T.cm[:, 256:320], HB, ["c20"])
+    if OPT["fq"] == "a":
+        lin(C("LI"), C("I"), L, 0.0, ["I"], ["LI"], 128, 0.5)
     lin(CD, dg, 0.0, col(11), ["dg", "c11"], ["CD"])
     ts(T.rs[:, 0:64], T.cf[:, 272:336], 0.0, -1.0e6, AL.is_equal, AL.mult, ["ml"], ["rs"])
     lin(T.rs[:, 64:128], T.cf[:, 272:336], 1.0e6, L, ["ml"], ["rs2"])
@@ -383,17 +399,21 @@ def build(g, T, topo, core, rank):
         for u in range(2):
             EU = n_("em%d" % u)
             ks = range(8 * u, 8 * u + 8)
-            if one:
-                first = [("nqI", KN)] if u == 0 else []
-                mm(group(PC, first + [("I", em[:, 64 * k:64 * k + 64]) for k in ks], 64, u == 0, u == 1), EU + LD + [X0] * u, [X0], X0)
             first = [("nP2", B("ci"))] if one and u == 0 else []
-            mm(group(PR, first + [("uu%d" % k, em[:, 64 * k:64 * k + 64]) for k in ks], 64, u == 0, u == 1),
-               EU + (n_("ci") if one else []) + [XT] * u, [XT], XT)
-        if one and not OPT["rmode"]:
-            mm(group(PB, [("bw%d" % k, em[:, 64 * k:64 * k + 64]) for k in range(16)]), n_("em0", "em1"), [X1], X1)
-        ts(B("ok"), PR, 0.0 if one else 0.5, None, AL.is_equal if one else AL.is_gt, None, [XT], n_("ok"), bank=[XT])
-        if one and OPT["rmode"]:
-            act(F("prs"), PR, AF.Relu, [XT], n_("prs"), bias=0.25, bank=[XT])
+            mm(group(PR, first + [(("bw%d" if one else "uu%d") % k, em[:, 64 * k:64 * k + 64]) for k in ks], 64, u == 0, u == 1),
+               EU + (n_("ci") + ZZ if one else []) + [XT] * u, [XT], XT)
+        if one:
+            if OPT["hi"] == "v":
+                ts(F("hi"), PR, M64, M64, AL.add, AL.subtract, [XT], n_("hi"), bank=[XT])
+                tt(F("y"), PR, F("hi"), AL.subtract, [XT] + n_("hi"), n_("cnt", "y"), bank=[XT])
+            else:
+                act(B("cnt"), PR, AF.Identity, [XT], n_("hi"), bias=12288.0, bank=[XT])
+                tt(F("y"), PR, B("cnt"), AL.subtract, [XT] + n_("hi"), n_("cnt", "y"), bank=[XT])
+            ts(B("ok"), PR, M64, M64, AL.add, AL.is_equal, [XT], n_("ok"), bank=[XT])
+            if OPT["rmode"]:
+                act(F("prs"), PR, AF.Relu, [XT], n_("prs"), bias=32.0, bank=[XT])
+        else:
+            ts(B("ok"), PR, 0.5, None, AL.is_gt, None, [XT], n_("ok"), bank=[XT])
         mm(group(R(2), [("T4", B("ok"))]), n_("ok"), n_("r2"), bk)
         ts(OHJ, R(2), M1, M1 + 1.0, AL.add, AL.is_equal, n_("r2"), n_("ohj"), bank=[bk])
         mm(group(R(2), [("I", CMj), ("Kw2", OHJ)]), n_("ohj") + ["CMj"], n_("r2"), bk)
@@ -406,19 +426,29 @@ def build(g, T, topo, core, rank):
             act(W("ljn", 2), R(3, 2), AF.Relu, n_("r3", "r4"), n_("ljn"), 128, bias=-L, bank=[bk])
             JN, JR, JB, JBR = ("I", W("ljn")), n_("ljn"), W("jb"), n_("ljn")
             tt(W("f"), W("pm"), W("zj"), AL.min, n_("pm", "zj"), n_("f"))
-            mm(group(R(5), [("I", NP), ("nhone", OHJ), ("eI", W("ljn")), ("one", W("f"))]), n_("ohj", "ljn", "f") + ["NP"], n_("r5"), bk)
-            ts(F("r"), R(5), M16, M16, AL.add, AL.subtract, n_("r5"), n_("r"), bank=[bk])
-            tt(B("oq"), F("r"), R(5), AL.is_equal, n_("r", "r5"), n_("oq"), bank=[bk])
-            tt(W("fq"), B("oq"), W("f"), AL.mult, n_("oq", "f"), n_("fq"))
+            if OPT["r"] == "v":
+                mm(group(R(5), [("I", NP), ("nhone", OHJ), ("eI", W("ljn")), ("one", W("f"))]), n_("ohj", "ljn", "f") + ["NP"], n_("r5"), bk)
+                ts(F("r"), R(5), M16, M16, AL.add, AL.subtract, n_("r5"), n_("r"), bank=[bk])
+                tt(B("oq"), F("r"), R(5), AL.is_equal, n_("r", "r5"), n_("oq"), bank=[bk])
+            else:
+                mm(group(R(5), [("I", NP), ("I", T.cm[:, 256:320]), ("nhone", OHJ), ("eI", W("ljn")), ("one", W("f"))]),
+                   n_("ohj", "ljn", "f") + ["NP", "c20"], n_("r5"), bk)
+                act(W("rb"), R(5), AF.Copy, n_("r5"), n_("r"), bank=[bk])
+                tt(B("oq"), W("rb"), R(5), AL.is_equal, n_("r", "r5"), n_("oq"), bank=[bk])
+            if OPT["fq"] == "v":
+                tt(W("fq"), B("oq"), W("f"), AL.mult, n_("oq", "f"), n_("fq"))
+            else:
+                mm(group(R(5), [("I", W("f")), ("LI", B("oq"))]), n_("oq", "f"), n_("r5"), bk)
+                act(W("fq"), R(5), AF.Relu, n_("r5"), n_("fq"), bias=-L, bank=[bk])
         else:
             JN, JR = ("Lone", OHJ), n_("ohj")
             if one:
                 mm(group(R(4), [("I", PB_), ("Lone", OHJ)]), LD + n_("ohj"), n_("r4"), bk)
                 act(out(0), R(4), AF.Relu, n_("r4"), [SN + "a"], bias=-L, bank=[bk])
                 JB, JBR = out(0), [SN + "a"]
-        OH, OHR = (B("oh"), n_("oh")) if one else (OHJ, n_("ohj"))
+        WR = n_("win") if one else []
         if one:
-            act(B("vp"), PC, AF.Exp, [X0], n_("vp"), scale=math.log(32.0), bank=[X0])
+            act(B("vp"), F("y"), AF.Exp, n_("cnt", "y"), n_("vp"), scale=math.log(32.0), bias=0.0 if OPT["hi"] == "v" else 12288.0 * math.log(32.0))
             mm(group(R(6), [("hugeone", B("ok")), ("Mw", B("vp"))]), n_("vp", "ok"), n_("r6"), bk)
             ts(B("win"), R(6), 2.0, None, AL.is_gt, None, n_("r6"), n_("win"), bank=[bk])
             if OPT["rmode"]:
@@ -426,20 +456,23 @@ def build(g, T, topo, core, rank):
                 tt(F("y"), F("prs"), R(6), AL.mult, n_("prs", "r6"), n_("y"), bank=[bk])
                 ts(F("ry"), F("y"), M1, M1, AL.add, AL.subtract, n_("y"), n_("ry"))
                 tt(B("bit"), F("ry"), F("y"), AL.is_gt, n_("ry", "y"), n_("bit"))
-                mm(group(R(6), [("T4", B("ok")), ("T4", B("bit"))]), n_("ok", "bit"), n_("r6"), bk)
+                mm(group(R(6), [("T4", B("bit"))]), n_("bit"), n_("r6"), bk)
             else:
-                tt(B("bit"), B("win"), PB, AL.mult, n_("win") + [X1], n_("bit"), bank=[X1])
-                mm(group(R(6), [("T4", B("ok")), ("S4", B("bit"))]), n_("ok", "bit"), n_("r6"), bk)
+                for u in range(2):
+                    mm(group(PC, [("bv%d" % k, em[:, 64 * k:64 * k + 64]) for k in range(8 * u, 8 * u + 8)], 64, u == 0, u == 1),
+                       n_("em%d" % u) + [X0] * u, [X0], X0)
+                tt(B("bit"), B("win"), PC, AL.mult, n_("win") + [X0], n_("bit"), bank=[X0])
+                mm(group(R(6), [("Q2", B("bit"))]), n_("bit"), n_("r6"), bk)
             ts(B("oh"), R(6), M1, M1 + 1.0, AL.add, AL.is_equal, n_("r6"), n_("oh"), bank=[bk])
             mm(group(R(6), [("I", CMg), ("Kw", B("oh"))]), n_("oh") + ["CMg"], n_("r6"), bk)
             scan(F("sg"), T.rs[:, 0:64], R(6), AL.add, AL.max, n_("r6") + ["rs"], n_("sg"), 64, bank=[bk])
             cp(offz[:, 4:8], wf[:, 64 * WF["sg"] + 15:64 * WF["sg"] + 64:16], n_("sg"), n_("offg"), 4)
             tt(W("wz"), yy[:].indirect(offz[:, 4:8]), B("win"), AL.mult, YR + n_("offg", "ym", "win"), n_("wz"), c=1.8)
-        keep = [("Lone", OH)] + ([("nLone", OHJ), JN] if two else [])
-        mm(group(xt[:, 0:64], [("I", KN)] + keep) + group(xt[:, 64:128], [("I", CD), ("I4", E1), ("nLone", OH)])
-           + group(xt[:, 128:192], [("I", E1), ("nLone", OH)]) + group(xt[:, 192:256], [("I", ER), JN]),
-           LD + OHR + JR + n_("ohj") + ["CD", "ee"], [XT], XT)
-        act(W("kk", 4), xt[:, 0:256], AF.Relu, [XT], n_("kk"), 256, bias=-L, bank=[XT])
+        alive = [("nLone", OHJ)] + ([("nLone", B("win"))] if one else [])
+        mm(group(x1[:, 0:64], [("I", KN), JN] + ([("Lone", B("win"))] if one else [])) + group(x1[:, 64:128], [("I", CD), ("I4", E1)] + alive)
+           + group(x1[:, 128:192], [("I", E1)] + alive) + group(x1[:, 192:256], [("I", ER), JN]),
+           LD + WR + JR + n_("ohj") + ["CD", "ee"], [X1], X1)
+        act(W("kk", 4), x1[:, 0:256], AF.Relu, [X1], n_("kk"), 256, bias=-L, bank=[X1])
         if two:
             d0, d1 = x0[:, 0:128:2], x0[:, 1:128:2]
             mm([(x0[:, 0:128], "nI", PAB, True, False, 128), (d0, "nLI", B("win"), False, False, 64), (d1, "nLI", B("win"), False, False, 64)],
@@ -464,8 +497,8 @@ def build(g, T, topo, core, rank):
             kt += [("CI", B("oq")), ("I", W("fq"))]
             et += [("W62", B("oq")), ("qone", W("fq"))]
             rd += n_("oq", "fq")
-        at = [("I", CMa), ("none", OH)] + ([("I", AO)] if one else []) + ([("one", OHJ), ("neI", W("ljn"))] if two else [])
-        mm(group(x1[:, 64:128], at), LD + OHR + JR + n_("ohj") + ["CMa"], [X1], X1)
+        at = [("I", CMa), ("neI", W("ljn")) if two else ("none", OHJ)] + ([("I", AO), ("none", B("win"))] if one else [])
+        mm(group(x1[:, 64:128], at), LD + WR + JR + ["CMa"], [X1], X1)
         scan(out(4), T.rs[:, 0:64], x1[:, 64:128], AL.add, AL.max, [X1, "rs"], [SN + "n"], 64, bank=[X1])
         if one:
             mm(group(x1[:, 0:64], et + [("W64", B("win"))], 64, True, False), rd + n_("win") + ["CMe"], [X1], X1)

@@ -17,16 +17,17 @@ LOW = 30000.0
 B1 = 1039
 TWN = B1 + 5128
 HB = 20480.0
-VG = (32, 32, 24, 24, 24, 24)
-ONA = ("I4", "I5", "I64", "wI", "hugeone", "L2one", "nhone", "NP", "CD", "nCI", "CI", "C0I", "nqI", "nLI", "eI", "neI", "nB", "qone",
-       "W64", "W62", "Kw", "CMg", "hI", "jc", "jr") + tuple("rk%d" % r for r in range(0, 16, 2))
-OPT = {"ci": "a", "kout": "a", "rmode": True, "r": "v", "fq": "v", "hi": "v"}
-SEED, TRIES, CLIMB, ROUNDS = 1, 8, 60, 40000
+VG = (32, 32) + (32, 16) * 5
+ONA = ("I4", "I5", "I128", "wI", "hugeone", "L2one", "nhone", "NP", "CD", "nCI", "CI", "C0I", "nqI", "nLI", "eI", "neI", "nB", "qone",
+       "W64", "W62", "Kw", "CMg", "hI", "jc", "jr", "z3", "z4") + tuple("rk%d" % r for r in range(16))
+OPT = {"ci": "a", "kout": "aa", "nout": "aa", "gate": False, "rmode": True, "r": "v", "fq": "v"}
+SEED, TRIES, CLIMB, PERIOD = 10, 4, 8, 16000.0
+ROUNDS = ((1500, 120.0, False, 0, 1), (6000, 300.0, True, 0, 1), (20000, 140.0, True, 1, 3), (5000, 40.0, False, 1, 3))
 FIX = {"v": (35.0, 50.0, 0.83, 80.0), "a": (70.0, 130.0, 0.83, 80.0), "p": (30.0, 40.0, 0.96, 120.0)}
 CSEND, CLAND = 600.0, 2400.0
 
 CB = ["I", "nI", "hI", "one", "T4", "Mw", "hugeone", "Kw", "nB", "BC", "nCI", "CI", "C0I", "Lone", "nLone", "L2one",
-      "nLI", "nhone", "eI", "I4", "I5", "I64", "qone", "W64", "wI", "none", "neI", "nP2", "Q2", "LI"]
+      "nLI", "nhone", "eI", "I4", "I5", "I128", "qone", "W64", "wI", "none", "neI", "nP2", "Q2", "LI"]
 CH = ["W62", "Kw2"]
 WB = ["ci", "ok", "vp", "win", "bit", "oh", "oq", "cnt"]
 WH = {"k0": 0, "ra": 1, "rb": 2, "pm": 3, "mx": 4, "mid": 5, "hf": 6, "e1": 7, "er": 8, "zj": 9, "ljn": 10, "jb": 11, "f": 12, "fq": 13,
@@ -38,7 +39,7 @@ SCRATCH = {
     "lw": ("sbuf", [128, 1024], "float32"), "tw": ("sbuf", [128, TWN], "float32"),
     "cf": ("sbuf", [128, 1536], "float32"), "ci": ("sbuf", [128, 64], "int32"), "col": ("sbuf", [128, 16], "float32"),
     "cb": ("sbuf", [128, len(CB) * 128], "bfloat16"), "ch": ("sbuf", [128, len(CH) * 128 + 160], "float16"),
-    "bw": ("sbuf", [128, 2048], "bfloat16"), "uu": ("sbuf", [128, 144], "bfloat16"),
+    "bw": ("sbuf", [128, 2048], "bfloat16" if OPT["rmode"] else "float16"), "uu": ("sbuf", [128, 144], "bfloat16"),
     "bt": ("sbuf", [128, 384], "bfloat16"), "bv": ("sbuf", [128, 2048], "bfloat16"),
     "cm": ("sbuf", [128, 320], "bfloat16"), "rs": ("sbuf", [128, 128], "float32"),
     "snd": ("sbuf", [128, 6 * 128, 5], "float16"), "land": ("sbuf", [128, 5 * 128, 5], "float16"),
@@ -54,6 +55,7 @@ for _h in range(2):
     SCRATCH["em%d" % _h] = ("sbuf", [128, 1024], "bfloat16")
     SCRATCH["off%d" % _h] = ("sbuf", [128, 8], "uint16")
     SCRATCH["offz%d" % _h] = ("sbuf", [128, 8], "uint16")
+    SCRATCH["ob%d" % _h] = ("sbuf", [128, 192], "bfloat16")
     SCRATCH["cc%d" % _h] = ("sbuf", [128, 64], "uint16")
     SCRATCH["wb%d" % _h] = ("sbuf", [128, len(WB) * 64], "bfloat16")
     SCRATCH["wh%d" % _h] = ("sbuf", [128, 22 * 64], "float16")
@@ -62,7 +64,7 @@ for _h in range(2):
         SCRATCH[_n + str(_h)] = ("psum", [128, 512], "float32")
 
 SEMAPHORES = ["sv", "sa", "sp", "sg", "sent", "le", "li", "ls0", "ls1", "stored"] + ["arr%d" % k for k in range(10)]
-BLK0 = (4, 0)
+BLK0 = (0, 4)
 
 
 def build(g, T, topo, core, rank):
@@ -163,13 +165,13 @@ def build(g, T, topo, core, rank):
     ts(am, T.cf[:, 0:128], col(0), None, AL.subtract, None, ["mi", "c0"], ["am"], 128)
     ts(C("I"), am, 0.0, None, AL.is_equal, None, ["am"], ["I"], 128)
     ts(C("one"), gi, col(1), None, AL.is_equal, None, ["gi", "c1"], ["one"], 128)
-    for src, lst in (("I", (("nI", -1.0), ("hI", 0.5), ("nCI", -CC), ("CI", CC), ("C0I", C0), ("nLI", -L), ("eI", 0.5 / L),
-                            ("neI", -1.0 / L), ("I4", 4.0), ("I5", 5.0), ("I64", 64.0), ("wI", 17.0 / 16))),
+    for src, lst in (("I", (("nI", -1.0), ("hI", 0.5), ("nCI", -CC), ("C0I", C0), ("nLI", -L), ("eI", 0.5 / L),
+                            ("neI", -1.0 / L), ("I4", 4.0), ("I5", 5.0), ("I128", 128.0), ("wI", 17.0 / 16))),
                      ("one", (("nB", -BIG), ("Lone", L), ("nLone", -L), ("none", -1.0), ("qone", 0.25), ("hugeone", -2.0 ** 90),
                               ("L2one", 2 * L), ("nhone", -0.5)))):
         for n, k in lst:
             lin(C(n), C(src), k, 0.0, [src], [n], 128, 0.5)
-    tt(C("BC"), C("nCI"), C("nB"), AL.subtract, ["nCI", "nB"], ["BC"], 128)
+    tt(C("BC"), C("nCI"), C("nB"), AL.add, ["nCI", "nB"], ["BC"], 128)
     ts(m16, T.cf[:, 0:16], col(2), None, AL.is_equal, None, ["mi", "c1"], ["m16"])
     ts(T.uu[:], mi, 15.0, col(1), AL.subtract, AL.is_equal, ["mi", "c1"], ["uu"], 144)
     LN2 = math.log(2.0)
@@ -190,15 +192,16 @@ def build(g, T, topo, core, rank):
     else:
         act(e3, ml, AF.Exp, ["ml"], ["e3"], 128, scale=2 * LN2)
         tt(C("Q2"), e3, C("one"), AL.mult, ["e3", "one"], ["Q2"], 128)
-        lin(t2, C("one"), -64.0, 0.0, ["one"], ["t2"], 128)
-        lin(wk, m16, 1.0, 64.0, ["m16"], ["wk"], 16)
+        lin(C("nP2"), C("I"), -16 * L, 0.0, ["I"], ["nP2"], 128, 0.5)
+        lin(wk, m16, L, 1.0, ["m16"], ["wk"], 16)
         lin(T.bv[:, 0:128], C("I"), 1.0, 0.0, ["I"], ["bv"], 128, 0.5)
         for j in range(4):
             lin(T.bv[:, 128 << j:256 << j], T.bv[:, 0:128 << j], 4.0 ** -(1 << j), 0.0, ["bv"], ["bv"], 128 << j, 0.5)
-    lin(t3, C("I"), -16.0, 0.0, ["I"], ["t3"], 128)
-    tt(C("nP2"), t2, t3, AL.add, ["t2", "t3"], ["nP2"], 128)
+    if OPT["rmode"]:
+        lin(t3, C("I"), -16.0, 0.0, ["I"], ["t3"], 128)
+        tt(C("nP2"), t2, t3, AL.add, ["t2", "t3"], ["nP2"], 128)
     ts(gm, T.cf[:, 144:272:16], col(1), None, AL.is_equal, None, ["gi", "c1"], ["gm"], 8)
-    lin(T.bw[:, 0:128], C("I"), 1.0, 0.0, ["I"], ["z0"], 128, 0.5)
+    lin(T.bw[:, 0:128], C("I"), 1.0 if OPT["rmode"] else L, 0.0, ["I"], ["z0"], 128, 0.5)
     for j in range(4):
         lin(T.bw[:, 128 << j:256 << j], T.bw[:, 0:128 << j], 1.0, 0.0, ["z%d" % x for x in range(j + 1)], ["z%d" % (j + 1)], 128 << j, 0.5)
     for q in range(8):
@@ -208,13 +211,12 @@ def build(g, T, topo, core, rank):
     act(t5, C("I"), AF.Identity, ["I"], ["t5"], 128, scale=67.0 / 64, bias=-3.0 / 64)
     tt(t7, t4, t5, AL.add, ["t4", "t5"], ["t7"], 128)
     tt(C("Mw"), t7, C("one"), AL.mult, ["t7", "one"], ["Mw"], 128)
-    lin(col(7), col(2), 64.0, -SH / 4, ["c1"], ["c7"], 1)
     lin(col(8), col(2), 1.0, 1040.0, ["c1"], ["c8"], 1)
     lin(col(9), col(2), -256.0, C0 - 4 * L, ["c1"], ["c9"], 1)
     lin(col(10), col(2), -1.0, 0.5, ["c1"], ["c10"], 1)
     lin(col(11), col(2), -256.0, C0 - 3 * L, ["c1"], ["c11"], 1)
     lin(col(12), col(2), 64.0, 0.0, ["c1"], ["c12"], 1)
-    for n, j in (("Kw", 2), ("W64", 12), ("W62", 7), ("Kw2", 8)):
+    for n, j in (("Kw", 2), ("W64", 12), ("Kw2", 8)):
         lin(C(n), C("one"), col(j), 0.0, ["one", "c1" if j == 2 else "c%d" % j], [n], 128, 0.5)
     ts(dg, T.cf[:, 272:336], col(2), None, AL.is_equal, None, ["ml", "c1"], ["dg"])
     CMg, CMj, CMa, NP = T.cm[:, 0:64], T.cm[:, 64:128], T.cm[:, 128:192], T.cm[:, 192:256]
@@ -226,6 +228,8 @@ def build(g, T, topo, core, rank):
     lin(CMa, dg, 65.0, -64.0, ["dg"], ["CMa"])
     lin(CMe, dg, LOW + 963.5, -LOW, ["dg"], ["CMe"])
     lin(NP, dg, 0.0, col(10), ["dg", "c10"], ["NP"])
+    add("v", vc(128, 0.5), lambda: V.memset(T.bt[:, 0:128], 0.0), ["T4"], ["e1"])
+    add("v", vc(64, 0.5), lambda: V.memset(T.bt[:, 128:192], -L), ["T4"], ["e2"])
     if OPT["r"] == "a":
         fill(T.cm[:, 256:320], HB, ["c20"])
     if OPT["fq"] == "a":
@@ -274,7 +278,7 @@ def build(g, T, topo, core, rank):
         off = T["off" + H]
         if s > 0:
             l0 = 128 * (s - 1) + 16 * BLK0[h]
-            LD = ["land%d_%d" % (s - 1, h)]
+            LD = ["land%d_%d" % (s - 1, h)] + ([] if BLK0[h] else ["stay%d" % (s - 1)])
             e16, a16 = T.land[:, l0 + 15:l0 + 64:16, 3], T.land[:, l0 + 15:l0 + 64:16, 4]
             ts(off[:, 4:8], e16, -L, None, AL.add, None, LD, ["offe" + H], 4)
         src, sn = (T.lw, "lw") if s else (T.ivs, "ivs")
@@ -284,7 +288,7 @@ def build(g, T, topo, core, rank):
         tag[0] = 2 * s + 1
         if s > 0:
             l0 = 128 * (s - 1)
-            LD = ["land%d_0" % (s - 1), "land%d_1" % (s - 1)]
+            LD = ["land%d_0" % (s - 1), "land%d_1" % (s - 1), "stay%d" % (s - 1)]
             e16, a16 = T.land[:, l0 + 15:l0 + 128:16, 3], T.land[:, l0 + 15:l0 + 128:16, 4]
             act(T.hb[:], e16, AF.Identity, LD, ["hb"], 8, bias=HB - L - 63.75)
             ps = T.ps1
@@ -343,19 +347,19 @@ def build(g, T, topo, core, rank):
         ER, E1 = T.ee[:, 16 * b0:16 * b0 + 64], T.ee[:, 128 + 16 * b0:192 + 16 * b0]
         if s > 0:
             l0 = 128 * (s - 1) + 16 * b0
-            LD = ["land%d_%d" % (s - 1, h)]
+            LD = ["land%d_%d" % (s - 1, h)] + ([] if b0 else ["stay%d" % (s - 1)])
             PA, PB_, KN, AO = [T.land[:, l0:l0 + 64, j] for j in (0, 1, 2, 4)]
             PAB = T.land[:, l0:l0 + 64, 0:2]
         else:
             LD, KN = n_("k0"), W("k0")
             act(KN, T.tw[:, 0:B1 + 1024].indirect(off[:, 0:4]), AF.Relu, RK1 + n_("offk") + ["c9", "num"], LD, bias=col(9), scale=4.0, c=1.5)
-        vg = VG[s]
+        vg = VG[2 * s + h]
         YR = []
         for e, a, b in (("v", 0, vg), ("a", vg, 64)):
             if b > a:
                 src = T.sts[:].indirect(cc[:, a:b])
                 if e == "v":
-                    cp(yy[:, 16 + 16 * a:16 + 16 * b], src, ["sts0", "sts1"] + n_("cc"), n_("yv"), 16 * (b - a), 1.5)
+                    cp(yy[:, 16 + 16 * a:16 + 16 * b], src, ["sts0", "sts1"] + n_("cc") + ["@g00"] * (h == 1 and s > 0), n_("yv"), 16 * (b - a), 1.5)
                 else:
                     act(yy[:, 16 + 16 * a:16 + 16 * b], src, AF.Copy, ["sts0", "sts1"] + n_("cc"), n_("ya"), 16 * (b - a), c=1.5)
         YR = n_("yv", "ya")
@@ -369,12 +373,12 @@ def build(g, T, topo, core, rank):
             tt(W("ra"), W("pm"), KN, AL.max, LD + n_("pm"), n_("ra"))
             mm(group(R(0), [("hI", PA), ("hI", PB_)]), LD, n_("r0"), bk)
             tt(W("mid"), KN, R(0), AL.max, LD + n_("r0"), n_("mid"), bank=[bk])
-            mm(group(R(1), [("I", W("ra")), ("BC", B("ci")), ("nI", W("mid"))]), n_("ra", "mid", "ci"), n_("r1"), bk)
-            act(W("hf"), R(1), AF.Identity, n_("r1"), n_("hf"), bias=-MIDO, bank=[bk])
-            MID, MR, hfl, hfr, HR, ab, eb = W("mid"), n_("mid"), "I", W("hf"), n_("hf"), SH, MIDO
+            mm(group(R(1), [("nI", W("ra")), ("nB", B("ci")), ("I", W("mid"))]), n_("ra", "mid", "ci"), n_("r1"), bk)
+            act(W("hf"), R(1), AF.Identity, n_("r1"), n_("hf"), bias=-MIDO, scale=-1.0, bank=[bk])
+            MID, MR, HR, ab, eb = W("mid"), n_("mid"), n_("hf"), SH, MIDO
         elif one:
             tt(W("mid"), PB_, KN, AL.max, LD, n_("mid"))
-            MID, MR, hfl, hfr, HR, ab, eb = W("mid"), n_("mid"), "nCI", B("ci"), n_("ci"), SH, BIG
+            MID, MR, HR, ab, eb = W("mid"), n_("mid"), [], SH, BIG
         else:
             MID, MR = KN, LD
         PR, PC, PB = xt[:, 0:64], x0[:, 0:64], x1[:, 0:64]
@@ -390,28 +394,29 @@ def build(g, T, topo, core, rank):
             if one:
                 act(dd[:, sv], px[:], AF.Abs, [xb], n_("d%d" % u), 512, bias=ab, bank=[xb])
                 ts(gd[:, sv], dd[:, sv], M8 - CC, M8, AL.add, AL.is_equal, n_("d%d" % u), n_("g%d" % u), 512, 0.5)
-                mm([(px[:], "I", dd[:, sv], True, False, 512)] + [(px[:, 64 * kk:64 * kk + 64], hfl, hfr, False, False, 64) for kk in range(8)],
+                mm([(px[:], "I", dd[:, sv], True, False, 512)] + [(px[:, 64 * kk:64 * kk + 64], "I", W("hf"), False, False, 64) for kk in range(8 * two)],
                    n_("d%d" % u) + HR, [xb], xb)
-                mm([(px[:], "nB", gd[:, sv], False, True, 512)], n_("g%d" % u) + [xb], [xb], xb)
+                mm([(px[:], "BC", gd[:, sv], False, True, 512)], n_("g%d" % u) + [xb], [xb], xb)
                 ts(em[:, sv], px[:], M8 + eb, M8, AL.add, AL.is_equal, [xb], EU, 512, bank=[xb])
             else:
                 ts(em[:, sv], px[:], M8 + C0, M8, AL.add, AL.is_equal, [xb], EU, 512, bank=[xb])
         for u in range(2):
             EU = n_("em%d" % u)
             ks = range(8 * u, 8 * u + 8)
-            first = [("nP2", B("ci"))] if one and u == 0 else []
+            first = ([("nP2", B("ci"))] + ([] if OPT["rmode"] else [("none", B("ci"))])) if one and u == 0 else []
             mm(group(PR, first + [(("bw%d" if one else "uu%d") % k, em[:, 64 * k:64 * k + 64]) for k in ks], 64, u == 0, u == 1),
                EU + (n_("ci") + ZZ if one else []) + [XT] * u, [XT], XT)
         if one:
-            if OPT["hi"] == "v":
+            if OPT["rmode"]:
                 ts(F("hi"), PR, M64, M64, AL.add, AL.subtract, [XT], n_("hi"), bank=[XT])
                 tt(F("y"), PR, F("hi"), AL.subtract, [XT] + n_("hi"), n_("cnt", "y"), bank=[XT])
-            else:
-                act(B("cnt"), PR, AF.Identity, [XT], n_("hi"), bias=12288.0, bank=[XT])
-                tt(F("y"), PR, B("cnt"), AL.subtract, [XT] + n_("hi"), n_("cnt", "y"), bank=[XT])
-            ts(B("ok"), PR, M64, M64, AL.add, AL.is_equal, [XT], n_("ok"), bank=[XT])
-            if OPT["rmode"]:
+                ts(B("ok"), PR, M64, M64, AL.add, AL.is_equal, [XT], n_("ok"), bank=[XT])
                 act(F("prs"), PR, AF.Relu, [XT], n_("prs"), bias=32.0, bank=[XT])
+                act(B("vp"), F("y"), AF.Exp, n_("cnt", "y"), n_("vp"), scale=math.log(32.0))
+            else:
+                act(B("vp"), PR, AF.Exp, [XT], n_("vp"), scale=math.log(32.0) / L, bank=[XT])
+                ts(F("hi"), PR, M64 * 16, M64 * 16, AL.add, AL.subtract, [XT], n_("hi"), bank=[XT])
+                tt(B("ok"), PR, F("hi"), AL.is_equal, [XT] + n_("hi"), n_("ok"), bank=[XT])
         else:
             ts(B("ok"), PR, 0.5, None, AL.is_gt, None, [XT], n_("ok"), bank=[XT])
         mm(group(R(2), [("T4", B("ok"))]), n_("ok"), n_("r2"), bk)
@@ -425,7 +430,8 @@ def build(g, T, topo, core, rank):
             mm(group(R(3), [("nLI", W("pm")), ("L2one", OHJ)]) + group(R(4), [("I", PB_), ("Lone", OHJ)]), LD + n_("pm", "ohj"), n_("r3", "r4"), bk)
             act(W("ljn", 2), R(3, 2), AF.Relu, n_("r3", "r4"), n_("ljn"), 128, bias=-L, bank=[bk])
             JN, JR, JB, JBR = ("I", W("ljn")), n_("ljn"), W("jb"), n_("ljn")
-            tt(W("f"), W("pm"), W("zj"), AL.min, n_("pm", "zj"), n_("f"))
+            act(W("mx"), W("pm"), AF.Identity, n_("pm"), n_("mx"), bias=-SH)
+            tt(W("f"), yy[:].indirect(offz[:, 0:4]), W("mx"), AL.min, YR + n_("offj", "ym", "mx"), n_("f"), c=1.8)
             if OPT["r"] == "v":
                 mm(group(R(5), [("I", NP), ("nhone", OHJ), ("eI", W("ljn")), ("one", W("f"))]), n_("ohj", "ljn", "f") + ["NP"], n_("r5"), bk)
                 ts(F("r"), R(5), M16, M16, AL.add, AL.subtract, n_("r5"), n_("r"), bank=[bk])
@@ -448,9 +454,16 @@ def build(g, T, topo, core, rank):
                 JB, JBR = out(0), [SN + "a"]
         WR = n_("win") if one else []
         if one:
-            act(B("vp"), F("y"), AF.Exp, n_("cnt", "y"), n_("vp"), scale=math.log(32.0), bias=0.0 if OPT["hi"] == "v" else 12288.0 * math.log(32.0))
-            mm(group(R(6), [("hugeone", B("ok")), ("Mw", B("vp"))]), n_("vp", "ok"), n_("r6"), bk)
-            ts(B("win"), R(6), 2.0, None, AL.is_gt, None, n_("r6"), n_("win"), bank=[bk])
+            if OPT["gate"]:
+                mm(group(R(6), [("Mw", B("vp"))]), n_("vp"), n_("r6"), bk)
+                ts(B("cnt"), R(6), 2.0, None, AL.is_gt, None, n_("r6"), n_("cnt"), bank=[bk])
+                mm(group(R(0), [("I", B("cnt")), ("none", OHJ)]), n_("cnt", "ohj"), n_("r0"), bk)
+                act(B("win"), R(0), AF.Relu, n_("r0"), n_("win"), bank=[bk])
+                W0, W0R = B("cnt"), n_("cnt")
+            else:
+                mm(group(R(6), [("hugeone", B("ok")), ("Mw", B("vp"))]), n_("vp", "ok"), n_("r6"), bk)
+                ts(B("win"), R(6), 2.0, None, AL.is_gt, None, n_("r6"), n_("win"), bank=[bk])
+                W0, W0R = B("win"), n_("win")
             if OPT["rmode"]:
                 mm(group(R(6), [("Q2", B("win"))]), n_("win"), n_("r6"), bk)
                 tt(F("y"), F("prs"), R(6), AL.mult, n_("prs", "r6"), n_("y"), bank=[bk])
@@ -461,7 +474,7 @@ def build(g, T, topo, core, rank):
                 for u in range(2):
                     mm(group(PC, [("bv%d" % k, em[:, 64 * k:64 * k + 64]) for k in range(8 * u, 8 * u + 8)], 64, u == 0, u == 1),
                        n_("em%d" % u) + [X0] * u, [X0], X0)
-                tt(B("bit"), B("win"), PC, AL.mult, n_("win") + [X0], n_("bit"), bank=[X0])
+                tt(B("bit"), W0, PC, AL.mult, W0R + [X0], n_("bit"), bank=[X0])
                 mm(group(R(6), [("Q2", B("bit"))]), n_("bit"), n_("r6"), bk)
             ts(B("oh"), R(6), M1, M1 + 1.0, AL.add, AL.is_equal, n_("r6"), n_("oh"), bank=[bk])
             mm(group(R(6), [("I", CMg), ("Kw", B("oh"))]), n_("oh") + ["CMg"], n_("r6"), bk)
@@ -479,12 +492,28 @@ def build(g, T, topo, core, rank):
                LD + n_("win"), [X0], X0)
             mm([(d0, "I", W("wz"), False, False, 64), (d1, "I", W("wz"), False, True, 64)], n_("wz") + [X0], [X0], X0)
             ts(W("s", 2), x0[:, 0:128], M8 + L + SH, M8, AL.add, AL.is_equal, [X0], n_("s"), 128, bank=[X0])
+        if last:
+            mm(group(R(4), [("I128", PA), ("I128", PB_)]), LD, n_("r4"), bk)
+            tt(W("rb"), W("ljn"), R(4), AL.min, n_("ljn", "r4"), n_("rb"), bank=[bk])
+            s0, s1 = wh[:, 64 * WH["s"]:64 * WH["s"] + 128:2], wh[:, 64 * WH["s"] + 1:64 * WH["s"] + 128:2]
+            n0, n1, n2 = xt[:, 0:64], xt[:, 64:128], xt[:, 128:192]
+            second = [("I", PB_), ("nI", JB), ("I", W("zj")), JN]
+            mm([(xt[:, 0:192], "I", T.bt[:, 0:192], True, False, 192)] + group(n0, [("I", PA), ("I", JB), JN], 64, False, False)
+               + group(n1, second + [("nI", W("rb"))], 64, False, False) + group(n2, second + [("I", W("rb"))], 64, False, False),
+               LD + n_("ljn", "zj", "rb") + ["e1", "e2"], [XT], XT)
+            mm(group(n0, [("Lone", s0)], 64, False, False) + group(n1, [("Lone", s1), ("nLone", s0)], 64, False, False)
+               + group(n2, [("Lone", s1), ("Lone", s0)], 64, False, True), n_("s") + [XT], [XT], XT)
+            ts(T["ob" + H][:], xt[:, 0:192], -L - SH, -1.0, AL.add, AL.max, [XT], n_("oy1"), 192, bank=[XT])
+        elif two:
             n0, n1 = xt[:, 0:128:2], xt[:, 1:128:2]
             mm([(xt[:, 0:128], "I", PAB, True, False, 128), (n0, "I", JB, False, False, 64), (n1, "nI", JB, False, False, 64),
                 (n1, "I", W("zj"), False, False, 64), (n0, "I", W("ljn"), False, False, 64), (n1, "I", W("ljn"), False, False, 64)],
                LD + n_("ljn", "zj"), [XT], XT)
             mm([(xt[:, 0:128], "Lone", W("s", 2), False, True, 128)], n_("s") + [XT], [XT], XT)
-            act(T.snd[:, sl:sl + 64, 0:2], xt[:, 0:128], AF.Relu, [XT], [SN + "a", SN + "b"], 128, bias=-L, bank=[XT])
+            if OPT["nout"][h] == "a":
+                act(T.snd[:, sl:sl + 64, 0:2], xt[:, 0:128], AF.Relu, [XT], [SN + "a", SN + "b"], 128, bias=-L, bank=[XT])
+            else:
+                ts(T.snd[:, sl:sl + 64, 0:2], xt[:, 0:128], -L, 0.0, AL.add, AL.max, [XT], [SN + "a", SN + "b"], 128, bank=[XT])
         elif one:
             mm(group(x0[:, 0:64], [("nI", PB_), ("nLI", B("win"))], 64, True, False), LD + n_("win"), [X0], X0)
             mm(group(x0[:, 0:64], [("I", W("wz"))], 64, False, True), n_("wz") + [X0], [X0], X0)
@@ -494,12 +523,12 @@ def build(g, T, topo, core, rank):
             act(out(1), xt[:, 0:64], AF.Relu, [XT], [SN + "b"], bias=-L, bank=[XT])
         kt, et, rd = [("I", W("kk")), ("I", W("dr"))], [("wI", CMe), ("one", W("de")), ("I", W("se"))], n_("kk")
         if two:
-            kt += [("CI", B("oq")), ("I", W("fq"))]
-            et += [("W62", B("oq")), ("qone", W("fq"))]
+            kt += [("C0I", B("oq")), ("I", W("fq"))]
+            et += [("W64", B("oq")), ("qone", W("fq"))]
             rd += n_("oq", "fq")
         at = [("I", CMa), ("neI", W("ljn")) if two else ("none", OHJ)] + ([("I", AO), ("none", B("win"))] if one else [])
-        mm(group(x1[:, 64:128], at), LD + WR + JR + ["CMa"], [X1], X1)
-        scan(out(4), T.rs[:, 0:64], x1[:, 64:128], AL.add, AL.max, [X1, "rs"], [SN + "n"], 64, bank=[X1])
+        mm(group(R(1), at), LD + WR + JR + ["CMa"], n_("r1"), bk)
+        scan(out(4), T.rs[:, 0:64], R(1), AL.add, AL.max, n_("r1") + ["rs"], [SN + "n"], 64, bank=[bk])
         if one:
             mm(group(x1[:, 0:64], et + [("W64", B("win"))], 64, True, False), rd + n_("win") + ["CMe"], [X1], X1)
             mm(group(x1[:, 0:64], [("qone", W("wz"))], 64, False, True), n_("wz") + [X1], [X1], X1)
@@ -512,39 +541,35 @@ def build(g, T, topo, core, rank):
         if last:
             o = slice(16 * b0, 16 * b0 + 64)
             ts(T.oyk[:, o], R(0), -C0, -1.0, AL.add, AL.max, n_("r0"), n_("oyk"), bank=[bk])
-            AB = [SN + "a", SN + "b"]
-            mm(group(R(1), [("I64", out(0))]), AB, n_("r1"), bk)
-            tt(W("y1"), out(1), R(1), AL.min, AB + n_("r1"), n_("y1"), bank=[bk])
-            mm(group(R(1), [("I", out(0)), ("I", out(1)), ("nI", W("y1"))]), AB + n_("y1"), n_("r1"), bk)
-            ts(T.oy0[:, o], R(1), -SH, -1.0, AL.add, AL.max, n_("r1"), n_("oy0"), bank=[bk])
-            ts(T.oy1[:, o], W("y1"), -SH, -1.0, AL.add, AL.max, n_("y1"), n_("oy1"))
+            ob = T["ob" + H]
+            tt(T.oy0[:, o], ob[:, 0:64], ob[:, 64:128], AL.max, n_("oy1"), n_("oy0"))
             act(T.oye[:, b0:b0 + 4], T.snd[:, sl + 15:sl + 64:16, 3], AF.Identity, [SN + "e"], n_("oye"), 4, bias=-L)
             act(T.oya[:, b0:b0 + 4], T.snd[:, sl + 15:sl + 64:16, 4], AF.Copy, [SN + "n"], n_("oya"), 4)
             for nm, q in (("yk", "s"), ("y0", "a"), ("y1", "s")):
-                dma(q, T[nm][:, o], T["o" + nm][:, o], "stored", n_("o" + nm), [], 2000.0)
+                dma(q, T[nm][:, o], ob[:, 128:192] if nm == "y1" else T["o" + nm][:, o], "stored", n_("o" + nm), [], 2000.0)
             return
-        if OPT["kout"] == "a":
+        if OPT["kout"][h] == "a":
             act(out(2), R(0), AF.Copy, n_("r0"), [SN + "k"], bank=[bk])
         else:
             cp(out(2), R(0), n_("r0"), [SN + "k"], bank=[bk])
         SR = [SN + x for x in "abken"]
-        blocks = [b for b in range(b0, b0 + 4) if b]
-        share = [len(eng) // 4] * 4 if len(blocks) == 4 else [len(eng) // 2, len(eng) // 4, len(eng) // 4]
+        calls = [[b for b in range(b0, b0 + 4) if b]]
         sem = "arr%d" % (2 * s + h)
-        trs, at = [], 0
-        for b, n in zip(blocks, share):
-            rid, pid = topo.addr(peers[b], core)
-            m = sum(1 << e for e in eng[at:at + n])
-            at += n
-            piece = slice(128 * s + 16 * b, 128 * s + 16 * b + 16)
-            trs.append(RemoteDMATransfer(dst_ids=[DstId(rid=rid, pnc=pid)], dma_engine_mask=m, remote_sem=T.sem[sem],
-                                         src=T.snd[:, piece, :], dst=T.land[:, piece, :]))
-        if h == 1:
-            at += 16
-            add("s", 60.0, lambda: Q.dma_start(T.land[:, 128 * s:128 * s + 16, :], T.snd[:, 128 * s:128 * s + 16, :]).then_inc(T.sem[sem], 16),
-                SR, ["stay%d" % s], own=("none", 0), lat=0.0)
-        add("g", CSEND, lambda: g.remote_dma_fused(trs, local_sem=T.sem.sent), SR + (["@stay%d" % s] if h == 1 else []),
-            ["land%d_%d" % (s, h)], own=(sem, -at), lat=CLAND)
+        if not b0:
+            act(T.land[:, 128 * s:128 * s + 16, :], T.snd[:, 128 * s:128 * s + 16, :], AF.Copy, SR, ["stay%d" % s], 80)
+        for c, blocks in enumerate(calls):
+            trs, n = [], len(eng) // 4
+            cut = [n * j for j in range(len(blocks))] + [len(eng)]
+            for j, b in enumerate(blocks):
+                rid, pid = topo.addr(peers[b], core)
+                piece = slice(128 * s + 16 * b, 128 * s + 16 * b + 16)
+                trs.append(RemoteDMATransfer(dst_ids=[DstId(rid=rid, pnc=pid)], dma_engine_mask=sum(1 << e for e in eng[cut[j]:cut[j + 1]]),
+                                             remote_sem=T.sem[sem], src=T.snd[:, piece, :], dst=T.land[:, piece, :]))
+            if c < len(calls) - 1:
+                add("g", CSEND / 2, lambda trs=trs: g.remote_dma_fused(trs, local_sem=T.sem.sent), SR, ["sent%d" % s], own=("none", 0), lat=0.0)
+            else:
+                add("g", CSEND / len(calls), lambda trs=trs: g.remote_dma_fused(trs, local_sem=T.sem.sent), SR + ["@sent%d" % s] * c,
+                    ["land%d_%d" % (s, h)], own=(sem, -len(eng) * len(calls)), lat=CLAND - 400.0 * c)
 
     for s in range(STEPS):
         head(s, 0)
@@ -641,11 +666,11 @@ def replay(ops, order, pred, scale, lat):
         e = ops[i][0]
         t = max([free.get(e, 0.0)] + [done[j] for j in pred[i] if not (e == "p" and ops[j][0] == "p")])
         free[e] = t + ops[i][1] * scale.get(e, 1.0)
-        done[i] = free[e] + ops[i][7] * lat
+        done[i] = free[e] + ops[i][7] * (lat if ops[i][6] is None else scale.get("dma", 1.0))
     return max(done.values()), done
 
 
-CASES = (({}, 1.0), ({"p": 1.2, "v": 1.1}, 1.2))
+CASES = (({"dma": 1.35}, 1.0), ({"dma": 1.05}, 1.8), ({"p": 1.45, "v": 1.45, "a": 1.45, "dma": 1.1}, 1.8))
 
 
 def place_all(ops, before, key, back):
@@ -715,53 +740,52 @@ def plan(ops):
         for j in before[i]:
             rev[j].add(i)
     rng = np.random.default_rng(SEED)
+
+    def fixed(order):
+        place = {x: j for j, x in enumerate(order)}
+        order, pred = ordered(ops, pred0, before, [place[i] for i in range(n)])
+        return [replay(ops, order, pred, a, b)[0] for a, b in CASES], order, pred
+
     best = None
     for j in range(TRIES):
         lead, slack = float(rng.choice([0.0, 2000.0, 4000.0, 7000.0, 10000.0])), float(rng.choice([40.0, 120.0, 250.0]))
         order, pred = schedule(ops, pred0, soft, lead, slack, float(rng.choice([0.0, 300.0, 800.0])), rng)
         cost = [replay(ops, order, pred, a, b)[0] for a, b in CASES]
         if best is None or sum(cost) < sum(best[0]):
-            best = (cost, order, pred, j)
+            best = (cost, order, pred)
     done = replay(ops, best[1], best[2], {}, 1.0)[1]
-    for j in range(TRIES):
-        jit = rng.random((2, n)) * 100.0
+    for j in range(TRIES + CLIMB):
+        if j >= TRIES:
+            done = replay(ops, best[1], best[2], {}, 1.0)[1]
+        jit = rng.random((2, n)) * (100.0 if j < TRIES else 400.0)
         done = place_all(ops, rev, [float(jit[0, i]) - done[i] for i in range(n)], True)[1]
         start, done = place_all(ops, before, [float(jit[1, i]) - done[i] for i in range(n)], False)
         order, pred = ordered(ops, pred0, before, start)
         cost = [replay(ops, order, pred, a, b)[0] for a, b in CASES]
         if sum(cost) < sum(best[0]):
-            best = (cost, order, pred, -j)
-    for j in range(CLIMB):
-        done = replay(ops, best[1], best[2], {}, 1.0)[1]
-        jit = rng.random(n) * float(rng.choice([150.0, 400.0, 900.0])) * (rng.random(n) < 0.3)
-        if j % 2:
-            done = place_all(ops, rev, [float(jit[i]) - done[i] for i in range(n)], True)[1]
-            key = [-x for x in done]
-        else:
-            key = [done[i] - ops[i][1] - ops[i][7] - float(jit[i]) for i in range(n)]
-        order, pred = ordered(ops, pred0, before, place_all(ops, before, key, False)[0])
-        cost = [replay(ops, order, pred, a, b)[0] for a, b in CASES]
-        if sum(cost) < sum(best[0]):
-            best = (cost, order, pred, 1000 + j)
-    order = tighten(ops, pred0, soft, best[1], rng)
-    place = {x: j for j, x in enumerate(order)}
-    order, pred = ordered(ops, pred0, before, [place[i] for i in range(n)])
-    return [replay(ops, order, pred, a, b)[0] for a, b in CASES], order, pred, 0
+            best = (cost, order, pred)
+    order, seen = best[1], []
+    for x in ROUNDS:
+        order = tighten(ops, pred0, soft, order, rng, x[0], x[1], x[2], CASES[slice(*x[3:])])
+        seen.append(round(fixed(order)[0][x[3]]))
+    return fixed(order) + (seen,)
 
 
-def tighten(ops, pred0, soft, order, rng, temp=120.0):
+def tighten(ops, pred0, soft, order, rng, rounds, temp, shared, cases):
     n = len(ops)
+    kind, shift, seen, first = list(range(n)), [0.0] * n, {}, {}
+    for i, o in enumerate(ops):
+        w = tuple(x[:3] + x[4:] if x[:3] == "snd" else x[:4] + x[5:] if x[:4] in ("land", "stay", "sent") else x for x in o[4])
+        seen[o[0], w, o[8]] = seen.get((o[0], w, o[8]), 0) + 1
+        if shared and o[8] >= 4:
+            kind[i], shift[i] = first.setdefault((o[0], w, o[8] % 2, seen[o[0], w, o[8]]), i), PERIOD * (o[8] // 2 - 3)
     names = sorted(set(o[0] for o in ops) | set(b for o in ops for b in o[5]))
     eng = [names.index(o[0]) for o in ops]
     banks = [[names.index(b) for b in o[5]] for o in ops]
     pe = names.index("p")
     before = [sorted(pred0[i] | soft[i]) for i in range(n)]
-    after = [[] for _ in range(n)]
-    for i in range(n):
-        for j in before[i]:
-            after[j].append(i)
     hard = [[j for j in pred0[i] if not (eng[i] == pe and eng[j] == pe)] for i in range(n)]
-    sets = [([o[1] * a.get(o[0], 1.0) for o in ops], [o[7] * b for o in ops]) for a, b in CASES]
+    sets = [([o[1] * a.get(o[0], 1.0) for o in ops], [o[7] * (b if o[6] is None else a.get("dma", 1.0)) for o in ops]) for a, b in cases]
 
     def run(order, cost, lat):
         free, last, done, why = [0.0] * len(names), [-1] * len(names), [0.0] * n, [-1] * n
@@ -780,36 +804,53 @@ def tighten(ops, pred0, soft, order, rng, temp=120.0):
             free[e], last[e], done[i], why[i] = t, i, t + lat[i], w
         return done, why
 
-    def value(order):
+    def value(key):
+        rank = [key[k] + x for k, x in zip(kind, shift)]
+        for i in range(n):
+            r = rank[i]
+            for j in before[i]:
+                if rank[j] > r:
+                    r = rank[j]
+            rank[i] = r + 1e-3
+        order = sorted(range(n), key=lambda x: rank[x])
         res = [run(order, c, l) for c, l in sets]
-        return sum(max(d) for d, w in res) / len(res), res
+        return sum(max(d) for d, w in res) / len(res), res, rank, order
 
-    now, res = value(order)
-    best, keep = now, order
-    for r in range(ROUNDS):
+    done = run(order, *sets[0])[0]
+    best, keep = sum(max(run(order, c, l)[0]) for c, l in sets) / len(sets), order
+    key = [0.0] * n
+    for i in sorted(range(n), key=lambda x: ops[x][8] // 2 == 3):
+        key[kind[i]] = done[i] - sets[0][0][i] - sets[0][1][i] - shift[i]
+    now, res, rank, order = value(key)
+    for r in range(rounds):
         done, why = res[int(rng.integers(len(res)))]
-        i = max(range(n), key=lambda x: done[x])
+        i = done.index(max(done))
         pairs = []
         while why[i] >= 0:
             if why[i] not in before[i]:
                 pairs.append((why[i], i))
             i = why[i]
         j, i = pairs[int(rng.integers(len(pairs)))]
-        a, b = order.index(j), order.index(i)
-        seg = order[a:b + 1]
-        ahead = rng.random() < 0.5
-        move = {i if ahead else j}
-        for x in (reversed(seg) if ahead else seg):
-            if any(y in move for y in (after[x] if ahead else before[x])):
-                move.add(x)
-        if i in move and j in move:
-            continue
-        trial = order[:a] + [x for x in seg if (x in move) == ahead] + [x for x in seg if (x in move) != ahead] + order[b + 1:]
-        v, rs = value(trial)
-        if v <= now or rng.random() < math.exp((now - v) / (temp * (1.0 - r / ROUNDS))):
-            order, now, res = trial, v, rs
+        new = list(key)
+        if rng.random() < 0.5:
+            t = rank[j] - 1.0 - 30.0 * float(rng.random())
+            todo, seen = [i], {i}
+            while todo:
+                x = todo.pop()
+                new[kind[x]] = min(new[kind[x]], t - shift[x])
+                for y in before[x]:
+                    if rank[y] > t and y not in seen:
+                        seen.add(y)
+                        todo.append(y)
+            if j in seen:
+                continue
+        else:
+            new[kind[j]] = rank[i] + 1.0 + 30.0 * float(rng.random()) - shift[j]
+        v, rs, rk, od = value(new)
+        if v <= now or rng.random() < math.exp((now - v) / (temp * (1.0 - r / rounds))):
+            key, now, res, rank = new, v, rs, rk
             if v < best:
-                best, keep = v, trial
+                best, keep = v, od
     return keep
 
 

import math
import numpy as np
from concourse.bass import DstId, RemoteDMATransfer
from concourse.mybir import AluOpType, AxisListType, ActivationFunctionType

AL = AluOpType
AF = ActivationFunctionType
STEPS = 6
SH = 8.0
C0 = 296.0
CC = C0 - SH
BIG = 264.0
MIDO = 792.0
L = 1024.0
M1, M8, M16, M64 = 1.5 * 2 ** 23, 1.5 * 2 ** 26, 1.5 * 2 ** 27, 1.5 * 2 ** 29
LOW = 30000.0
B1 = 1039
TWN = B1 + 5128
HB = 20480.0
VG = (32, 32) + (32, 16) * 5
ONA = ("I4", "I5", "I128", "wI", "hugeone", "L2one", "nhone", "NP", "CD", "nCI", "CI", "C0I", "nqI", "nLI", "eI", "neI", "nB", "qone",
       "W64", "W62", "Kw", "CMg", "hI", "jc", "jr", "z3", "z4") + tuple("rk%d" % r for r in range(16))
OPT = {"ci": "a", "kout": "aa", "nout": "aa", "gate": False, "rmode": True, "r": "v", "fq": "v"}
SEED, TRIES, CLIMB, PERIOD = 10, 4, 8, 16000.0
ROUNDS = ((1500, 120.0, False, 0, 1), (6000, 300.0, True, 0, 1), (20000, 140.0, True, 1, 3), (5000, 40.0, False, 1, 3))
FIX = {"v": (35.0, 50.0, 0.83, 80.0), "a": (70.0, 130.0, 0.83, 80.0), "p": (30.0, 40.0, 0.96, 120.0)}
CSEND, CLAND = 600.0, 2400.0

CB = ["I", "nI", "hI", "one", "T4", "Mw", "hugeone", "Kw", "nB", "BC", "nCI", "CI", "C0I", "Lone", "nLone", "L2one",
      "nLI", "nhone", "eI", "I4", "I5", "I128", "qone", "W64", "wI", "none", "neI", "nP2", "Q2", "LI"]
CH = ["W62", "Kw2"]
WB = ["ci", "ok", "vp", "win", "bit", "oh", "oq", "cnt"]
WH = {"k0": 0, "ra": 1, "rb": 2, "pm": 3, "mx": 4, "mid": 5, "hf": 6, "e1": 7, "er": 8, "zj": 9, "ljn": 10, "jb": 11, "f": 12, "fq": 13,
      "wz": 14, "s": 15, "kk": 17, "dr": 18, "de": 19, "se": 20, "y1": 21}
WF = {"sj": 0, "sg": 1, "r": 2, "prs": 3, "y": 4, "ry": 5, "hi": 6}

SCRATCH = {
    "sts": ("sbuf", [128, 4096], "bfloat16"), "ivs": ("sbuf", [128, 1024], "int32"), "e0s": ("sbuf", [128, 8], "int32"),
    "lw": ("sbuf", [128, 1024], "float32"), "tw": ("sbuf", [128, TWN], "float32"),
    "cf": ("sbuf", [128, 1536], "float32"), "ci": ("sbuf", [128, 64], "int32"), "col": ("sbuf", [128, 16], "float32"),
    "cb": ("sbuf", [128, len(CB) * 128], "bfloat16"), "ch": ("sbuf", [128, len(CH) * 128 + 160], "float16"),
    "bw": ("sbuf", [128, 2048], "bfloat16" if OPT["rmode"] else "float16"), "uu": ("sbuf", [128, 144], "bfloat16"),
    "bt": ("sbuf", [128, 384], "bfloat16"), "bv": ("sbuf", [128, 2048], "bfloat16"),
    "cm": ("sbuf", [128, 320], "bfloat16"), "rs": ("sbuf", [128, 128], "float32"),
    "snd": ("sbuf", [128, 6 * 128, 5], "float16"), "land": ("sbuf", [128, 5 * 128, 5], "float16"),
    "offw": ("sbuf", [128, 32], "uint16"), "ee": ("sbuf", [128, 256], "float16"), "hb": ("sbuf", [128, 8], "bfloat16"), "ohj": ("sbuf", [128, 128], "bfloat16"),
    "jf": ("sbuf", [128, 4 * 128], "float32"), "ji": ("sbuf", [128, 256], "int32"),
    "oyk": ("sbuf", [128, 128], "bfloat16"), "oy0": ("sbuf", [128, 128], "bfloat16"), "oy1": ("sbuf", [128, 128], "bfloat16"),
    "oye": ("sbuf", [128, 8], "float32"), "oya": ("sbuf", [128, 8], "float32"), "oyi": ("sbuf", [128, 512], "float32"),
}
for _h in range(2):
    SCRATCH["yy%d" % _h] = ("sbuf", [128, 1040], "bfloat16")
    SCRATCH["dd%d" % _h] = ("sbuf", [128, 1024], "float16")
    SCRATCH["gd%d" % _h] = ("sbuf", [128, 1024], "bfloat16")
    SCRATCH["em%d" % _h] = ("sbuf", [128, 1024], "bfloat16")
    SCRATCH["off%d" % _h] = ("sbuf", [128, 8], "uint16")
    SCRATCH["offz%d" % _h] = ("sbuf", [128, 8], "uint16")
    SCRATCH["ob%d" % _h] = ("sbuf", [128, 192], "bfloat16")
    SCRATCH["cc%d" % _h] = ("sbuf", [128, 64], "uint16")
    SCRATCH["wb%d" % _h] = ("sbuf", [128, len(WB) * 64], "bfloat16")
    SCRATCH["wh%d" % _h] = ("sbuf", [128, 22 * 64], "float16")
    SCRATCH["wf%d" % _h] = ("sbuf", [128, 7 * 64], "float32")
    for _n in ("px0", "px1", "ps", "pt"):
        SCRATCH[_n + str(_h)] = ("psum", [128, 512], "float32")

SEMAPHORES = ["sv", "sa", "sp", "sg", "sent", "le", "li", "ls0", "ls1", "stored"] + ["arr%d" % k for k in range(10)]
BLK0 = (0, 4)


def build(g, T, topo, core, rank):
    ops = []
    tag = [-1]
    V, S, P, Q = g.vector, g.scalar, g.tensor, g.sync

    def add(eng, cost, emit, rd, wr, bank=(), own=None, lat=60.0):
        if own is None and eng in FIX:
            cost, lat = FIX[eng][1] + FIX[eng][2] * (cost - FIX[eng][0]), FIX[eng][3]
        ops.append((eng, cost, emit, tuple(rd), tuple(wr), tuple(bank), own, lat, tag[0]))

    def vc(n, c):
        return 35.0 + max(64.0, n * c)

    def ts(out, in0, s1, s2, o0, o1, rd, wr, n=64, c=1.0, bank=()):
        if o1 is None:
            add("v", vc(n, c), lambda: V.tensor_scalar(out, in0, s1, None, o0), rd, wr, bank)
        else:
            add("v", vc(n, c), lambda: V.tensor_scalar(out, in0, s1, s2, o0, o1), rd, wr, bank)

    def tt(out, a, b, o, rd, wr, n=64, bank=(), c=None):
        add("v", vc(n, c or (1.0 if bank else 1.6)), lambda: V.tensor_tensor(out, a, b, o), rd, wr, bank)

    def cp(out, a, rd, wr, n=64, c=1.0, bank=()):
        add("v", vc(n, c), lambda: V.tensor_copy(out, a), rd, wr, bank)

    def fill(out, k, wr, n=64):
        add("v", vc(n, 0.5), lambda: V.memset(out, k), [], wr)

    def scan(out, d0, d1, o0, o1, rd, wr, n, bank=(), init=0.0):
        add("v", vc(n, 1.0), lambda: V.tensor_tensor_scan(out, d0, d1, init, o0, o1), rd, wr, bank)

    def act(out, a, f, rd, wr, n=64, bias=0.0, scale=1.0, c=1.0, bank=()):
        add("a", 70.0 + n * c, lambda: S.activation(out, a, f, bias=bias, scale=scale), rd, wr, bank)

    def C(n):
        if n in CH:
            j = CH.index(n)
            return T.ch[:, 128 * j:128 * j + 128]
        if n[:2] == "uu":
            k = int(n[2:])
            return T.uu[:, 15 - k:143 - k]
        if n[:2] in ("bw", "bv"):
            k = int(n[2:])
            return T[n[:2]][:, 128 * k:128 * k + 128]
        j = CB.index(n)
        return T.cb[:, 128 * j:128 * j + 128]

    def mm(lst, rd, wr, bank):
        def emit():
            last = None
            for o, l, r, a, b, n in lst:
                last = P.matmul(o, C(l), r, a, b)
            return last
        names = sorted(set(x[1][:2] if x[1][:2] in ("uu", "bw", "bv") else x[1] for x in lst))
        add("p", 30.0 + sum(0.5 * max(64, x[5]) for x in lst), emit, list(rd) + names, wr, [bank], lat=100.0)

    def group(out, terms, n=64, start=True, stop=True):
        return [(out, l, r, start and j == 0, stop and j == len(terms) - 1, n) for j, (l, r) in enumerate(terms)]

    def io(out, pat, base, cmul, wr, n, flt=True):
        if flt:
            add("g", 130.0 + 1.66 * n, lambda: g.iota(out, pat, base, cmul, allow_small_or_imprecise_dtypes=True), [], wr)
        else:
            add("g", 130.0 + 1.66 * n, lambda: g.iota(out, pat, base, cmul), [], wr)

    def dma(q, out, in_, sem, rd, wr, lat):
        e = {"s": Q, "a": S}[q]
        add(q, 60.0, lambda: e.dma_start(out, in_).then_inc(T.sem[sem], 16), rd, wr, own=(sem, 16), lat=lat)

    def lin(out, a, k, b, rd, wr, n=64, c=1.0):
        if wr[0] in ONA:
            act(out, a, AF.Identity, rd, wr, n, bias=b, scale=k)
        else:
            ts(out, a, k, b, AL.mult, AL.add, rd, wr, n, c)

    def col(j):
        return T.col[:, j:j + 1]

    dma("s", T.e0s[:], T.e0[:], "le", [], ["e0s"], 2000.0)
    dma("a", T.ivs[:], T.iv[:], "li", [], ["ivs"], 3200.0)
    dma("s", T.sts[:, 0:2048], T.st[:, 0:2048], "ls0", ["@e0s"], ["sts0"], 5000.0)
    dma("a", T.sts[:, 2048:4096], T.st[:, 2048:4096], "ls1", ["@ivs"], ["sts1"], 5500.0)

    mi, gi, ml, am = T.cf[:, 0:144], T.cf[:, 144:272], T.cf[:, 272:400], T.cf[:, 400:528]
    t1, t2, t3, t4, t5 = [T.cf[:, 528 + 128 * j:656 + 128 * j] for j in range(5)]
    dg, m16, t6, t7 = T.cf[:, 1168:1232], T.cf[:, 1232:1248], T.cf[:, 1248:1312], T.cf[:, 1312:1440]
    io(T.ci[:, 0:1], [[0, 1]], 0, 1, ["pint"], 1, False)
    io(mi, [[1, 144]], 0, 0, ["mi"], 144)
    io(gi, [[16, 8], [0, 16]], 0, 0, ["gi"], 128)
    io(ml, [[0, 8], [1, 16]], 0, 0, ["ml"], 128)
    io(T.tw[:, 0:B1], [[1, B1]], 0, 0, ["num"], B1)
    cp(col(0), T.ci[:, 0:1], ["pint"], ["c0"])
    for j, msk in ((1, 112), (2, 15)):
        ts(T.ci[:, j:j + 1], T.ci[:, 0:1], msk, None, AL.bitwise_and, None, ["pint"], ["ci%d" % j])
    cp(T.col[:, 1:3], T.ci[:, 1:3], ["ci1", "ci2"], ["c1"])
    ts(am, T.cf[:, 0:128], col(0), None, AL.subtract, None, ["mi", "c0"], ["am"], 128)
    ts(C("I"), am, 0.0, None, AL.is_equal, None, ["am"], ["I"], 128)
    ts(C("one"), gi, col(1), None, AL.is_equal, None, ["gi", "c1"], ["one"], 128)
    for src, lst in (("I", (("nI", -1.0), ("hI", 0.5), ("nCI", -CC), ("C0I", C0), ("nLI", -L), ("eI", 0.5 / L),
                            ("neI", -1.0 / L), ("I4", 4.0), ("I5", 5.0), ("I128", 128.0), ("wI", 17.0 / 16))),
                     ("one", (("nB", -BIG), ("Lone", L), ("nLone", -L), ("none", -1.0), ("qone", 0.25), ("hugeone", -2.0 ** 90),
                              ("L2one", 2 * L), ("nhone", -0.5)))):
        for n, k in lst:
            lin(C(n), C(src), k, 0.0, [src], [n], 128, 0.5)
    tt(C("BC"), C("nCI"), C("nB"), AL.add, ["nCI", "nB"], ["BC"], 128)
    ts(m16, T.cf[:, 0:16], col(2), None, AL.is_equal, None, ["mi", "c1"], ["m16"])
    ts(T.uu[:], mi, 15.0, col(1), AL.subtract, AL.is_equal, ["mi", "c1"], ["uu"], 144)
    LN2 = math.log(2.0)
    e1, e2, e3 = [T.bt[:, 128 * j:128 * j + 128] for j in range(3)]
    lin(col(5), col(2), -2 * LN2, 0.0, ["c1"], ["c5"], 1)
    act(e1, ml, AF.Exp, ["ml", "c5"], ["e1"], 128, bias=col(5), scale=2 * LN2)
    tt(C("T4"), e1, C("one"), AL.mult, ["e1", "one"], ["T4"], 128)
    wk, gm = T.cf[:, 1440:1456], T.cf[:, 1456:1464]
    if OPT["rmode"]:
        io(T.ji[:, 0:128], [[-1, 128]], 128, 1, ["vi"], 128, False)
        ts(T.ji[:, 128:256], T.ji[:, 0:128], 15, None, AL.bitwise_and, None, ["vi"], ["nv"], 128)
        cp(t1, T.ji[:, 128:256], ["nv"], ["t1"], 128)
        act(e2, t1, AF.Exp, ["t1"], ["e2"], 128, bias=6 * LN2, scale=LN2)
        act(e3, t1, AF.Exp, ["t1"], ["e3"], 128, bias=-7 * LN2, scale=-LN2)
        tt(C("Q2"), e3, C("one"), AL.mult, ["e3", "one"], ["Q2"], 128)
        tt(t2, e2, C("none"), AL.mult, ["e2", "none"], ["t2"], 128)
        tt(wk, T.bt[:, 128:144], m16, AL.add, ["e2", "m16"], ["wk"], 16)
    else:
        act(e3, ml, AF.Exp, ["ml"], ["e3"], 128, scale=2 * LN2)
        tt(C("Q2"), e3, C("one"), AL.mult, ["e3", "one"], ["Q2"], 128)
        lin(C("nP2"), C("I"), -16 * L, 0.0, ["I"], ["nP2"], 128, 0.5)
        lin(wk, m16, L, 1.0, ["m16"], ["wk"], 16)
        lin(T.bv[:, 0:128], C("I"), 1.0, 0.0, ["I"], ["bv"], 128, 0.5)
        for j in range(4):
            lin(T.bv[:, 128 << j:256 << j], T.bv[:, 0:128 << j], 4.0 ** -(1 << j), 0.0, ["bv"], ["bv"], 128 << j, 0.5)
    if OPT["rmode"]:
        lin(t3, C("I"), -16.0, 0.0, ["I"], ["t3"], 128)
        tt(C("nP2"), t2, t3, AL.add, ["t2", "t3"], ["nP2"], 128)
    ts(gm, T.cf[:, 144:272:16], col(1), None, AL.is_equal, None, ["gi", "c1"], ["gm"], 8)
    lin(T.bw[:, 0:128], C("I"), 1.0 if OPT["rmode"] else L, 0.0, ["I"], ["z0"], 128, 0.5)
    for j in range(4):
        lin(T.bw[:, 128 << j:256 << j], T.bw[:, 0:128 << j], 1.0, 0.0, ["z%d" % x for x in range(j + 1)], ["z%d" % (j + 1)], 128 << j, 0.5)
    for q in range(8):
        lin(T.bw[:, 16 * q:16 * q + 1936:129], wk, T.cf[:, 1456 + q:1457 + q], 0.0, ["wk", "gm"] + ["z%d" % x for x in range(5)], ["zz%d" % q], 16)
    ZZ = ["zz%d" % q for q in range(8)]
    ts(t4, am, 0.0, -93.0 / 64, AL.is_gt, AL.mult, ["am"], ["t4"], 128)
    act(t5, C("I"), AF.Identity, ["I"], ["t5"], 128, scale=67.0 / 64, bias=-3.0 / 64)
    tt(t7, t4, t5, AL.add, ["t4", "t5"], ["t7"], 128)
    tt(C("Mw"), t7, C("one"), AL.mult, ["t7", "one"], ["Mw"], 128)
    lin(col(8), col(2), 1.0, 1040.0, ["c1"], ["c8"], 1)
    lin(col(9), col(2), -256.0, C0 - 4 * L, ["c1"], ["c9"], 1)
    lin(col(10), col(2), -1.0, 0.5, ["c1"], ["c10"], 1)
    lin(col(11), col(2), -256.0, C0 - 3 * L, ["c1"], ["c11"], 1)
    lin(col(12), col(2), 64.0, 0.0, ["c1"], ["c12"], 1)
    for n, j in (("Kw", 2), ("W64", 12), ("Kw2", 8)):
        lin(C(n), C("one"), col(j), 0.0, ["one", "c1" if j == 2 else "c%d" % j], [n], 128, 0.5)
    ts(dg, T.cf[:, 272:336], col(2), None, AL.is_equal, None, ["ml", "c1"], ["dg"])
    CMg, CMj, CMa, NP = T.cm[:, 0:64], T.cm[:, 64:128], T.cm[:, 128:192], T.cm[:, 192:256]
    CMe, CD, JC = T.ch[:, 256:320], T.ch[:, 320:384], T.ch[:, 384:416]
    lin(t6, T.cf[:, 0:64], 16.0, LOW + 16.0, ["mi"], ["t6"])
    tt(t6, t6, dg, AL.mult, ["t6", "dg"], ["t6"])
    lin(CMg, t6, 1.0, -LOW, ["t6"], ["CMg"])
    lin(CMj, t6, 1.0, -LOW - 1040.0, ["t6"], ["CMj"])
    lin(CMa, dg, 65.0, -64.0, ["dg"], ["CMa"])
    lin(CMe, dg, LOW + 963.5, -LOW, ["dg"], ["CMe"])
    lin(NP, dg, 0.0, col(10), ["dg", "c10"], ["NP"])
    add("v", vc(128, 0.5), lambda: V.memset(T.bt[:, 0:128], 0.0), ["T4"], ["e1"])
    add("v", vc(64, 0.5), lambda: V.memset(T.bt[:, 128:192], -L), ["T4"], ["e2"])
    if OPT["r"] == "a":
        fill(T.cm[:, 256:320], HB, ["c20"])
    if OPT["fq"] == "a":
        lin(C("LI"), C("I"), L, 0.0, ["I"], ["LI"], 128, 0.5)
    lin(CD, dg, 0.0, col(11), ["dg", "c11"], ["CD"])
    ts(T.rs[:, 0:64], T.cf[:, 272:336], 0.0, -1.0e6, AL.is_equal, AL.mult, ["ml"], ["rs"])
    lin(T.rs[:, 64:128], T.cf[:, 272:336], 1.0e6, L, ["ml"], ["rs2"])
    lin(T.ch[:, 384:392], T.cf[:, 0:8], 16.0, col(2), ["mi", "c1"], ["icb"], 8)
    lin(T.ch[:, 392:408], T.cf[:, 0:16], 0.0, HB - L, ["mi"], ["jc"], 16)
    lin(T.ch[:, 408:416], T.cf[:, 0:8], 0.0, HB - 5 * L + 1 + B1, ["mi"], ["jr"], 8)
    lin(T.cf[:, 1472:1488], m16, L, 0.0, ["m16"], ["mL"], 16)
    RK1 = []
    for r in range(16):
        lin(T.tw[:, B1 + 64 * r:B1 + 64 * r + 64], T.tw[:, 64 * r:64 * r + 64], T.cf[:, 1232 + r:1233 + r], T.cf[:, 1472 + r:1473 + r],
            ["num", "m16", "mL"], ["rk%d" % r])
        RK1.append("rk%d" % r)
    RK5 = list(RK1)
    for j, (a, n) in enumerate(((1024, 1024), (2048, 1024), (3072, 1024), (4096, 1024), (5120, 8))):
        add("g", 170.0 + 1.66 * n, lambda a=a, n=n: g.affine_select(T.tw[:, B1 + a:B1 + a + n], T.tw[:, B1:B1 + n], [[0, n]], AL.is_gt, 0.0, 1, 0),
            RK1, ["rkw%d" % j])
        RK5.append("rkw%d" % j)
    act(T.snd[:, 0:128, 0], C("I"), AF.Copy, ["I"], ["snd0_0a", "snd0_1a"], 128, scale=0.0)
    for h in range(2):
        fill(T["yy%d" % h][:, 0:16], -SH, ["ym%d" % h])
    cp(T.lw[:], T.ivs[:], ["ivs"], ["lw"], 1024)

    ts(T.ci[:, 8:16], T.e0s[:], 896, None, AL.bitwise_and, None, ["e0s"], ["i8"])
    tt(T.ci[:, 16:24], T.ci[:, 8:16], T.ch[:, 384:392], AL.add, ["i8", "icb"], ["i16"], 8)
    ts(T.ci[:, 24:32], T.e0s[:], 5.0, 1.0, AL.mult, AL.add, ["e0s"], ["i24"])
    ts(T.ci[:, 32:40], T.ci[:, 24:32], 1023, None, AL.bitwise_and, None, ["i24"], ["i32"])
    cp(T.offw[:, 0:8], T.ci[:, 16:24], ["i16"], ["offd"])
    for j in (8, 16):
        cp(T.offw[:, j:j + 8], T.e0s[:], ["e0s"], ["offa" if j == 8 else "offc"])
    for h in range(2):
        b0, off = BLK0[h], T["off%d" % h]
        cp(off[:, 4:8], T.e0s[:, b0:b0 + 4], ["e0s"], ["offe%d" % h])
        ts(off[:, 0:4], T.e0s[:, b0:b0 + 4], float(B1), None, AL.add, None, ["e0s"], ["offk%d" % h])
    ts(T.offw[:, 24:32], T.ci[:, 32:40], float(B1), None, AL.add, None, ["i32"], ["offr"])

    peers = [T.cores[(rank + b) % len(T.cores)] for b in range(8)]
    eng = [e for e in topo.engines(core, peers[1]) if all(e in topo.engines(core, d) for d in peers[1:])]

    def head(s, h):
        tag[0] = 2 * s + h
        H = str(h)
        off = T["off" + H]
        if s > 0:
            l0 = 128 * (s - 1) + 16 * BLK0[h]
            LD = ["land%d_%d" % (s - 1, h)] + ([] if BLK0[h] else ["stay%d" % (s - 1)])
            e16, a16 = T.land[:, l0 + 15:l0 + 64:16, 3], T.land[:, l0 + 15:l0 + 64:16, 4]
            ts(off[:, 4:8], e16, -L, None, AL.add, None, LD, ["offe" + H], 4)
        src, sn = (T.lw, "lw") if s else (T.ivs, "ivs")
        cp(T["cc" + H][:], src[:].indirect(off[:, 4:8]), [sn, "offe" + H], ["cc" + H], 64, 2.0)

    def before_write(s):
        tag[0] = 2 * s + 1
        if s > 0:
            l0 = 128 * (s - 1)
            LD = ["land%d_0" % (s - 1), "land%d_1" % (s - 1), "stay%d" % (s - 1)]
            e16, a16 = T.land[:, l0 + 15:l0 + 128:16, 3], T.land[:, l0 + 15:l0 + 128:16, 4]
            act(T.hb[:], e16, AF.Identity, LD, ["hb"], 8, bias=HB - L - 63.75)
            ps = T.ps1
            mm([(ps[:, 456:488], "I", JC, True, False, 32), (ps[:, 456:464], "I", T.hb[:], False, False, 8), (ps[:, 464:472], "I", e16, False, False, 8),
                (ps[:, 464:472], "I", a16, False, False, 8), (ps[:, 472:480], "I", e16, False, False, 8),
                (ps[:, 480:488], "I5", e16, False, False, 8), (ps[:, 480:488], "I", a16, False, True, 8)], LD + ["hb", "icb", "jc", "jr"], ["rw"], "ps1")
            ts(T.offw[:], ps[:, 456:488], -HB, None, AL.add, None, ["rw"], ["offd", "offa", "offc", "offr"], 32, bank=["ps1"])
        tw, twr = (T.tw[:], RK5) if s else (T.tw[:, 0:B1 + 1024], RK1)
        act(T.ee[:], tw.indirect(T.offw[:, 16:32]), AF.Copy, twr + ["num", "offc", "offr"], ["ee"], 256, c=1.5)
        c37, old, dv = T.jf[:, 0:128], T.jf[:, 128:256], T.jf[:, 256:384]
        act(c37, T.lw[:].indirect(T.offw[:, 16:24]), AF.Copy, ["lw", "offc"], ["c37"], 128, scale=37.0, c=1.5)
        act(old, T.lw[:].indirect(T.offw[:, 0:8]), AF.Copy, ["lw", "offd"], ["old"], 128, c=1.5)
        tt(T.ji[:, 0:128], T.tw[:, 0:B1].indirect(T.offw[:, 8:16]), c37, AL.add, ["num", "c37", "offa"], ["vi"], 128, c=1.8)
        ts(T.ji[:, 128:256], T.ji[:, 0:128], 4095, None, AL.bitwise_and, None, ["vi"], ["nv"], 128)
        tt(dv, T.ji[:, 128:256], old, AL.subtract, ["nv", "old"], ["dv"], 128)

    def write(s):
        tag[0] = 2 * s + 1
        tt(T.jf[:, 384:512], T.ohj[:], T.jf[:, 256:384], AL.mult, ["ohj0", "ohj1", "dv"], ["t"], 128)
        add("v", vc(128, 4.0), lambda: V.tensor_tensor(T.lw[:].indirect(T.offw[:, 0:8]), T.jf[:, 384:512], T.jf[:, 128:256], AL.add),
            ["t", "old", "offd"], ["lw"])

    def body(s, h):
        tag[0] = 2 * s + h
        H = str(h)
        b0 = BLK0[h]
        off, offz, ps, bk = T["off" + H], T["offz" + H], T["ps" + H], "ps" + H
        yy, dd, gd, em, cc = T["yy" + H], T["dd" + H], T["gd" + H], T["em" + H], T["cc" + H]
        wb, wh, wf = T["wb" + H], T["wh" + H], T["wf" + H]
        X0, X1, XT = "px0" + H, "px1" + H, "pt" + H
        x0, x1, xt = T[X0], T[X1], T[XT]
        last, one, two = s == STEPS - 1, s >= 1, s >= 2
        sl = 128 * s + 16 * b0
        SN = "snd%d_%d" % (s, h)
        OHJ = T.ohj[:, 16 * b0:16 * b0 + 64]

        def B(n):
            j = WB.index(n)
            return wb[:, 64 * j:64 * j + 64]

        def W(n, w=1):
            return wh[:, 64 * WH[n]:64 * (WH[n] + w)]

        def F(n):
            return wf[:, 64 * WF[n]:64 * WF[n] + 64]

        def R(j, w=1):
            return ps[:, 64 * j:64 * (j + w)]

        def out(q):
            return T.snd[:, sl:sl + 64, q]

        def n_(*a):
            return [x + H for x in a]

        ER, E1 = T.ee[:, 16 * b0:16 * b0 + 64], T.ee[:, 128 + 16 * b0:192 + 16 * b0]
        if s > 0:
            l0 = 128 * (s - 1) + 16 * b0
            LD = ["land%d_%d" % (s - 1, h)] + ([] if b0 else ["stay%d" % (s - 1)])
            PA, PB_, KN, AO = [T.land[:, l0:l0 + 64, j] for j in (0, 1, 2, 4)]
            PAB = T.land[:, l0:l0 + 64, 0:2]
        else:
            LD, KN = n_("k0"), W("k0")
            act(KN, T.tw[:, 0:B1 + 1024].indirect(off[:, 0:4]), AF.Relu, RK1 + n_("offk") + ["c9", "num"], LD, bias=col(9), scale=4.0, c=1.5)
        vg = VG[2 * s + h]
        YR = []
        for e, a, b in (("v", 0, vg), ("a", vg, 64)):
            if b > a:
                src = T.sts[:].indirect(cc[:, a:b])
                if e == "v":
                    cp(yy[:, 16 + 16 * a:16 + 16 * b], src, ["sts0", "sts1"] + n_("cc") + ["@g00"] * (h == 1 and s > 0), n_("yv"), 16 * (b - a), 1.5)
                else:
                    act(yy[:, 16 + 16 * a:16 + 16 * b], src, AF.Copy, ["sts0", "sts1"] + n_("cc"), n_("ya"), 16 * (b - a), c=1.5)
        YR = n_("yv", "ya")
        if one:
            if OPT["ci"] == "v":
                ts(B("ci"), KN, 0.5, None, AL.is_gt, None, LD, n_("ci"))
            else:
                act(B("ci"), KN, AF.Sign, LD, n_("ci"))
        if two:
            tt(W("pm"), PA, PB_, AL.min, LD, n_("pm"))
            tt(W("ra"), W("pm"), KN, AL.max, LD + n_("pm"), n_("ra"))
            mm(group(R(0), [("hI", PA), ("hI", PB_)]), LD, n_("r0"), bk)
            tt(W("mid"), KN, R(0), AL.max, LD + n_("r0"), n_("mid"), bank=[bk])
            mm(group(R(1), [("nI", W("ra")), ("nB", B("ci")), ("I", W("mid"))]), n_("ra", "mid", "ci"), n_("r1"), bk)
            act(W("hf"), R(1), AF.Identity, n_("r1"), n_("hf"), bias=-MIDO, scale=-1.0, bank=[bk])
            MID, MR, HR, ab, eb = W("mid"), n_("mid"), n_("hf"), SH, MIDO
        elif one:
            tt(W("mid"), PB_, KN, AL.max, LD, n_("mid"))
            MID, MR, HR, ab, eb = W("mid"), n_("mid"), [], SH, BIG
        else:
            MID, MR = KN, LD
        PR, PC, PB = xt[:, 0:64], x0[:, 0:64], x1[:, 0:64]
        for u in range(2):
            xb = (X0, X1)[u]
            px = T[xb]
            lst = []
            for kk in range(8):
                lst += group(px[:, 64 * kk:64 * kk + 64], [("nI", MID), ("I", yy[:, 16 + 8 * u + kk:1040:16])])
            mm(lst, YR + MR, [xb], xb)
            sv = slice(512 * u, 512 * u + 512)
            EU = n_("em%d" % u)
            if one:
                act(dd[:, sv], px[:], AF.Abs, [xb], n_("d%d" % u), 512, bias=ab, bank=[xb])
                ts(gd[:, sv], dd[:, sv], M8 - CC, M8, AL.add, AL.is_equal, n_("d%d" % u), n_("g%d" % u), 512, 0.5)
                mm([(px[:], "I", dd[:, sv], True, False, 512)] + [(px[:, 64 * kk:64 * kk + 64], "I", W("hf"), False, False, 64) for kk in range(8 * two)],
                   n_("d%d" % u) + HR, [xb], xb)
                mm([(px[:], "BC", gd[:, sv], False, True, 512)], n_("g%d" % u) + [xb], [xb], xb)
                ts(em[:, sv], px[:], M8 + eb, M8, AL.add, AL.is_equal, [xb], EU, 512, bank=[xb])
            else:
                ts(em[:, sv], px[:], M8 + C0, M8, AL.add, AL.is_equal, [xb], EU, 512, bank=[xb])
        for u in range(2):
            EU = n_("em%d" % u)
            ks = range(8 * u, 8 * u + 8)
            first = ([("nP2", B("ci"))] + ([] if OPT["rmode"] else [("none", B("ci"))])) if one and u == 0 else []
            mm(group(PR, first + [(("bw%d" if one else "uu%d") % k, em[:, 64 * k:64 * k + 64]) for k in ks], 64, u == 0, u == 1),
               EU + (n_("ci") + ZZ if one else []) + [XT] * u, [XT], XT)
        if one:
            if OPT["rmode"]:
                ts(F("hi"), PR, M64, M64, AL.add, AL.subtract, [XT], n_("hi"), bank=[XT])
                tt(F("y"), PR, F("hi"), AL.subtract, [XT] + n_("hi"), n_("cnt", "y"), bank=[XT])
                ts(B("ok"), PR, M64, M64, AL.add, AL.is_equal, [XT], n_("ok"), bank=[XT])
                act(F("prs"), PR, AF.Relu, [XT], n_("prs"), bias=32.0, bank=[XT])
                act(B("vp"), F("y"), AF.Exp, n_("cnt", "y"), n_("vp"), scale=math.log(32.0))
            else:
                act(B("vp"), PR, AF.Exp, [XT], n_("vp"), scale=math.log(32.0) / L, bank=[XT])
                ts(F("hi"), PR, M64 * 16, M64 * 16, AL.add, AL.subtract, [XT], n_("hi"), bank=[XT])
                tt(B("ok"), PR, F("hi"), AL.is_equal, [XT] + n_("hi"), n_("ok"), bank=[XT])
        else:
            ts(B("ok"), PR, 0.5, None, AL.is_gt, None, [XT], n_("ok"), bank=[XT])
        mm(group(R(2), [("T4", B("ok"))]), n_("ok"), n_("r2"), bk)
        ts(OHJ, R(2), M1, M1 + 1.0, AL.add, AL.is_equal, n_("r2"), n_("ohj"), bank=[bk])
        mm(group(R(2), [("I", CMj), ("Kw2", OHJ)]), n_("ohj") + ["CMj"], n_("r2"), bk)
        scan(F("sj"), T.rs[:, 0:64], R(2), AL.add, AL.max, n_("r2") + ["rs"], n_("sj"), 64, bank=[bk])
        cp(offz[:, 0:4], wf[:, 64 * WF["sj"] + 15:64 * WF["sj"] + 64:16], n_("sj"), n_("offj"), 4)
        act(W("zj") if one else out(1), yy[:].indirect(offz[:, 0:4]), AF.Identity, YR + n_("offj", "ym"), n_("zj") if one else [SN + "b"],
            bias=SH, c=1.5)
        if two:
            mm(group(R(3), [("nLI", W("pm")), ("L2one", OHJ)]) + group(R(4), [("I", PB_), ("Lone", OHJ)]), LD + n_("pm", "ohj"), n_("r3", "r4"), bk)
            act(W("ljn", 2), R(3, 2), AF.Relu, n_("r3", "r4"), n_("ljn"), 128, bias=-L, bank=[bk])
            JN, JR, JB, JBR = ("I", W("ljn")), n_("ljn"), W("jb"), n_("ljn")
            act(W("mx"), W("pm"), AF.Identity, n_("pm"), n_("mx"), bias=-SH)
            tt(W("f"), yy[:].indirect(offz[:, 0:4]), W("mx"), AL.min, YR + n_("offj", "ym", "mx"), n_("f"), c=1.8)
            if OPT["r"] == "v":
                mm(group(R(5), [("I", NP), ("nhone", OHJ), ("eI", W("ljn")), ("one", W("f"))]), n_("ohj", "ljn", "f") + ["NP"], n_("r5"), bk)
                ts(F("r"), R(5), M16, M16, AL.add, AL.subtract, n_("r5"), n_("r"), bank=[bk])
                tt(B("oq"), F("r"), R(5), AL.is_equal, n_("r", "r5"), n_("oq"), bank=[bk])
            else:
                mm(group(R(5), [("I", NP), ("I", T.cm[:, 256:320]), ("nhone", OHJ), ("eI", W("ljn")), ("one", W("f"))]),
                   n_("ohj", "ljn", "f") + ["NP", "c20"], n_("r5"), bk)
                act(W("rb"), R(5), AF.Copy, n_("r5"), n_("r"), bank=[bk])
                tt(B("oq"), W("rb"), R(5), AL.is_equal, n_("r", "r5"), n_("oq"), bank=[bk])
            if OPT["fq"] == "v":
                tt(W("fq"), B("oq"), W("f"), AL.mult, n_("oq", "f"), n_("fq"))
            else:
                mm(group(R(5), [("I", W("f")), ("LI", B("oq"))]), n_("oq", "f"), n_("r5"), bk)
                act(W("fq"), R(5), AF.Relu, n_("r5"), n_("fq"), bias=-L, bank=[bk])
        else:
            JN, JR = ("Lone", OHJ), n_("ohj")
            if one:
                mm(group(R(4), [("I", PB_), ("Lone", OHJ)]), LD + n_("ohj"), n_("r4"), bk)
                act(out(0), R(4), AF.Relu, n_("r4"), [SN + "a"], bias=-L, bank=[bk])
                JB, JBR = out(0), [SN + "a"]
        WR = n_("win") if one else []
        if one:
            if OPT["gate"]:
                mm(group(R(6), [("Mw", B("vp"))]), n_("vp"), n_("r6"), bk)
                ts(B("cnt"), R(6), 2.0, None, AL.is_gt, None, n_("r6"), n_("cnt"), bank=[bk])
                mm(group(R(0), [("I", B("cnt")), ("none", OHJ)]), n_("cnt", "ohj"), n_("r0"), bk)
                act(B("win"), R(0), AF.Relu, n_("r0"), n_("win"), bank=[bk])
                W0, W0R = B("cnt"), n_("cnt")
            else:
                mm(group(R(6), [("hugeone", B("ok")), ("Mw", B("vp"))]), n_("vp", "ok"), n_("r6"), bk)
                ts(B("win"), R(6), 2.0, None, AL.is_gt, None, n_("r6"), n_("win"), bank=[bk])
                W0, W0R = B("win"), n_("win")
            if OPT["rmode"]:
                mm(group(R(6), [("Q2", B("win"))]), n_("win"), n_("r6"), bk)
                tt(F("y"), F("prs"), R(6), AL.mult, n_("prs", "r6"), n_("y"), bank=[bk])
                ts(F("ry"), F("y"), M1, M1, AL.add, AL.subtract, n_("y"), n_("ry"))
                tt(B("bit"), F("ry"), F("y"), AL.is_gt, n_("ry", "y"), n_("bit"))
                mm(group(R(6), [("T4", B("bit"))]), n_("bit"), n_("r6"), bk)
            else:
                for u in range(2):
                    mm(group(PC, [("bv%d" % k, em[:, 64 * k:64 * k + 64]) for k in range(8 * u, 8 * u + 8)], 64, u == 0, u == 1),
                       n_("em%d" % u) + [X0] * u, [X0], X0)
                tt(B("bit"), W0, PC, AL.mult, W0R + [X0], n_("bit"), bank=[X0])
                mm(group(R(6), [("Q2", B("bit"))]), n_("bit"), n_("r6"), bk)
            ts(B("oh"), R(6), M1, M1 + 1.0, AL.add, AL.is_equal, n_("r6"), n_("oh"), bank=[bk])
            mm(group(R(6), [("I", CMg), ("Kw", B("oh"))]), n_("oh") + ["CMg"], n_("r6"), bk)
            scan(F("sg"), T.rs[:, 0:64], R(6), AL.add, AL.max, n_("r6") + ["rs"], n_("sg"), 64, bank=[bk])
            cp(offz[:, 4:8], wf[:, 64 * WF["sg"] + 15:64 * WF["sg"] + 64:16], n_("sg"), n_("offg"), 4)
            tt(W("wz"), yy[:].indirect(offz[:, 4:8]), B("win"), AL.mult, YR + n_("offg", "ym", "win"), n_("wz"), c=1.8)
        alive = [("nLone", OHJ)] + ([("nLone", B("win"))] if one else [])
        mm(group(x1[:, 0:64], [("I", KN), JN] + ([("Lone", B("win"))] if one else [])) + group(x1[:, 64:128], [("I", CD), ("I4", E1)] + alive)
           + group(x1[:, 128:192], [("I", E1)] + alive) + group(x1[:, 192:256], [("I", ER), JN]),
           LD + WR + JR + n_("ohj") + ["CD", "ee"], [X1], X1)
        act(W("kk", 4), x1[:, 0:256], AF.Relu, [X1], n_("kk"), 256, bias=-L, bank=[X1])
        if two:
            d0, d1 = x0[:, 0:128:2], x0[:, 1:128:2]
            mm([(x0[:, 0:128], "nI", PAB, True, False, 128), (d0, "nLI", B("win"), False, False, 64), (d1, "nLI", B("win"), False, False, 64)],
               LD + n_("win"), [X0], X0)
            mm([(d0, "I", W("wz"), False, False, 64), (d1, "I", W("wz"), False, True, 64)], n_("wz") + [X0], [X0], X0)
            ts(W("s", 2), x0[:, 0:128], M8 + L + SH, M8, AL.add, AL.is_equal, [X0], n_("s"), 128, bank=[X0])
        if last:
            mm(group(R(4), [("I128", PA), ("I128", PB_)]), LD, n_("r4"), bk)
            tt(W("rb"), W("ljn"), R(4), AL.min, n_("ljn", "r4"), n_("rb"), bank=[bk])
            s0, s1 = wh[:, 64 * WH["s"]:64 * WH["s"] + 128:2], wh[:, 64 * WH["s"] + 1:64 * WH["s"] + 128:2]
            n0, n1, n2 = xt[:, 0:64], xt[:, 64:128], xt[:, 128:192]
            second = [("I", PB_), ("nI", JB), ("I", W("zj")), JN]
            mm([(xt[:, 0:192], "I", T.bt[:, 0:192], True, False, 192)] + group(n0, [("I", PA), ("I", JB), JN], 64, False, False)
               + group(n1, second + [("nI", W("rb"))], 64, False, False) + group(n2, second + [("I", W("rb"))], 64, False, False),
               LD + n_("ljn", "zj", "rb") + ["e1", "e2"], [XT], XT)
            mm(group(n0, [("Lone", s0)], 64, False, False) + group(n1, [("Lone", s1), ("nLone", s0)], 64, False, False)
               + group(n2, [("Lone", s1), ("Lone", s0)], 64, False, True), n_("s") + [XT], [XT], XT)
            ts(T["ob" + H][:], xt[:, 0:192], -L - SH, -1.0, AL.add, AL.max, [XT], n_("oy1"), 192, bank=[XT])
        elif two:
            n0, n1 = xt[:, 0:128:2], xt[:, 1:128:2]
            mm([(xt[:, 0:128], "I", PAB, True, False, 128), (n0, "I", JB, False, False, 64), (n1, "nI", JB, False, False, 64),
                (n1, "I", W("zj"), False, False, 64), (n0, "I", W("ljn"), False, False, 64), (n1, "I", W("ljn"), False, False, 64)],
               LD + n_("ljn", "zj"), [XT], XT)
            mm([(xt[:, 0:128], "Lone", W("s", 2), False, True, 128)], n_("s") + [XT], [XT], XT)
            if OPT["nout"][h] == "a":
                act(T.snd[:, sl:sl + 64, 0:2], xt[:, 0:128], AF.Relu, [XT], [SN + "a", SN + "b"], 128, bias=-L, bank=[XT])
            else:
                ts(T.snd[:, sl:sl + 64, 0:2], xt[:, 0:128], -L, 0.0, AL.add, AL.max, [XT], [SN + "a", SN + "b"], 128, bank=[XT])
        elif one:
            mm(group(x0[:, 0:64], [("nI", PB_), ("nLI", B("win"))], 64, True, False), LD + n_("win"), [X0], X0)
            mm(group(x0[:, 0:64], [("I", W("wz"))], 64, False, True), n_("wz") + [X0], [X0], X0)
            ts(W("s"), x0[:, 0:64], M8 + L + SH, M8, AL.add, AL.is_equal, [X0], n_("s"), bank=[X0])
            mm(group(xt[:, 0:64], [("I", PB_), ("nI", JB), ("I", W("zj")), JN], 64, True, False), LD + JBR + JR + n_("zj"), [XT], XT)
            mm(group(xt[:, 0:64], [("Lone", W("s"))], 64, False, True), n_("s") + [XT], [XT], XT)
            act(out(1), xt[:, 0:64], AF.Relu, [XT], [SN + "b"], bias=-L, bank=[XT])
        kt, et, rd = [("I", W("kk")), ("I", W("dr"))], [("wI", CMe), ("one", W("de")), ("I", W("se"))], n_("kk")
        if two:
            kt += [("C0I", B("oq")), ("I", W("fq"))]
            et += [("W64", B("oq")), ("qone", W("fq"))]
            rd += n_("oq", "fq")
        at = [("I", CMa), ("neI", W("ljn")) if two else ("none", OHJ)] + ([("I", AO), ("none", B("win"))] if one else [])
        mm(group(R(1), at), LD + WR + JR + ["CMa"], n_("r1"), bk)
        scan(out(4), T.rs[:, 0:64], R(1), AL.add, AL.max, n_("r1") + ["rs"], [SN + "n"], 64, bank=[bk])
        if one:
            mm(group(x1[:, 0:64], et + [("W64", B("win"))], 64, True, False), rd + n_("win") + ["CMe"], [X1], X1)
            mm(group(x1[:, 0:64], [("qone", W("wz"))], 64, False, True), n_("wz") + [X1], [X1], X1)
            kt += [("C0I", B("win")), ("I", W("wz"))]
            rd += n_("win", "wz")
        else:
            mm(group(x1[:, 0:64], et), rd + ["CMe"], [X1], X1)
        scan(out(3), T.rs[:, 64:128], x1[:, 0:64], AL.min, AL.max, [X1, "rs2"], [SN + "e"], 64, bank=[X1], init=L)
        mm(group(R(0), kt), rd, n_("r0"), bk)
        if last:
            o = slice(16 * b0, 16 * b0 + 64)
            ts(T.oyk[:, o], R(0), -C0, -1.0, AL.add, AL.max, n_("r0"), n_("oyk"), bank=[bk])
            ob = T["ob" + H]
            tt(T.oy0[:, o], ob[:, 0:64], ob[:, 64:128], AL.max, n_("oy1"), n_("oy0"))
            act(T.oye[:, b0:b0 + 4], T.snd[:, sl + 15:sl + 64:16, 3], AF.Identity, [SN + "e"], n_("oye"), 4, bias=-L)
            act(T.oya[:, b0:b0 + 4], T.snd[:, sl + 15:sl + 64:16, 4], AF.Copy, [SN + "n"], n_("oya"), 4)
            for nm, q in (("yk", "s"), ("y0", "a"), ("y1", "s")):
                dma(q, T[nm][:, o], ob[:, 128:192] if nm == "y1" else T["o" + nm][:, o], "stored", n_("o" + nm), [], 2000.0)
            return
        if OPT["kout"][h] == "a":
            act(out(2), R(0), AF.Copy, n_("r0"), [SN + "k"], bank=[bk])
        else:
            cp(out(2), R(0), n_("r0"), [SN + "k"], bank=[bk])
        SR = [SN + x for x in "abken"]
        calls = [[b for b in range(b0, b0 + 4) if b]]
        sem = "arr%d" % (2 * s + h)
        if not b0:
            act(T.land[:, 128 * s:128 * s + 16, :], T.snd[:, 128 * s:128 * s + 16, :], AF.Copy, SR, ["stay%d" % s], 80)
        for c, blocks in enumerate(calls):
            trs, n = [], len(eng) // 4
            cut = [n * j for j in range(len(blocks))] + [len(eng)]
            for j, b in enumerate(blocks):
                rid, pid = topo.addr(peers[b], core)
                piece = slice(128 * s + 16 * b, 128 * s + 16 * b + 16)
                trs.append(RemoteDMATransfer(dst_ids=[DstId(rid=rid, pnc=pid)], dma_engine_mask=sum(1 << e for e in eng[cut[j]:cut[j + 1]]),
                                             remote_sem=T.sem[sem], src=T.snd[:, piece, :], dst=T.land[:, piece, :]))
            if c < len(calls) - 1:
                add("g", CSEND / 2, lambda trs=trs: g.remote_dma_fused(trs, local_sem=T.sem.sent), SR, ["sent%d" % s], own=("none", 0), lat=0.0)
            else:
                add("g", CSEND / len(calls), lambda trs=trs: g.remote_dma_fused(trs, local_sem=T.sem.sent), SR + ["@sent%d" % s] * c,
                    ["land%d_%d" % (s, h)], own=(sem, -len(eng) * len(calls)), lat=CLAND - 400.0 * c)

    for s in range(STEPS):
        head(s, 0)
        head(s, 1)
        before_write(s)
        body(s, 0)
        body(s, 1)
        write(s)
    for u in range(2):
        xb = "px%d0" % u
        pz = T[xb]
        act(pz[:, 0:256], T.lw[:, 512 + 256 * u:768 + 256 * u], AF.Copy, ["lw"], [xb], 256, scale=4096.0, bank=[xb])
        tt(T.oyi[:, 256 * u:256 * u + 256], T.lw[:, 256 * u:256 * u + 256], pz[:, 0:256], AL.add, ["lw", xb], ["oyi%d" % u], 256, bank=[xb])
        dma("s", T.yi[:, 256 * u:256 * u + 256], T.oyi[:, 256 * u:256 * u + 256], "stored", ["oyi%d" % u], [], 2600.0)
    dma("s", T.ye[:], T.oye[:], "stored", ["oye0", "oye1"], [], 2000.0)
    dma("a", T.ya[:], T.oya[:], "stored", ["oya0", "oya1"], [], 2000.0)
    return ops, len(eng)


def depends(ops):
    n = len(ops)
    pred = [set() for _ in range(n)]
    soft = [set() for _ in range(n)]
    lw, rd = {}, {}
    for i, o in enumerate(ops):
        for r in o[3]:
            if r[0] == "@":
                soft[i].add(lw[r[1:]])
            elif r in lw:
                pred[i].add(lw[r])
        for w in o[4]:
            if w in lw:
                pred[i].add(lw[w])
            pred[i].update(rd.get(w, ()))
        for r in o[3]:
            rd.setdefault(r, []).append(i)
        for w in o[4]:
            lw[w] = i
            rd[w] = []
        pred[i].discard(i)
    return pred, soft


def schedule(ops, pred0, soft, lead, slack, noise, rng):
    n = len(ops)
    pred = [set(x) for x in pred0]
    succ = [[] for _ in range(n)]
    left = [0] * n
    for i in range(n):
        for j in pred[i] | soft[i]:
            succ[j].append(i)
            left[i] += 1
    prio = [0.0] * n
    for i in range(n - 1, -1, -1):
        prio[i] = ops[i][1] + ops[i][7] + max([prio[j] for j in succ[i]], default=0.0)
    jit = rng.random(n)
    key = [prio[i] - lead * (ops[i][8] % 2 if ops[i][8] >= 0 else 0) + noise * float(jit[i]) for i in range(n)]
    free, done, bankl, base = {}, [0.0] * n, {}, [0.0] * n
    ready = [i for i in range(n) if left[i] == 0]
    order = []

    def start(i):
        t = max(free.get(ops[i][0], 0.0), base[i])
        for b in ops[i][5]:
            j = bankl.get(b)
            if j is not None and ops[j][0] != ops[i][0]:
                t = max(t, done[j])
        return t
    while ready:
        st = [(start(i), i) for i in ready]
        t0, i0 = min(st)
        i = max([i for t, i in st if ops[i][0] == ops[i0][0] and t <= t0 + slack], key=lambda x: key[x])
        t = start(i)
        for b in ops[i][5]:
            j = bankl.get(b)
            if j is not None and ops[j][0] != ops[i][0]:
                pred[i].add(j)
            bankl[b] = i
        free[ops[i][0]] = t + ops[i][1]
        done[i] = t + ops[i][1] + ops[i][7]
        order.append(i)
        ready.remove(i)
        for j in succ[i]:
            left[j] -= 1
            if left[j] == 0:
                base[j] = max([done[x] for x in pred0[j]], default=0.0)
                ready.append(j)
    return order, pred


def replay(ops, order, pred, scale, lat):
    free, done = {}, {}
    for i in order:
        e = ops[i][0]
        t = max([free.get(e, 0.0)] + [done[j] for j in pred[i] if not (e == "p" and ops[j][0] == "p")])
        free[e] = t + ops[i][1] * scale.get(e, 1.0)
        done[i] = free[e] + ops[i][7] * (lat if ops[i][6] is None else scale.get("dma", 1.0))
    return max(done.values()), done


CASES = (({"dma": 1.35}, 1.0), ({"dma": 1.05}, 1.8), ({"p": 1.45, "v": 1.45, "a": 1.45, "dma": 1.1}, 1.8))


def place_all(ops, before, key, back):
    n = len(ops)
    after = [[] for _ in range(n)]
    left = [len(x) for x in before]
    for i in range(n):
        for j in before[i]:
            after[j].append(i)
    busy, start, done = {}, [0.0] * n, [0.0] * n
    ready = [i for i in range(n) if left[i] == 0]
    while ready:
        i = min(ready, key=lambda x: key[x])
        ready.remove(i)
        e, c, lat = ops[i][0], ops[i][1], ops[i][7]
        t = 0.0
        for j in before[i]:
            if ops[i][6] is not None and ops[j][6] is not None and ops[i][8] < 0 and ops[j][8] < 0 and ops[i][0] == ops[j][0]:
                t = max(t, start[j])
            elif e == "p" and ops[j][0] == "p":
                t = max(t, done[j] - (lat if back else ops[j][7]))
            else:
                t = max(t, done[j])
        need = [(e, lat if back else 0.0, c)] + [(b, 0.0, c + lat) for b in ops[i][5]]
        moved = True
        while moved:
            moved = False
            for r, o, w in need:
                for a, b, who in busy.get(r, ()):
                    if a < t + o + w and t + o < b and (r == e or who != e):
                        t = b - o
                        moved = True
        for r, o, w in need:
            busy.setdefault(r, []).append((t + o, t + o + w, e))
        start[i], done[i] = t, t + c + lat
        for j in after[i]:
            left[j] -= 1
            if left[j] == 0:
                ready.append(j)
    return start, done


def ordered(ops, pred0, before, start):
    n = len(ops)
    rank = list(start)
    for i in range(n):
        for j in before[i]:
            rank[i] = max(rank[i], rank[j] + 1e-6)
    order = sorted(range(n), key=lambda x: (rank[x], x))
    pred = [set(x) for x in pred0]
    bankl = {}
    for i in order:
        for b in ops[i][5]:
            j = bankl.get(b)
            if j is not None and ops[j][0] != ops[i][0]:
                pred[i].add(j)
            bankl[b] = i
    return order, pred


def plan(ops):
    pred0, soft = depends(ops)
    n = len(ops)
    before = [pred0[i] | soft[i] for i in range(n)]
    rev = [set() for _ in range(n)]
    for i in range(n):
        for j in before[i]:
            rev[j].add(i)
    rng = np.random.default_rng(SEED)

    def fixed(order):
        place = {x: j for j, x in enumerate(order)}
        order, pred = ordered(ops, pred0, before, [place[i] for i in range(n)])
        return [replay(ops, order, pred, a, b)[0] for a, b in CASES], order, pred

    best = None
    for j in range(TRIES):
        lead, slack = float(rng.choice([0.0, 2000.0, 4000.0, 7000.0, 10000.0])), float(rng.choice([40.0, 120.0, 250.0]))
        order, pred = schedule(ops, pred0, soft, lead, slack, float(rng.choice([0.0, 300.0, 800.0])), rng)
        cost = [replay(ops, order, pred, a, b)[0] for a, b in CASES]
        if best is None or sum(cost) < sum(best[0]):
            best = (cost, order, pred)
    done = replay(ops, best[1], best[2], {}, 1.0)[1]
    for j in range(TRIES + CLIMB):
        if j >= TRIES:
            done = replay(ops, best[1], best[2], {}, 1.0)[1]
        jit = rng.random((2, n)) * (100.0 if j < TRIES else 400.0)
        done = place_all(ops, rev, [float(jit[0, i]) - done[i] for i in range(n)], True)[1]
        start, done = place_all(ops, before, [float(jit[1, i]) - done[i] for i in range(n)], False)
        order, pred = ordered(ops, pred0, before, start)
        cost = [replay(ops, order, pred, a, b)[0] for a, b in CASES]
        if sum(cost) < sum(best[0]):
            best = (cost, order, pred)
    order, seen = best[1], []
    for x in ROUNDS:
        order = tighten(ops, pred0, soft, order, rng, x[0], x[1], x[2], CASES[slice(*x[3:])])
        seen.append(round(fixed(order)[0][x[3]]))
    return fixed(order) + (seen,)


def tighten(ops, pred0, soft, order, rng, rounds, temp, shared, cases):
    n = len(ops)
    kind, shift, seen, first = list(range(n)), [0.0] * n, {}, {}
    for i, o in enumerate(ops):
        w = tuple(x[:3] + x[4:] if x[:3] == "snd" else x[:4] + x[5:] if x[:4] in ("land", "stay", "sent") else x for x in o[4])
        seen[o[0], w, o[8]] = seen.get((o[0], w, o[8]), 0) + 1
        if shared and o[8] >= 4:
            kind[i], shift[i] = first.setdefault((o[0], w, o[8] % 2, seen[o[0], w, o[8]]), i), PERIOD * (o[8] // 2 - 3)
    names = sorted(set(o[0] for o in ops) | set(b for o in ops for b in o[5]))
    eng = [names.index(o[0]) for o in ops]
    banks = [[names.index(b) for b in o[5]] for o in ops]
    pe = names.index("p")
    before = [sorted(pred0[i] | soft[i]) for i in range(n)]
    hard = [[j for j in pred0[i] if not (eng[i] == pe and eng[j] == pe)] for i in range(n)]
    sets = [([o[1] * a.get(o[0], 1.0) for o in ops], [o[7] * (b if o[6] is None else a.get("dma", 1.0)) for o in ops]) for a, b in cases]

    def run(order, cost, lat):
        free, last, done, why = [0.0] * len(names), [-1] * len(names), [0.0] * n, [-1] * n
        for i in order:
            e = eng[i]
            t, w = free[e], last[e]
            for j in hard[i]:
                if done[j] > t:
                    t, w = done[j], j
            for b in banks[i]:
                j = last[b]
                if j >= 0 and eng[j] != e and done[j] > t:
                    t, w = done[j], j
                last[b] = i
            t += cost[i]
            free[e], last[e], done[i], why[i] = t, i, t + lat[i], w
        return done, why

    def value(key):
        rank = [key[k] + x for k, x in zip(kind, shift)]
        for i in range(n):
            r = rank[i]
            for j in before[i]:
                if rank[j] > r:
                    r = rank[j]
            rank[i] = r + 1e-3
        order = sorted(range(n), key=lambda x: rank[x])
        res = [run(order, c, l) for c, l in sets]
        return sum(max(d) for d, w in res) / len(res), res, rank, order

    done = run(order, *sets[0])[0]
    best, keep = sum(max(run(order, c, l)[0]) for c, l in sets) / len(sets), order
    key = [0.0] * n
    for i in sorted(range(n), key=lambda x: ops[x][8] // 2 == 3):
        key[kind[i]] = done[i] - sets[0][0][i] - sets[0][1][i] - shift[i]
    now, res, rank, order = value(key)
    for r in range(rounds):
        done, why = res[int(rng.integers(len(res)))]
        i = done.index(max(done))
        pairs = []
        while why[i] >= 0:
            if why[i] not in before[i]:
                pairs.append((why[i], i))
            i = why[i]
        j, i = pairs[int(rng.integers(len(pairs)))]
        new = list(key)
        if rng.random() < 0.5:
            t = rank[j] - 1.0 - 30.0 * float(rng.random())
            todo, seen = [i], {i}
            while todo:
                x = todo.pop()
                new[kind[x]] = min(new[kind[x]], t - shift[x])
                for y in before[x]:
                    if rank[y] > t and y not in seen:
                        seen.add(y)
                        todo.append(y)
            if j in seen:
                continue
        else:
            new[kind[j]] = rank[i] + 1.0 + 30.0 * float(rng.random()) - shift[j]
        v, rs, rk, od = value(new)
        if v <= now or rng.random() < math.exp((now - v) / (temp * (1.0 - r / rounds))):
            key, now, res, rank = new, v, rs, rk
            if v < best:
                best, keep = v, od
    return keep


def waits(ops, order, pred):
    pos, cnt = {}, {}
    for i in order:
        if ops[i][6] is None:
            cnt[ops[i][0]] = cnt.get(ops[i][0], 0) + 1
            pos[i] = (ops[i][0], cnt[ops[i][0]])
        else:
            pos[i] = ("x%d" % i, 1)
    know, at, need = {}, {}, {}
    place = {x: j for j, x in enumerate(order)}
    for i in order:
        e = ops[i][0]
        k = know.setdefault(e, {})
        lst = []
        for j in sorted(pred[i], key=lambda x: -place[x]):
            if e == "p" and ops[j][0] == "p":
                continue
            key, val = pos[j]
            if k.get(key, 0) >= val:
                continue
            lst.append(j)
            k[key] = val
            for a, b in at[j].items():
                if k.get(a, 0) < b:
                    k[a] = b
        need[i] = lst
        arrival = ops[i][6] is not None and ops[i][6][1] < 0
        at[i] = {} if arrival else dict(k)
    return need


PLAN = {}


def rank_program(g, core, T, topo):
    rank = T.rank_of(core)
    if rank is None:
        return
    ops, neng = build(g, T, topo, core, rank)
    if "p" not in PLAN:
        cost, order, pred, how = plan(ops)
        PLAN["p"] = (order, waits(ops, order, pred), pred, cost, how)
    order, need = PLAN["p"][:2]
    wanted = set(j for i in order for j in need[i])
    queue = {"v": g.vector, "a": g.scalar, "p": g.tensor, "g": g, "s": g.sync}
    sems = {"v": T.sem.sv, "a": T.sem.sa, "p": T.sem.sp, "g": T.sem.sg}
    cnt, val, stored = {}, {}, 0
    for i in order:
        e, own = ops[i][0], ops[i][6]
        for j in need[i]:
            queue[e].wait_ge(val[j][0], val[j][1])
        ins = ops[i][2]()
        if own is None:
            if i in wanted:
                cnt[e] = cnt.get(e, 0) + 1
                ins.then_inc(sems[e], 1)
                val[i] = (sems[e], cnt[e])
        elif own[0] == "stored":
            stored += 16
        elif own[0] != "none":
            val[i] = (T.sem[own[0]], abs(own[1]))
    g.wait_ge(T.sem.sent, 2 * (STEPS - 1) * neng)
    g.sync.wait_ge(T.sem.stored, stored)
